import numpy as np, ml_dtypes
CORES = [1,5,17,21,33,37,49,53]
N = 8
BF = ml_dtypes.bfloat16
def gentries(a):
    return np.ascontiguousarray(a.reshape(8, 16, -1).transpose(0, 2, 1)).reshape(8, -1)
def gtable(e):
    e = np.asarray(e); return np.ascontiguousarray(e.reshape(8, -1, 16).transpose(0, 2, 1)).reshape(128, -1).astype(np.int32)
C, M, G, T, TH, S = 4096, 1024, 512, 3, 9, 8
def parts(rng):
    R = rng.integers(0, 256, (N, 8, 16, C)); P = rng.integers(0, M, (N, 8, 16, M)); O = rng.integers(0, M, (N, 8, 16, M))
    z = (256 * rng.choice(np.array([0.6, 0.8, 1.0]), (N, 8, 1, G)) * rng.random((N, 8, 16, G))).astype(np.int64)
    return R, P, O, z, rng.integers(0, M, (N, 8, G)), rng.integers(1, 257, (N, 8, 16))
def pack(R, P, O, z, mv, w):
    P = np.array(P); O = np.array(O); P[:, :, 0] = np.arange(M); O[:, :, 0] = np.arange(M)
    return {"strat": R.reshape(N, 128, C).astype(np.float32).astype(BF), "vp": P.reshape(N, 128, M).astype(np.int32), "vo": O.reshape(N, 128, M).astype(np.int32),
            "z0": z.reshape(N, 128, G).astype(np.float32).astype(BF), "mv": np.stack([gtable(a) for a in mv]), "wt": w.reshape(N, 128, 1).astype(np.int32)}
def plant(rng, R, P, O, z, mv, w):
    h = 17 - TH; m = np.arange(M)
    w[:, :, 13] = 16; w[:, :, 14] = 1; w[:, 2, :13] = np.maximum(w[:, 2, :13], 160)
    for r in range(N):
        q = (r + 1) % N
        for g in range(8):
            own = rng.permutation(M)[:12]; i = 1 + rng.permutation(G - 17)[:5]; wq = w[q, g]
            for e in range(4):
                a = int(i[e]); mv[r, g, a] = own[e]; P[r, g, 3 + 4 * e, own[e]] = M - 1
                z[r, g, :h, a] = 255; z[r, g, 13:15, a] = 0
                d = (4065 - int(np.sum(wq * z[r, g, :, a]))) & 4095
                z[r, g, 13, a] = d >> 4; z[r, g, 14, a] = d & 15
            if g == 2:
                left = 2 ** 19
                for j in list(range(13)) + [15, 13, 14]:
                    n = min(255, left // int(wq[j])); z[r, g, j, int(i[4])] = n; left -= n * int(wq[j])
            end = G - 15 + 2 * np.arange(8); mv[r, g, end] = own[4:]
            z[r, g, :h, G - 15::2] = 255
            u = np.sum(wq[:, None] * z[r, g], axis=0) & 4095; p0 = int(u[0]) & (S - 1)
            R[q, g, :, p0] = 255 * rng.integers(0, 2, 16)
            ad = (((m[:, None] * u[end][None, :]) >> 5) + m[:, None] + 37 * 15) & (C - 1)
            for e in range(8):
                good = np.flatnonzero(ad[:, e] == p0)
                if len(good): P[r, g, 15, own[4 + e]] = rng.choice(good)
    return R, P, O, z, mv, w
def setup_inputs(rng):
    return pack(*plant(rng, *parts(rng)))
def corner(rng, first):
    R, P, O, z, mv, w = parts(rng); R = np.maximum(R, 1); m = np.arange(M)[None, :]; j = np.arange(16)[:, None]
    forms = [m + 0 * j, np.maximum(m - j, 0), np.minimum(m + j, M - 1), np.where((m + j) % 2 == 0, 0, M - 1)]
    P = np.stack([np.stack([forms[(g + r) % 4] for g in range(8)]) for r in range(N)])
    O = np.stack([np.stack([forms[(g + r + 1 + g // 4) % 4] for g in range(8)]) for r in range(N)])
    cnt = np.array([255, 256, 1024, 512, 257, 511, 1, 8 * G - 1, 8 * G, 0, 1536, 4 * G, 6 * G, 8 * G - 256, 1023, 1025])[first * N:first * N + N]
    cnt = np.roll(cnt, int(rng.integers(0, N)))
    for r in range(N):
        for g in range(8):
            e = (g + r) % 3
            if e == 0: mv[r, g] = rng.choice(np.array([0, M - 1]), G)
            elif e == 1: mv[r, g] = rng.integers(0, M)
            else: mv[r, g] = rng.permutation(M)[:G]
        hit = np.zeros(8 * G, bool); hit[rng.permutation(8 * G)[:int(cnt[r])]] = True
        z[r] = np.where(hit.reshape(8, 1, G), 0, 255)
    w[:, 1] = 1; w[:, 5] = 256
    return pack(R, P, O, z, mv, w)
def setup_inputs_corners(rng):
    return corner(rng, 0)
def setup_inputs_corners_two(rng):
    return corner(rng, 1)
def setup_inputs_ends(rng):
    R = np.where(rng.random((N, 8, 16, C)) < rng.choice(np.array([0.1, 0.5, 0.75, 0.9]), (N, 8, 1, C)), 255, 0)
    z = np.where(rng.random((N, 8, 16, G)) < rng.choice(np.array([0.05, 0.3, 0.8]), (N, 8, 1, G)), 255, 0)
    P = (M - 1) * rng.integers(0, 2, (N, 8, 16, M)); O = (M - 1) * rng.integers(0, 2, (N, 8, 16, M)); mv = (M - 1) * rng.integers(0, 2, (N, 8, G))
    w = np.where(rng.random((N, 8, 16)) < 0.5, 256, 1)
    mv[:, :, G - 1] = M - 1; P[:, :, 15, M - 1] = M - 1; O[:, :, 15, M - 1] = M - 1
    w[:, 0] = 256; R[:, 0] = np.where(rng.random((N, 1, C)) < 0.5, 255, 0); z[:, 0, :, G - 1] = 255; z[:, 0, :, 0] = 0
    w[:, 5:] = 256; w[:, 5:, 15] = 1
    c = np.zeros(16, np.int64); c[3] = 255; c[15] = 255
    x8 = np.array([0, 1, 2, 4, 5, 6, 7, 8]); y4 = np.array([9, 10, 11, 12])
    for g in (6, 7):
        hot = ((np.arange(C) >> 7) + g) % 2 == 1
        R[:, g] = c[None, :, None]
        R[:, g, x8] = np.where(hot, 192, 64 * rng.integers(0, 2, (N, 1, C))); R[:, g, y4] = np.where(hot, 128, 0)
        z[:, g, :, 1::2] = c[None, :, None]; z[:, g, :, G - 1] = c[None, :]
    R[:, 5] = 0; R[:, 5, 15] = 255; R[:, 5, y4] = 128 * rng.integers(0, 2, (N, 1, C))
    R[:, 5, x8, C - 1] = 192; R[:, 5, y4, C - 1] = 128
    z[:, 5] = 0; z[:, 5, 15] = 255
    m = np.arange(M); f = ((m * 255) >> 5) + m
    for j in range(1, 14):
        near = m[((f + 37 * (j + 1)) & (C - 1)) >= C - 256]
        P[:, 5, j] = rng.choice(near, (N, M)); O[:, 5, j] = rng.choice(near, (N, M))
    P[:, 5, 14:] = rng.integers(0, M, (N, 2, M)); O[:, 5, 14:] = rng.integers(0, M, (N, 2, M))
    mv[:, 5] = np.argsort(rng.random((N, M)), axis=1)[:, :G]; mv[:, 5, G - 1] = M - 1
    keep = np.array(R[3, 5])
    z[1, :, :17 - TH] = 255; z[2, :, :TH] = 0; R[3, :, :TH] = 255
    a0 = f[mv[2, 5]] & (C - 1); keep[np.ix_(x8, a0)] = 192; keep[np.ix_(y4, a0)] = 128; R[3, 5] = keep
    return pack(R, P, O, z, mv, w)
def setup_inputs_spread(rng):
    R = np.minimum((np.exp2(8 * rng.random((N, 8, 1, C))) * rng.random((N, 8, 16, C))).astype(np.int64), 255)
    z = np.minimum((np.exp2(8 * rng.random((N, 8, 1, G))) * rng.random((N, 8, 16, G))).astype(np.int64), 255)
    P = np.minimum((M * rng.random((N, 8, 16, M)) ** 3).astype(np.int64), M - 1); O = np.minimum((M * rng.random((N, 8, 16, M)) ** 3).astype(np.int64), M - 1)
    mv = np.minimum((M * rng.random((N, 8, G)) ** 2).astype(np.int64), M - 1)
    w = np.minimum(np.maximum(np.rint(np.exp2(8 * rng.random((N, 8, 16)))).astype(np.int64), 1), 256)
    v0 = [v for v in range(M + G * (T - 2), M + G * (T - 1)) if (-(2 ** 22)) % v < 32][0]
    u0 = (2 ** 22 + v0 - 1) // v0 - 32
    r = int(rng.integers(0, N)); q = (r + 1 + (T - 1) % (N - 1)) % N; p = (r + 1 + (T - 2) % (N - 1)) % N
    R[q, :, :17 - TH] = 0
    for g in (1, 3, 4, 6):
        w[q, g, 13] = 16; w[q, g, 14] = 1
        c = rng.integers(0, 256, 16); c[13:15] = 0
        d = (u0 - int(np.sum(w[q, g] * c))) & 4095
        c[13] = d >> 4; c[14] = d & 15
        R[p, g] = c[:, None]
        R[q, g, 15] = 0; R[q, g, 15, 0] = 255
    return pack(R, P, O, z, mv, w)
def setup_inputs_ties(rng):
    R, P, O, z, mv, w = parts(rng)
    b = rng.integers(0, 255, (8, 16)); b[0] = 0; b[6] = 254
    share = rng.permutation(np.array([0.02, 0.04, 0.07, 0.1, 0.15, 0.2, 0.3, 0.5])).reshape(1, 8, 1, 1)
    cnt = np.where(rng.random((N, 8, 1, C)) < share, rng.choice(np.array([TH, TH, TH, TH + 1, 16]), (N, 8, 1, C)), rng.choice(np.array([TH - 1, TH - 1, TH - 1, 0]), (N, 8, 1, C)))
    R = b[None, :, :, None] + (np.argsort(rng.random((N, 8, 16, C)), axis=2) < cnt)
    z = b[None, :, :, None] + (rng.random((N, 8, 1, G)) < 0.125) + np.zeros((N, 8, 16, G), np.int64)
    return pack(R, P, O, z, mv, w)
def check_inputs(d):
    bad = []
    for k, lo, hi in (("strat", 0, 255), ("vp", 0, M - 1), ("vo", 0, M - 1), ("z0", 0, 255), ("mv", 0, M - 1), ("wt", 1, 256)):
        a = np.asarray(d[k]).astype(np.float64)
        if not (np.min(a) >= lo and np.max(a) <= hi): bad.append("range of " + k)
        elif np.any(a != np.floor(a)): bad.append("whole numbers in " + k)
    for k in ("vp", "vo"):
        if np.any(np.asarray(d[k]).reshape(-1, 8, 16, M)[:, :, 0] != np.arange(M)): bad.append("row 0 of the views in " + k)
    return bad
def reference(strat, vp, vo, z0, mv, wt):
    R = strat.astype(np.float32).astype(np.int32).reshape(N, 8, 16, C); z = z0.astype(np.float32).astype(np.int32).reshape(N, 8, 16, G)
    w = wt.astype(np.int32).reshape(N, 8, 16, 1); v = np.stack([gentries(a) for a in mv]).astype(np.int64)
    room = np.zeros((N, 8, 16, G * T), np.int32)
    views = [np.concatenate([a.astype(np.int32).reshape(N, 8, 16, M), room], axis=3) for a in (vp, vo)]
    count = np.zeros(N, np.int64); kk = np.arange(16)[None, None, :, None]; verdicts = np.zeros((N, 8, T, G), np.int64)
    for t in range(T):
        mover, other = views[t % 2], views[1 - t % 2]
        q = (np.arange(N) + 1 + t % (N - 1)) % N
        L = np.take_along_axis(mover, v[:, :, None, :], 3).astype(np.int64)
        u = np.add.reduce(w[q] * z, axis=2).astype(np.int64) & 4095
        ad = (((L * u[:, :, None, :]) >> 5) + L + 37 * kk + (count[q] & 255)[:, None, None, None]) & (C - 1)
        Y = np.take_along_axis(R[q], ad.reshape(N, 8, 1, 16 * G), 3).reshape(N, 8, 16, 16, G)
        hit = np.add.reduce((Y > z[:, :, :, None, :]).astype(np.int32), axis=2) >= TH
        hit[:, :, 15] = True
        kap = np.argmax(hit, axis=2)
        use = (kk <= kap[:, :, None, :])[:, :, None]
        z = (np.maximum.reduce(np.where(use, Y, 0), axis=3) + np.minimum.reduce(np.where(use, Y, 255), axis=3)) >> 1
        z = z.astype(np.int32)
        if t < T - 1:
            place = S * np.arange(G) + (u & (S - 1))
            for r in range(N):
                ix = np.repeat(place[r][:, None, :], 16, axis=1); mine = R[int(q[r])]
                np.put_along_axis(mine, ix, (np.take_along_axis(mine, ix, 2) + z[r]) >> 1, 2)
        count[q] = np.add.reduce((kap < 15).reshape(N, 8 * G).astype(np.int64), axis=1)
        named = np.take_along_axis(L, kap[:, :, None, :], 2)
        resumed = np.take_along_axis(other, named, 3)
        n0 = M + G * t; n = np.zeros((N, 8, 1, G), np.int64) + n0 + np.arange(G)
        mover[..., n0:n0 + G] = np.concatenate([n, L[:, :, :15]], axis=2)
        other[..., n0:n0 + G] = np.concatenate([n, resumed[:, :, :15]], axis=2)
        v = n[:, :, 0]; verdicts[:, :, t] = kap
    e = M + G * (T - 1)
    return {"yp": views[0][..., e:e + G].reshape(N, 128, G).astype(np.float32), "yo": views[1][..., e:e + G].reshape(N, 128, G).astype(np.float32),
            "yz": z.reshape(N, 128, G).astype(np.float32).astype(BF), "yk": verdicts.reshape(N, 8, T * G).astype(np.float32)}

@@ -1,0 +1,581 @@
+from concourse.mybir import AluOpType as ALU, AxisListType, ActivationFunctionType as ACTF
+
+NT, G, NC, CH = 3, 512, 4, 128
+RW = 4096 + 816
+DG = (2, 3)
+BIG = 8388608.0
+EN = 8
+
+SCRATCH = {
+    "rw": ("sbuf", [128, RW], "bfloat16"), "pt": ("sbuf", [128, 1536], "int32"), "ot": ("sbuf", [128, 2048], "int32"),
+    "mvs": ("sbuf", [128, 32], "int32"), "mvu": ("sbuf", [128, 32], "uint16"),
+    "wti": ("sbuf", [128, 8], "int32"), "zst": ("sbuf", [128, G], "bfloat16"),
+    "yy": ("sbuf", [128, 16 * G], "bfloat16"), "hi": ("sbuf", [128, 16 * G], "bfloat16"), "lo": ("sbuf", [128, 16 * G], "bfloat16"),
+    "bt": ("sbuf", [128, 16 * G], "bfloat16"), "mhi": ("sbuf", [128, 16 * CH], "bfloat16"), "mlo": ("sbuf", [128, 16 * CH], "bfloat16"),
+    "qf": ("sbuf", [128, G], "float16"), "xi": ("sbuf", [128, G], "int32"), "ai": ("sbuf", [128, G], "int32"),
+    "hit": ("sbuf", [128, G], "bfloat16"), "oh": ("sbuf", [128, 2 * G], "float16"),
+    "hp": ("sbuf", [128, G], "bfloat16"), "sm": ("sbuf", [128, G], "float16"), "z16": ("sbuf", [128, G], "float16"),
+    "lp": ("sbuf", [128, G], "bfloat16"), "big": ("sbuf", [128, G], "float32"), "nwb": ("sbuf", [128, G], "bfloat16"), "kq": ("sbuf", [128, 128], "float16"),
+    "old": ("sbuf", [128, G], "bfloat16"), "nw": ("sbuf", [128, G], "int32"), "res": ("sbuf", [128, G], "float16"),
+    "pli": ("sbuf", [128, 32], "int32"), "plm": ("sbuf", [128, 32], "int32"), "plu": ("sbuf", [128, 32], "uint16"),
+    "kint": ("sbuf", [128, 32], "int32"), "kand": ("sbuf", [128, 32], "int32"), "kf": ("sbuf", [128, 32], "bfloat16"),
+    "yps": ("sbuf", [128, G], "float32"), "yos": ("sbuf", [128, G], "float32"), "yks": ("sbuf", [128, NT * G], "float32"),
+    "acc": ("sbuf", [128, 4 * NT], "float32"), "an": ("sbuf", [128, 4], "float32"), "ani": ("sbuf", [128, 8], "int32"),
+    "xint": ("sbuf", [128, G], "int32"), "xgi": ("sbuf", [128, 128], "int32"), "xx": ("sbuf", [128, G], "float32"), "xg": ("sbuf", [128, 128], "float32"),
+    "pint": ("sbuf", [128, 8], "int32"), "col": ("sbuf", [128, 32], "float32"),
+    "zb_": ("sbuf", [128, 144], "bfloat16"), "zh_": ("sbuf", [128, 144], "float16"), "zw_": ("sbuf", [128, 144], "bfloat16"),
+    "bw": ("sbuf", [128, 128], "bfloat16"), "bb": ("sbuf", [128, 128], "bfloat16"), "ib": ("sbuf", [128, 128], "bfloat16"),
+    "hib": ("sbuf", [128, 128], "bfloat16"), "ih": ("sbuf", [128, 128], "float16"),
+    "i4": ("sbuf", [128, 128], "float16"), "sh": ("sbuf", [128, 128], "float16"), "tri": ("sbuf", [128, 128], "bfloat16"), "tr2": ("sbuf", [128, 128], "bfloat16"),
+    "kc": ("sbuf", [128, 128], "float16"), "one": ("sbuf", [128, G], "float16"), "it2": ("sbuf", [128, G], "float16"),
+    "a15": ("sbuf", [128, 128], "float32"), "cst": ("sbuf", [128, 16], "float16"), "c8": ("sbuf", [128, 32], "int32"),
+}
+for _t in range(NT):
+    SCRATCH["nn%d" % _t] = ("sbuf", [128, 128], "float16")
+    SCRATCH["li%d" % _t] = ("sbuf", [128, G], "float16")
+    SCRATCH["ls%d" % _t] = ("sbuf", [128, G], "float16")
+    SCRATCH["of%d" % _t] = ("sbuf", [128, G], "uint16")
+    SCRATCH["sb%d" % _t] = ("sbuf", [128, 16 * NC], "uint16")
+    SCRATCH["nm%d" % _t] = ("sbuf", [128, 16 * NC], "uint16")
+    SCRATCH["zo%d" % _t] = ("sbuf", [128, G], "bfloat16")
+for _t in range(NT + 1):
+    SCRATCH["zi%d" % _t] = ("sbuf", [128, G], "bfloat16")
+BANKS = ("pz", "pd0", "pd1", "pc", "pf", "pr", "pu", "ps")
+for _b in BANKS:
+    SCRATCH[_b] = ("psum", [128, 512], "float32")
+
+LDS = ["ld_mv", "ld_wt", "ld_z", "ld_p", "ld_o", "ld_r"]
+OUTS = ["o_p", "o_o0", "o_o1", "o_z0", "o_z1", "o_k0", "o_k1", "o_k2"]
+SEMAPHORES = ["qv", "qs", "qp", "qg", "loc", "za0", "la0", "lb0", "lc0"] + LDS + OUTS
+for _t in range(NT):
+    for _c in range(NC):
+        SEMAPHORES += ["nm%d%d" % (_t, _c), "za%d%d" % (_t + 1, _c)]
+        if _t:
+            SEMAPHORES.append("la%d%d" % (_t, _c))
+
+
+def rank_program(g, core, T, topo):
+    me = T.rank_of(core)
+    if me is None:
+        return
+    cores = list(T.cores)
+    N = len(cores)
+    Q = {"v": g.vector, "s": g.scalar, "p": g.tensor, "g": g, "y": g.sync}
+    cnt, known, recs = {}, {e: {} for e in Q}, {}
+
+    def need(e, tok):
+        sem, val, vc = tok
+        k = known[e]
+        if k.get(sem, 0) >= val:
+            return
+        Q[e].wait_ge(T.sem[sem], val)
+        k[sem] = val
+        for s2, v2 in vc.items():
+            if k.get(s2, 0) < v2:
+                k[s2] = v2
+
+    def deps(e, eng, reads, writes):
+        for w, lst in ((0, reads), (1, writes)):
+            for n, lo, hi in lst:
+                for rec in recs.get(n, ()):
+                    if n in BANKS:
+                        hit = rec[3] != eng or (eng != "p" and (w or rec[2]))
+                    else:
+                        hit = rec[0] < hi and lo < rec[1] and (rec[2] or (w and rec[3] != eng))
+                    if hit:
+                        need(e, rec[4])
+
+    def note(eng, tok, reads, writes):
+        for w, lst in ((0, reads), (1, writes)):
+            for n, lo, hi in lst:
+                old = recs.get(n, [])
+                if n in BANKS:
+                    w0 = any(r[2] for r in old if r[3] == eng)
+                    recs[n] = [(lo, hi, w or w0, eng, tok)]
+                    continue
+                if w:
+                    old = [r for r in old if not (lo <= r[0] and r[1] <= hi)]
+                else:
+                    old = [r for r in old if not (r[3] == eng and not r[2] and lo <= r[0] and r[1] <= hi)]
+                recs[n] = old + [(lo, hi, w, eng, tok)]
+
+    def A(n, lo=0, hi=None, st=1, p=128):
+        t = T[n]
+        hi = t.shape[1] if hi is None else hi
+        return (t[0:p, lo:hi:st], (n, lo, hi)) if st > 1 else (t[0:p, lo:hi], (n, lo, hi))
+
+    def run(e, fn, reads, writes, inc=True):
+        rd, wr = [r[1] for r in reads], [w[1] for w in writes]
+        deps(e, e, rd, wr)
+        ins = fn(Q[e])
+        sem = "q" + e
+        val = cnt.get(sem, 0) + 1
+        if inc:
+            ins.then_inc(T.sem[sem], 1)
+            cnt[sem] = val
+        note(e, (sem, val, dict(known[e])), rd, wr)
+
+    def dma(e, sem, out, in_, reads=(), writes=()):
+        rd, wr = [r[1] for r in reads], [w[1] for w in writes]
+        deps(e, "d" + sem, rd, wr)
+        Q[e].dma_start(out, in_).then_inc(T.sem[sem], 16)
+        cnt[sem] = cnt.get(sem, 0) + 16
+        note("d" + sem, (sem, cnt[sem], dict(known[e])), rd, wr)
+
+    def arrives(buf, lo, hi, sem):
+        recs.setdefault(buf, []).append((lo, hi, 1, "r", (sem, EN, {})))
+
+    def send(buf, src, lo, hi, sem, to):
+        dst = cores[to % N]
+        deps("g", "r", [(src, lo, hi)], [])
+        rid, pid, _ = topo.addr(dst)
+        m = 0
+        for x in topo.engines(core, dst)[:EN]:
+            m |= 1 << x
+        g.remote_dma(T[buf][:, lo:hi], T[src][:, lo:hi], T.sem[sem], T.sem["loc"], pid, rid, m)
+        cnt["loc"] = cnt.get("loc", 0) + EN
+
+    def mm(out, l, r, start=True, stop=True, inc=None):
+        run("p", lambda q: q.matmul(out[0], l[0], r[0], start, stop), [l, r], [out], stop if inc is None else inc)
+
+    def copy(out, in_):
+        run("v", lambda q: q.tensor_copy(out[0], in_[0]), [in_], [out])
+
+    def ts(out, in_, s1, op0, s2=None, op1=None):
+        rd = [in_] + [s for s in (s1, s2) if isinstance(s, tuple)]
+        a1 = s1[0] if isinstance(s1, tuple) else s1
+        a2 = s2[0] if isinstance(s2, tuple) else s2
+        if op1 is None:
+            run("v", lambda q: q.tensor_scalar(out[0], in_[0], a1, None, op0), rd, [out])
+        else:
+            run("v", lambda q: q.tensor_scalar(out[0], in_[0], a1, a2, op0, op1), rd, [out])
+
+    def tt(out, a, b, op):
+        run("v", lambda q: q.tensor_tensor(out[0], a[0], b[0], op), [a, b], [out])
+
+    def act(out, in_, fn, acc=None, **kw):
+        rd = [in_] + [x for x in kw.values() if isinstance(x, tuple)]
+        kw = {n: x[0] if isinstance(x, tuple) else x for n, x in kw.items()}
+        if acc is not None:
+            kw["accum_out"] = acc[0]
+        run("s", lambda q: q.activation(out[0], in_[0], fn, **kw), rd, [out] if acc is None else [out, acc])
+
+    def gather_v(out, win, off):
+        run("v", lambda q: q.tensor_copy(out[0], win[0].indirect(off[0])), [win, off], [out])
+
+    def gather_s(out, win, off):
+        run("s", lambda q: q.activation(out[0], win[0].indirect(off[0]), ACTF.Copy), [win, off], [out])
+
+    def fill(out, c):
+        run("v", lambda q: q.memset(out[0], c), [], [out])
+
+    def iota(out, pattern, base, cm):
+        run("g", lambda q: q.iota(out[0], pattern, base, cm), [], [out])
+
+    arrives("zi0", 0, G, "za0")
+    arrives("li0", 0, CH, "la0")
+    arrives("li0", CH, 2 * CH, "lb0")
+    arrives("li0", 2 * CH, G, "lc0")
+    for t in range(NT):
+        for c in range(NC):
+            arrives("nm%d" % t, 16 * c, 16 * c + 16, "nm%d%d" % (t, c))
+            arrives("zi%d" % (t + 1), CH * c, CH * c + CH, "za%d%d" % (t + 1, c))
+            if t:
+                arrives("li%d" % t, CH * c, CH * c + CH, "la%d%d" % (t, c))
+
+    dma("s", "ld_z", T.zst[:], T.z0[:], writes=[A("zst")])
+    dma("y", "ld_mv", T.mvs[:], T.mv[:], writes=[A("mvs")])
+    dma("y", "ld_p", T.pt[:, 0:1024], T.vp[:], writes=[A("pt", 0, 1024)])
+    dma("s", "ld_wt", T.wti[:, 0:1], T.wt[:], writes=[A("wti", 0, 1)])
+    dma("s", "ld_r", T.rw[:, 0:4096], T.strat[:], writes=[A("rw", 0, 4096)])
+    dma("y", "ld_o", T.ot[:, 0:1024], T.vo[:], writes=[A("ot", 0, 1024)])
+
+    C = lambda i: A("col", i, i + 1)
+    cp, ck, cg16, cz15, c37, ck16, c8k, cj0, cj1, cnl, cshp, cthr, cw, cg, ct, cadd = [C(i) for i in range(16)]
+    cv = [C(16 + i) for i in range(NT)]
+
+    def addr1(t, lo, hi):
+        mm(A("pu", 0, hi - lo), A("bw"), A("zi%d" % t, lo, hi))
+
+    def addr2(t, lo, hi):
+        n = hi - lo
+        pu = A("pu", 0, n)
+        ts(A("qf", lo, hi), pu, 1.0 / 4096, ALU.mult, 1025 - 2047.5 / 4096, ALU.add)
+        mm(pu, A("kc"), A("one", 0, n), True, False)
+        mm(pu, A("bw"), A("zi%d" % t, lo, hi), False, False)
+        mm(pu, A("i4"), A("qf", lo, hi), False, True)
+
+    def addr3(t, lo, hi):
+        tt(A("xi", lo, hi), A("li%d" % t, lo, hi), A("pu", 0, hi - lo), ALU.mult)
+        ts(A("ai", lo, hi), A("xi", lo, hi), 5, ALU.arith_shift_right, 4095, ALU.bitwise_and)
+
+    def addr(t, lo, hi):
+        addr1(t, lo, hi)
+        addr2(t, lo, hi)
+        addr3(t, lo, hi)
+
+    def afin(t, lo, hi):
+        ts(A("of%d" % t, lo, hi), A("ai", lo, hi), cadd if t else c37, ALU.add)
+
+    def gath(t, c, pieces, e="s"):
+        for s in pieces:
+            i0 = CH * c + 32 * s
+            (gather_s if e == "s" else gather_v)(A("yy", 16 * i0, 16 * i0 + 512), A("rw", 0, RW), A("of%d" % t, i0, i0 + 32))
+
+    def blk(c, q):
+        return (2048 * c + 512 * q, 2048 * c + 512 * q + 512)
+
+    def zx(t, c):
+        for e in range(4):
+            mm(A("pz", e, 512, 4), A("ib"), A("zi%d" % t, CH * c, CH * c + CH), inc=e == 3)
+
+    def cmpv(t, c, qs):
+        for q in qs:
+            tt(A("bt", *blk(c, q)), A("yy", 2048 * c + q, 2048 * c + 2048, 4), A("pz"), ALU.is_gt)
+
+    def count(t, c):
+        ks = [(q, m) for q in range(4) for m in range(4)]
+        for n, (q, m) in enumerate(ks):
+            k = 4 * m + q
+            lo, hi = blk(c, q)
+            mm(A("pc", 0, CH), A("zb_", 15 - k, 143 - k), A("bt", lo + m, hi, 4), n == 0, n == 15)
+
+    def scan(t, c, hi):
+        s = (2048 * c, 2048 * c + 2048)
+        o, m = (A("hi", *s), A("mhi")) if hi else (A("lo", *s), A("mlo"))
+        o0, o1 = (ALU.min, ALU.max) if hi else (ALU.max, ALU.min)
+        y = A("yy", *s)
+        run("v", lambda q: q.tensor_tensor_scan(o[0], m[0], y[0], 0.0, o0, o1), [m, y], [o])
+
+    def hits(t, c):
+        h = A("hit", CH * c, CH * c + CH)
+        ts(h, A("pc", 0, CH), cthr, ALU.is_ge)
+        mm(A("pd0", 0, CH), A("tri"), h)
+        mm(A("pf", 0, CH), A("tri"), h)
+        act(A("pr", 0, CH), A("pd0", 0, CH), ACTF.Relu, acc=A("acc", 4 * t + c, 4 * t + c + 1), scale=4096.0)
+
+    def lists1(t, c):
+        o = 2 * CH * c
+        ts(A("oh", o, o + CH), A("pf", 0, CH), 0.0, ALU.max, ck, ALU.mult)
+        tt(A("oh", o + CH, o + 2 * CH), A("li%d" % t, CH * c, CH * c + CH), A("pr", 0, CH), ALU.min)
+        pl = A("pf", 256, 272)
+        mm(pl, A("ih"), A("cst"), True, False)
+        for k in range(16):
+            mm(pl, A("zh_", 15 - k, 143 - k), A("oh", o + k, o + 2 * CH, 16), False, k == 15)
+
+    def lists2(t, c):
+        copy(A("sb%d" % t, 16 * c, 16 * c + 16), A("pf", 256, 272))
+        send("nm%d" % t, "sb%d" % t, 16 * c, 16 * c + 16, "nm%d%d" % (t, c), me - 1 - t)
+
+    def pick1(t, c):
+        a, b = CH * c, CH * c + CH
+        gather_s(A("hp", a, b), A("hi", 16 * a, 16 * b), A("sb%d" % t, 16 * c, 16 * c + 8))
+        if c < 3:
+            gather_s(A("lp", a, b), A("lo", 16 * a, 16 * b), A("sb%d" % t, 16 * c, 16 * c + 8))
+
+    def send_z(t, c):
+        send("zi%d" % (t + 1), "zo%d" % t, CH * c, CH * c + CH, "za%d%d" % (t + 1, c), me + 1 if t + 1 < NT else me - 1 - t)
+
+    def half(p, a, b, lo, hi):
+        mm(p, A("kq"), A("one", lo, hi), True, False)
+        mm(p, A("hib"), A(a, lo, hi), False, False)
+        mm(p, A("hib"), A(b, lo, hi), False, True)
+
+    def whole(out, p, lo, hi):
+        act(A("big", lo, hi), p, ACTF.Copy, bias=BIG)
+        act(A(out, lo, hi), A("big", lo, hi), ACTF.Copy, bias=-BIG)
+
+    def pick3(t, c):
+        half(A("pr", CH, 2 * CH), "hp", "lp", CH * c, CH * c + CH)
+        whole("zo%d" % t, A("pr", CH, 2 * CH), CH * c, CH * c + CH)
+        send_z(t, c)
+
+    def pick2(t, c):
+        a, b = CH * c, CH * c + CH
+        off, w, h, s = A("sb%d" % t, 16 * c, 16 * c + 8), A("lo", 16 * a, 16 * b), A("hp", a, b), A("sm", a, b)
+        run("v", lambda q: q.tensor_tensor(s[0], w[0].indirect(off[0]), h[0], ALU.add), [w, off, h], [s])
+        ts(A("z16", a, b), s, 0.5, ALU.mult, 1024.75, ALU.add)
+        ts(A("zo%d" % t, a, b), A("z16", a, b), -1025.0, ALU.add)
+        send_z(t, c)
+
+    def place1(t):
+        for k in range(16):
+            mm(A("pr", 256, 288), A("zw_", 15 - k, 143 - k), A("zi%d" % t, k, G, 16), k == 0, k == 15)
+
+    def place2(t):
+        copy(A("pli"), A("pr", 256, 288))
+        ts(A("plm"), A("pli"), 7, ALU.bitwise_and)
+        tt(A("pli"), A("plm"), A("c8"), ALU.add)
+        copy(A("plu"), A("pli"))
+
+    def olds(t):
+        gather_s(A("old"), A("rw", 0, 4096), A("plu"))
+
+    def upd1(t, lo, hi):
+        mm(A("ps", CH, CH + hi - lo), A("hib"), A("old", lo, hi), True, False)
+        mm(A("ps", CH, CH + hi - lo), A("hib"), A("zo%d" % t, lo, hi), False, True)
+
+    def upd2(t, lo, hi):
+        ts(A("nw", lo, hi), A("ps", CH, CH + hi - lo), -0.25, ALU.add)
+
+    def upd3(t, lo, hi):
+        p = A("ps", CH, CH + hi - lo)
+        half(p, "old", "zo%d" % t, lo, hi)
+        whole("nwb", p, lo, hi)
+
+    def scat(t, lo, hi, src):
+        w, o, i = A("rw", 0, 4096), A("plu", lo // 16, hi // 16), A(src, lo, hi)
+        run("v", lambda q: q.tensor_copy(w[0].indirect(o[0]), i[0]), [o, i], [w])
+
+    def mirror():
+        copy(A("rw", 4096, RW), A("rw", 0, RW - 4096))
+
+    def tally1(t):
+        mm(A("pr", 320, 324), A("a15"), A("acc", 4 * t, 4 * t + 4))
+
+    def tally2(t):
+        o, i = A("an", 0, 1), A("pr", 320, 324)
+        run("v", lambda q: q.tensor_reduce(o[0], i[0], AxisListType.X, ALU.add, negate=True), [i], [o])
+        copy(A("ani", 0, 1), o)
+        ts(A("ani", 1, 2), A("ani", 0, 1), 255, ALU.bitwise_and)
+        ts(cadd, A("ani", 1, 2), c37, ALU.add)
+
+    def shift(t, src, lo, hi, b="ps"):
+        p = A(b, 0, hi - lo)
+        mm(p, A("sh"), A(src, lo, hi), True, False)
+        mm(p, A("nn%d" % t), A("it2", lo, hi), False, True)
+
+    def home1(t, c):
+        a, b = CH * c, CH * c + CH
+        gather_v(A("res", a, b), A(("ot", "pt", "ot")[t], 0, 1024 + 512 * t), A("nm%d" % t, 16 * c + 8, 16 * c + 16))
+
+    def home2(t, c):
+        a, b = CH * c, CH * c + CH
+        p = A("ps", 0, CH)
+        if t + 1 < NT:
+            copy(A("ls%d" % (t + 1), a, b), p)
+            send("li%d" % (t + 1), "ls%d" % (t + 1), a, b, "la%d%d" % (t + 1, c), me + 2 + t)
+            if t == 0:
+                copy(A("ot", 1024 + a, 1024 + b), p)
+        else:
+            act(A("yos", a, b), p, ACTF.Copy)
+        copy(A("kint", 8 * c, 8 * c + 8), A("nm%d" % t, 16 * c, 16 * c + 8))
+
+    def ext2(t):
+        p = A("pu", 0, G)
+        if t == 0:
+            copy(A("pt", 1024, 1536), p)
+        elif t == 1:
+            copy(A("ot", 1536, 2048), p)
+        else:
+            act(A("yps"), p, ACTF.Copy)
+            dma("y", "o_p", T.yp[:], T.yps[:], reads=[A("yps")])
+
+    def kand(t):
+        ts(A("kand"), A("kint"), 15, ALU.bitwise_and)
+        copy(A("kf"), A("kand"))
+
+    def verd1(t):
+        for k in range(16):
+            mm(A("pd1", k, 512, 16, p=8), A("ib", k, 128, 16), A("kf"), inc=k == 15)
+
+    def verd2(t):
+        act(A("yks", t * G, t * G + G, p=8), A("pd1", 0, 512, p=8), ACTF.Copy)
+        dma("y", "o_k%d" % t, T.yk[:, t * G:t * G + G], T.yks[0:8, t * G:t * G + G], reads=[A("yks", t * G, t * G + G)])
+
+    iota(A("pint", 0, 1), [[1, 1]], 0, 1)
+    iota(A("xint"), [[1, G]], 0, 0)
+    X, X144 = A("xx", 0, 128), A("xx", 0, 144)
+    ts(A("pint", 1, 2), A("pint", 0, 1), 15, ALU.bitwise_and)
+    copy(cp, A("pint", 0, 1))
+    copy(ck, A("pint", 1, 2))
+    tt(cg16, cp, ck, ALU.subtract)
+    ts(c37, ck, 37.0, ALU.mult)
+    ts(ct, cp, 0.0, ALU.is_equal, 32.0, ALU.mult)
+    ts(cg, cg16, 1.0 / 16, ALU.mult)
+    ts(cz15, cg16, 15.0, ALU.add)
+    ts(ct, ct, 32800.0, ALU.add)
+    copy(A("xx"), A("xint"))
+    send("zi0", "zst", 0, G, "za0", me + 1)
+    ts(A("xgi"), A("xint", 0, 128), 4, ALU.arith_shift_right)
+    ts(A("one"), A("xx"), 0.0, ALU.mult, 1.0, ALU.add)
+    copy(A("xg"), A("xgi"))
+    ts(A("kc"), X, 0.0, ALU.mult, ct, ALU.add)
+    ts(A("i4"), X, cp, ALU.is_equal, -4096.0, ALU.mult)
+    ts(A("ib"), X, cp, ALU.is_equal)
+    copy(A("mvu"), A("mvs"))
+    ts(A("kq"), X, 0.0, ALU.mult, -2.0 ** -9, ALU.add)
+    ts(A("zb_"), X144, cz15, ALU.is_equal)
+    ts(A("zh_"), X144, cz15, ALU.is_equal)
+    ts(A("bb"), A("xg"), cg, ALU.is_equal)
+    ts(A("tr2"), X, cp, ALU.is_gt)
+    ts(A("ih"), X, cp, ALU.is_equal)
+    tt(A("tr2"), A("tr2"), A("bb"), ALU.mult)
+    gather_v(A("ls0", 0, CH), A("pt", 0, 1024), A("mvu", 0, CH // 16))
+    send("li0", "ls0", 0, CH, "la0", me + 1)
+    gather_v(A("ls0", CH, G), A("pt", 0, 1024), A("mvu", CH // 16, 32))
+    send("li0", "ls0", CH, 2 * CH, "lb0", me + 1)
+    send("li0", "ls0", 2 * CH, G, "lc0", me + 1)
+    copy(cw, A("wti", 0, 1))
+    ts(ck16, ck, 16.0, ALU.mult)
+    ts(A("bw"), A("xg"), cg, ALU.is_equal, cw, ALU.mult)
+    tt(A("tri"), A("ib"), A("tr2"), ALU.subtract)
+    ts(ct, ck, 15.0, ALU.is_equal, 1.0 / 4096, ALU.mult)
+    act(A("hib"), A("ib"), ACTF.Copy, scale=0.5)
+    act(A("zw_"), A("zb_"), ACTF.Copy, scale=cw)
+    act(A("a15"), X, ACTF.Identity, scale=0.0, bias=ct)
+    for i in range(0, 16 * CH, G):
+        act(A("mhi", i, i + G), A("xx"), ACTF.Copy, scale=0.0, bias=256.0)
+        act(A("mlo", i, i + G), A("xx"), ACTF.Copy, scale=0.0)
+    act(A("mhi", 0, 16 * CH, 16), X, ACTF.Copy, scale=0.0)
+    act(A("mlo", 0, 16 * CH, 16), X, ACTF.Copy, scale=0.0, bias=256.0)
+    ts(cj0, ck, 0.0, ALU.is_equal)
+    ts(cj1, ck, 1.0, ALU.is_equal)
+    ts(cnl, ck, 15.0, ALU.is_lt)
+    ts(cshp, cp, 1.0, ALU.add)
+    ts(c8k, ck, 8.0, ALU.mult)
+    ts(A("it2"), A("xx"), cj0, ALU.mult, cj1, ALU.add)
+    for t in range(NT):
+        ts(cv[t], cj1, 1024.0 + 512 * t, ALU.mult)
+    ts(A("sh"), X, cshp, ALU.is_equal, cnl, ALU.mult)
+    for t in range(NT):
+        tt(cv[t], cv[t], cj0, ALU.add)
+    for t in range(NT):
+        ts(A("nn%d" % t), X, cg16, ALU.is_equal, cv[t], ALU.mult)
+    ts(A("c8"), A("xx", 0, 32), 128.0, ALU.mult, c8k, ALU.add)
+    ts(cthr, ck, 15.0, ALU.is_equal, -100.0, ALU.mult)
+    ts(A("cst", 8, 16), A("xx", 0, 8), 0.0, ALU.mult)
+    ts(cthr, cthr, 9.0, ALU.add)
+    ts(A("cst", 0, 8), A("xx", 0, 8), 256.0, ALU.mult, ck16, ALU.add)
+    addr(0, 0, CH)
+    afin(0, 0, CH)
+    mirror()
+    gath(0, 0, [s for s in range(4) if s not in DG])
+    gath(0, 0, DG, "v")
+    addr(0, CH, 2 * CH)
+    afin(0, CH, 2 * CH)
+    gath(0, 1, (0, 1))
+    zx(0, 0)
+
+    for t in range(NT):
+        last = t + 1 == NT
+        if t:
+            afin(t, 0, CH)
+            gath(t, 0, [s for s in range(4) if s not in DG])
+            gath(t, 0, DG, "v")
+            zx(t, 0)
+            addr3(t, CH, 2 * CH)
+            afin(t, CH, 2 * CH)
+            gath(t, 1, (0, 1))
+            home1(t - 1, 2)
+            shift(t - 1, "res", 2 * CH, 3 * CH)
+            if t > 1:
+                verd1(t - 2)
+                verd2(t - 2)
+        for c in range(NC):
+            n = c + 1 if c + 1 < NC else None
+            j = None
+            if t and c < 2:
+                j = (t, CH * (c + 2), CH * (c + 3))
+            elif c == 0:
+                j = (0, 2 * CH, G)
+            elif c == 3 and not last:
+                j = (t + 1, 0, CH)
+            if j and c < 3:
+                addr1(*j)
+            cmpv(t, c, (0, 1))
+            if t and c == 0:
+                home2(t - 1, 2)
+            if n and c:
+                gath(t, n, (0,))
+            if c:
+                lists2(t, c - 1)
+                pick1(t, c - 1)
+                if n:
+                    gath(t, n, (1,))
+            cmpv(t, c, (2, 3))
+            scan(t, c, True)
+            count(t, c)
+            if c:
+                pick3(t, c - 1)
+            if c >= 2:
+                shift(t, "res", CH * (c - 2), CH * (c - 1))
+            if j and c < 3:
+                addr2(*j)
+            if t and c == 0:
+                home1(t - 1, 3)
+                shift(t - 1, "res", 3 * CH, G)
+            hits(t, c)
+            if c == 1 and not last:
+                place1(t)
+            if c == 2:
+                shift(t, "ls%d" % t, 0, G, "pu")
+            if n:
+                gath(t, n, (2, 3))
+            if c == 2 and not last:
+                olds(t)
+            if c == 3:
+                home2(t, 1)
+            if c < 3:
+                scan(t, c, False)
+                if c == 2:
+                    home2(t, 0)
+                if j and c:
+                    addr3(*j)
+                    afin(*j)
+            elif not last:
+                addr1(*j)
+                addr2(*j)
+                upd3(t, 0, 3 * CH)
+            if t and c == 0:
+                home2(t - 1, 3)
+            if c + 1 < NC:
+                zx(t, c + 1)
+            lists1(t, c)
+            if j and c == 0:
+                addr3(*j)
+                afin(*j)
+            if c == 3:
+                scan(t, c, False)
+                if not last:
+                    addr3(*j)
+            if c == 1 and not last:
+                place2(t)
+            if c == 2:
+                ext2(t)
+            if 1 <= c < 3:
+                home1(t, c - 1)
+            if t and c == 1:
+                kand(t - 1)
+        lists2(t, 3)
+        pick1(t, 3)
+        if not last:
+            addr1(t + 1, CH, 2 * CH)
+            scat(t, 0, 3 * CH, "nwb")
+            tally1(t)
+            act(A("rw", 4096, RW), A("rw", 0, RW - 4096), ACTF.Copy)
+            addr2(t + 1, CH, 2 * CH)
+        pick2(t, 3)
+        if not last:
+            upd1(t, 3 * CH, G)
+            tally2(t)
+            upd2(t, 3 * CH, G)
+            scat(t, 3 * CH, G, "nw")
+    home1(2, 2)
+    shift(2, "res", 2 * CH, 3 * CH)
+    verd1(1)
+    home2(2, 2)
+    verd2(1)
+    dma("y", "o_o0", T.yo[:, 0:3 * CH], T.yos[:, 0:3 * CH], reads=[A("yos", 0, 3 * CH)])
+    dma("y", "o_z0", T.yz[:, 0:3 * CH], T.zi3[:, 0:3 * CH], reads=[A("zi3", 0, 3 * CH)])
+    home1(2, 3)
+    shift(2, "res", 3 * CH, G)
+    home2(2, 3)
+    dma("s", "o_o1", T.yo[:, 3 * CH:G], T.yos[:, 3 * CH:G], reads=[A("yos", 3 * CH, G)])
+    kand(2)
+    verd1(2)
+    verd2(2)
+    dma("y", "o_z1", T.yz[:, 3 * CH:G], T.zi3[:, 3 * CH:G], reads=[A("zi3", 3 * CH, G)])
+    for s in OUTS + ["loc", "qv", "qs", "qp", "qg"]:
+        if cnt.get(s, 0) > known["g"].get(s, 0):
+            g.wait_ge(T.sem[s], cnt[s])

@@ -1,52 +1,57 @@
 from concourse.mybir import AluOpType as ALU, AxisListType, ActivationFunctionType as ACTF
 
-NT, G, NC, CH = 3, 512, 4, 128
+NT, G = 3, 512
+CHS = (0, 128, 256, 384, 448, 512)
+NC = len(CHS) - 1
+PC = 32
 RW = 4096 + 816
-DG = (2, 3)
-BIG = 8388608.0
+SEG = 128
 EN = 8
+ZO, QO = 1056.0, 1048.0
+CY, GA, SC = 0.83e-3, 1.5, 3.5
+LAT, HOP = 0.1, 1.6
+HOLD, SPARE = 0.1, 0.3
 
 SCRATCH = {
-    "rw": ("sbuf", [128, RW], "bfloat16"), "pt": ("sbuf", [128, 1536], "int32"), "ot": ("sbuf", [128, 2048], "int32"),
+    "rw": ("sbuf", [128, RW], "bfloat16"), "pt0": ("sbuf", [128, 1024], "int32"),
+    "pts": ("sbuf", [128, 1536], "int32"), "ots": ("sbuf", [128, 2048], "int32"),
     "mvs": ("sbuf", [128, 32], "int32"), "mvu": ("sbuf", [128, 32], "uint16"),
     "wti": ("sbuf", [128, 8], "int32"), "zst": ("sbuf", [128, G], "bfloat16"),
     "yy": ("sbuf", [128, 16 * G], "bfloat16"), "hi": ("sbuf", [128, 16 * G], "bfloat16"), "lo": ("sbuf", [128, 16 * G], "bfloat16"),
-    "bt": ("sbuf", [128, 16 * G], "bfloat16"), "mhi": ("sbuf", [128, 16 * CH], "bfloat16"), "mlo": ("sbuf", [128, 16 * CH], "bfloat16"),
+    "bt": ("sbuf", [128, 16 * G], "bfloat16"), "mhi": ("sbuf", [128, 2048], "bfloat16"), "mlo": ("sbuf", [128, 2048], "bfloat16"),
     "qf": ("sbuf", [128, G], "float16"), "xi": ("sbuf", [128, G], "int32"), "ai": ("sbuf", [128, G], "int32"),
-    "hit": ("sbuf", [128, G], "bfloat16"), "oh": ("sbuf", [128, 2 * G], "float16"),
-    "hp": ("sbuf", [128, G], "bfloat16"), "sm": ("sbuf", [128, G], "float16"), "z16": ("sbuf", [128, G], "float16"),
-    "lp": ("sbuf", [128, G], "bfloat16"), "big": ("sbuf", [128, G], "float32"), "nwb": ("sbuf", [128, G], "bfloat16"), "kq": ("sbuf", [128, 128], "float16"),
-    "old": ("sbuf", [128, G], "bfloat16"), "nw": ("sbuf", [128, G], "int32"), "res": ("sbuf", [128, G], "float16"),
+    "sg": ("sbuf", [128, G], "bfloat16"), "oh": ("sbuf", [128, 2 * G], "float16"), "vl": ("sbuf", [128, 64], "uint16"),
+    "hp": ("sbuf", [128, G], "bfloat16"), "lp": ("sbuf", [128, G], "bfloat16"), "sm": ("sbuf", [128, G], "float16"), "s2": ("sbuf", [128, G], "float16"),
+    "z16": ("sbuf", [128, G], "float16"), "old": ("sbuf", [128, G], "float16"), "nw": ("sbuf", [128, G], "int32"),
     "pli": ("sbuf", [128, 32], "int32"), "plm": ("sbuf", [128, 32], "int32"), "plu": ("sbuf", [128, 32], "uint16"),
-    "kint": ("sbuf", [128, 32], "int32"), "kand": ("sbuf", [128, 32], "int32"), "kf": ("sbuf", [128, 32], "bfloat16"),
-    "yps": ("sbuf", [128, G], "float32"), "yos": ("sbuf", [128, G], "float32"), "yks": ("sbuf", [128, NT * G], "float32"),
-    "acc": ("sbuf", [128, 4 * NT], "float32"), "an": ("sbuf", [128, 4], "float32"), "ani": ("sbuf", [128, 8], "int32"),
-    "xint": ("sbuf", [128, G], "int32"), "xgi": ("sbuf", [128, 128], "int32"), "xx": ("sbuf", [128, G], "float32"), "xg": ("sbuf", [128, 128], "float32"),
+    "yps": ("sbuf", [128, G], "float32"), "yos": ("sbuf", [128, G], "float32"),
+    "an": ("sbuf", [128, 4], "float32"), "ani": ("sbuf", [128, 8], "int32"),
+    "xx": ("sbuf", [128, G], "float32"), "xb": ("sbuf", [128, 144], "bfloat16"), "xg": ("sbuf", [128, 128], "bfloat16"),
     "pint": ("sbuf", [128, 8], "int32"), "col": ("sbuf", [128, 32], "float32"),
-    "zb_": ("sbuf", [128, 144], "bfloat16"), "zh_": ("sbuf", [128, 144], "float16"), "zw_": ("sbuf", [128, 144], "bfloat16"),
-    "bw": ("sbuf", [128, 128], "bfloat16"), "bb": ("sbuf", [128, 128], "bfloat16"), "ib": ("sbuf", [128, 128], "bfloat16"),
-    "hib": ("sbuf", [128, 128], "bfloat16"), "ih": ("sbuf", [128, 128], "float16"),
-    "i4": ("sbuf", [128, 128], "float16"), "sh": ("sbuf", [128, 128], "float16"), "tri": ("sbuf", [128, 128], "bfloat16"), "tr2": ("sbuf", [128, 128], "bfloat16"),
-    "kc": ("sbuf", [128, 128], "float16"), "one": ("sbuf", [128, G], "float16"), "it2": ("sbuf", [128, G], "float16"),
-    "a15": ("sbuf", [128, 128], "float32"), "cst": ("sbuf", [128, 16], "float16"), "c8": ("sbuf", [128, 32], "int32"),
+    "zb_": ("sbuf", [128, 144], "bfloat16"), "zw_": ("sbuf", [128, 144], "bfloat16"), "neg": ("sbuf", [128, G], "bfloat16"),
+    "nr0": ("sbuf", [128, G], "float16"), "nr1": ("sbuf", [128, G], "float16"), "nr2": ("sbuf", [128, G], "float32"),
+    "cst": ("sbuf", [128, 64], "float16"), "c8": ("sbuf", [128, 32], "int32"),
 }
+for _n in ("bw", "kc", "kcw", "ib", "i4", "hib", "qib", "tri", "tr1", "tr2", "sh1", "sh2", "a15", "k1"):
+    SCRATCH[_n] = ("sbuf", [128, 128], "bfloat16")
 for _t in range(NT):
-    SCRATCH["nn%d" % _t] = ("sbuf", [128, 128], "float16")
     SCRATCH["li%d" % _t] = ("sbuf", [128, G], "float16")
     SCRATCH["ls%d" % _t] = ("sbuf", [128, G], "float16")
     SCRATCH["of%d" % _t] = ("sbuf", [128, G], "uint16")
-    SCRATCH["sb%d" % _t] = ("sbuf", [128, 16 * NC], "uint16")
-    SCRATCH["nm%d" % _t] = ("sbuf", [128, 16 * NC], "uint16")
-    SCRATCH["zo%d" % _t] = ("sbuf", [128, G], "bfloat16")
+    SCRATCH["sb%d" % _t] = ("sbuf", [128, 64], "uint16")
+    SCRATCH["nm%d" % _t] = ("sbuf", [128, 64], "uint16")
+    SCRATCH["vs%d" % _t] = ("sbuf", [128, 32], "float32")
+    SCRATCH["vi%d" % _t] = ("sbuf", [128, 32], "float32")
+    SCRATCH["zo%d" % _t] = ("sbuf", [128, G], "float16" if _t + 1 < NT else "bfloat16")
 for _t in range(NT + 1):
-    SCRATCH["zi%d" % _t] = ("sbuf", [128, G], "bfloat16")
-BANKS = ("pz", "pd0", "pd1", "pc", "pf", "pr", "pu", "ps")
+    SCRATCH["zi%d" % _t] = ("sbuf", [128, G], "float16" if 0 < _t < NT else "bfloat16")
+BANKS = ("pz0", "pz1", "pu", "pc", "pf", "pl", "ph", "pe")
 for _b in BANKS:
     SCRATCH[_b] = ("psum", [128, 512], "float32")
 
-LDS = ["ld_mv", "ld_wt", "ld_z", "ld_p", "ld_o", "ld_r"]
+LDS = ["ld_mv", "ld_wt", "ld_z", "ld_p", "ld_r", "ld_o", "ld_o0", "ld_q", "ld_q0"]
 OUTS = ["o_p", "o_o0", "o_o1", "o_z0", "o_z1", "o_k0", "o_k1", "o_k2"]
-SEMAPHORES = ["qv", "qs", "qp", "qg", "loc", "za0", "la0", "lb0", "lc0"] + LDS + OUTS
+SEMAPHORES = ["qv", "qs", "qp", "qg", "loc", "za0", "zb0", "la0", "lb0", "lc0", "va0", "va1", "va2"] + LDS + OUTS
 for _t in range(NT):
     for _c in range(NC):
         SEMAPHORES += ["nm%d%d" % (_t, _c), "za%d%d" % (_t + 1, _c)]
@@ -61,521 +66,434 @@ def rank_program(g, core, T, topo):
     cores = list(T.cores)
     N = len(cores)
     Q = {"v": g.vector, "s": g.scalar, "p": g.tensor, "g": g, "y": g.sync}
-    cnt, known, recs = {}, {e: {} for e in Q}, {}
 
-    def need(e, tok):
-        sem, val, vc = tok
-        k = known[e]
-        if k.get(sem, 0) >= val:
-            return
-        Q[e].wait_ge(T.sem[sem], val)
-        k[sem] = val
-        for s2, v2 in vc.items():
-            if k.get(s2, 0) < v2:
-                k[s2] = v2
+    steps, recs = [], {}
 
-    def deps(e, eng, reads, writes):
+    def step(on, reads, writes, lat=LAT, sem=None, n=1, lands=None, after=()):
+        i, pre = len(steps), {j: False for j in after}
         for w, lst in ((0, reads), (1, writes)):
-            for n, lo, hi in lst:
-                for rec in recs.get(n, ()):
-                    if n in BANKS:
-                        hit = rec[3] != eng or (eng != "p" and (w or rec[2]))
-                    else:
-                        hit = rec[0] < hi and lo < rec[1] and (rec[2] or (w and rec[3] != eng))
-                    if hit:
-                        need(e, rec[4])
-
-    def note(eng, tok, reads, writes):
+            for _, (b, lo, hi) in lst:
+                for r in recs.get(b, []):
+                    if b in BANKS:
+                        pre[r[3]] = pre.get(r[3], False) or ("p" not in on and bool(w or r[2]))
+                    elif r[0] < hi and lo < r[1] and (w or r[2]):
+                        pre[r[3]] = pre.get(r[3], False) or bool(r[2])
         for w, lst in ((0, reads), (1, writes)):
-            for n, lo, hi in lst:
-                old = recs.get(n, [])
-                if n in BANKS:
-                    w0 = any(r[2] for r in old if r[3] == eng)
-                    recs[n] = [(lo, hi, w or w0, eng, tok)]
-                    continue
-                if w:
-                    old = [r for r in old if not (lo <= r[0] and r[1] <= hi)]
+            for _, (b, lo, hi) in lst:
+                old = recs.get(b, [])
+                if b in BANKS:
+                    recs[b] = [(lo, hi, w or any(r[2] for r in old if r[3] == i), i)]
                 else:
-                    old = [r for r in old if not (r[3] == eng and not r[2] and lo <= r[0] and r[1] <= hi)]
-                recs[n] = old + [(lo, hi, w, eng, tok)]
+                    recs[b] = [r for r in old if not (w and lo <= r[0] and r[1] <= hi)] + [(lo, hi, w, i)]
+        if lands:
+            recs.setdefault(lands[0], []).append((lands[1], lands[2], 1, i))
+        pre.pop(i, None)
+        steps.append({"on": on, "pre": pre, "lat": lat, "sem": sem, "n": n, "order": set(after)})
+        return i
 
     def A(n, lo=0, hi=None, st=1, p=128):
         t = T[n]
         hi = t.shape[1] if hi is None else hi
         return (t[0:p, lo:hi:st], (n, lo, hi)) if st > 1 else (t[0:p, lo:hi], (n, lo, hi))
 
-    def run(e, fn, reads, writes, inc=True):
-        rd, wr = [r[1] for r in reads], [w[1] for w in writes]
-        deps(e, e, rd, wr)
-        ins = fn(Q[e])
-        sem = "q" + e
-        val = cnt.get(sem, 0) + 1
-        if inc:
-            ins.then_inc(T.sem[sem], 1)
-            cnt[sem] = val
-        note(e, (sem, val, dict(known[e])), rd, wr)
+    def width(a):
+        return a[0].shape[1]
 
-    def dma(e, sem, out, in_, reads=(), writes=()):
-        rd, wr = [r[1] for r in reads], [w[1] for w in writes]
-        deps(e, "d" + sem, rd, wr)
-        Q[e].dma_start(out, in_).then_inc(T.sem[sem], 16)
-        cnt[sem] = cnt.get(sem, 0) + 16
-        note("d" + sem, (sem, cnt[sem], dict(known[e])), rd, wr)
+    def cyc(n, rate, *aps):
+        if aps and all(SCRATCH[a[1][0]][2] in ("bfloat16", "float16", "uint16") for a in aps):
+            rate /= 2
+        return max(64, n * rate) * CY
 
-    def arrives(buf, lo, hi, sem):
-        recs.setdefault(buf, []).append((lo, hi, 1, "r", (sem, EN, {})))
+    def dma(e, sem, out, in_, size, reads=(), writes=(), after=()):
+        return step({e: (lambda q: q.dma_start(out, in_), 0.05)}, reads, writes, HOP + size / 4e5, sem, 16, after=after)
 
     def send(buf, src, lo, hi, sem, to):
         dst = cores[to % N]
-        deps("g", "r", [(src, lo, hi)], [])
         rid, pid, _ = topo.addr(dst)
         m = 0
         for x in topo.engines(core, dst)[:EN]:
             m |= 1 << x
-        g.remote_dma(T[buf][:, lo:hi], T[src][:, lo:hi], T.sem[sem], T.sem["loc"], pid, rid, m)
-        cnt["loc"] = cnt.get("loc", 0) + EN
+        call = lambda q: q.remote_dma(T[buf][:, lo:hi], T[src][:, lo:hi], T.sem[sem], T.sem["loc"], pid, rid, m)
+        step({"g": (call, 0.3)}, [A(src, lo, hi)], [], HOP + 256 * (hi - lo) / 1e5, sem, -EN, (buf, lo, hi))
 
-    def mm(out, l, r, start=True, stop=True, inc=None):
-        run("p", lambda q: q.matmul(out[0], l[0], r[0], start, stop), [l, r], [out], stop if inc is None else inc)
+    def issue():
+        n = len(steps)
+        post = [[] for _ in steps]
+        for i, s in enumerate(steps):
+            for j in s["pre"]:
+                post[j].append(i)
+
+        def gap(j, i, ej, ei):
+            if j in steps[i]["order"] or (ej == ei and not steps[i]["pre"][j] and steps[j]["sem"] is None and steps[i]["sem"] is None):
+                return 0.0
+            return steps[j]["lat"]
+
+        first = [list(s["on"])[0] for s in steps]
+        way = [0.0] * n
+        for i in range(n - 1, -1, -1):
+            way[i] = steps[i]["on"][first[i]][1] + max([way[j] + gap(i, j, first[i], first[j]) for j in post[i]] + [steps[i]["lat"]])
+        left, free, eng, end = [len(s["pre"]) for s in steps], {e: 0.0 for e in Q}, [None] * n, [0.0] * n
+        pool, order = {e: {} for e in Q}, []
+
+        def offer(i):
+            for e in steps[i]["on"]:
+                pool[e][i] = max([end[j] + gap(j, i, eng[j], e) for j in steps[i]["pre"]] + [0.0])
+
+        for i in range(n):
+            if not left[i]:
+                offer(i)
+        while len(order) < n:
+            now, e = min((max(free[e], min(pool[e].values())), e) for e in Q if pool[e])
+            near = [i for i, r in pool[e].items() if r <= now + HOLD]
+            if e == "v":
+                near = [i for i, r in pool[e].items() if r <= now + SPARE and len(steps[i]["on"]) == 1] or near
+                near = [i for i in near if pool[e][i] <= max(now, min(pool[e][j] for j in near)) + HOLD]
+            i = max(near, key=lambda i: (way[i], -i))
+            free[e] = end[i] = max(now, pool[e][i]) + steps[i]["on"][e][1]
+            eng[i] = e
+            order.append(i)
+            for x in steps[i]["on"]:
+                del pool[x][i]
+            for j in post[i]:
+                left[j] -= 1
+                if not left[j]:
+                    offer(j)
+        cnt, known, tok = {}, {e: {} for e in Q}, {}
+        for i in order:
+            s, e = steps[i], eng[i]
+            k = known[e]
+            for j in sorted((j for j in s["pre"] if gap(j, i, eng[j], e)), key=lambda j: -tok[j][1]):
+                sem, val, vc = tok[j]
+                if k.get(sem, 0) < val:
+                    Q[e].wait_ge(T.sem[sem], val)
+                    k[sem] = val
+                    for s2, v2 in vc.items():
+                        k[s2] = max(k.get(s2, 0), v2)
+            ins = s["on"][e][0](Q[e])
+            if s["n"] < 0:
+                cnt["loc"] = cnt.get("loc", 0) + EN
+                tok[i] = (s["sem"], EN, {})
+                continue
+            sem = s["sem"] or "q" + e
+            if e != "p" or any(eng[j] != "p" for j in post[i]):
+                cnt[sem] = cnt.get(sem, 0) + s["n"]
+                ins.then_inc(T.sem[sem], s["n"])
+            tok[i] = (sem, cnt.get(sem, 0), dict(k))
+        for sem in OUTS + ["loc", "qv", "qs", "qp", "qg"]:
+            if cnt.get(sem, 0) > known["g"].get(sem, 0):
+                g.wait_ge(T.sem[sem], cnt[sem])
+
+    def mm(out, l, r, start=True, stop=True):
+        step({"p": (lambda q: q.matmul(out[0], l[0], r[0], start, stop), max(64, width(r)) * CY / 2)}, [l, r], [out])
 
     def copy(out, in_):
-        run("v", lambda q: q.tensor_copy(out[0], in_[0]), [in_], [out])
+        step({"v": (lambda q: q.tensor_copy(out[0], in_[0]), cyc(width(out), 1, out, in_))}, [in_], [out])
 
     def ts(out, in_, s1, op0, s2=None, op1=None):
         rd = [in_] + [s for s in (s1, s2) if isinstance(s, tuple)]
         a1 = s1[0] if isinstance(s1, tuple) else s1
         a2 = s2[0] if isinstance(s2, tuple) else s2
         if op1 is None:
-            run("v", lambda q: q.tensor_scalar(out[0], in_[0], a1, None, op0), rd, [out])
+            call = lambda q: q.tensor_scalar(out[0], in_[0], a1, None, op0)
         else:
-            run("v", lambda q: q.tensor_scalar(out[0], in_[0], a1, a2, op0, op1), rd, [out])
+            call = lambda q: q.tensor_scalar(out[0], in_[0], a1, a2, op0, op1)
+        step({"v": (call, cyc(width(out), 1, out, in_))}, rd, [out])
 
     def tt(out, a, b, op):
-        run("v", lambda q: q.tensor_tensor(out[0], a[0], b[0], op), [a, b], [out])
+        step({"v": (lambda q: q.tensor_tensor(out[0], a[0], b[0], op), cyc(width(out), 1 if b[1][0] in BANKS else 2))}, [a, b], [out])
 
-    def act(out, in_, fn, acc=None, **kw):
+    def act(out, in_, fn, **kw):
         rd = [in_] + [x for x in kw.values() if isinstance(x, tuple)]
         kw = {n: x[0] if isinstance(x, tuple) else x for n, x in kw.items()}
-        if acc is not None:
-            kw["accum_out"] = acc[0]
-        run("s", lambda q: q.activation(out[0], in_[0], fn, **kw), rd, [out] if acc is None else [out, acc])
+        step({"s": (lambda q: q.activation(out[0], in_[0], fn, **kw), 0.03 + cyc(width(out), 1))}, rd, [out])
 
-    def gather_v(out, win, off):
-        run("v", lambda q: q.tensor_copy(out[0], win[0].indirect(off[0])), [win, off], [out])
+    def lin(out, in_, scale, bias, on="sv"):
+        col = isinstance(bias, tuple)
+        b = bias[0] if col else bias
+        calls = {"s": (lambda q: q.activation(out[0], in_[0], ACTF.Identity if col else ACTF.Copy, scale=scale, bias=b), 0.03 + cyc(width(out), 1)),
+                 "v": (lambda q: q.tensor_scalar(out[0], in_[0], scale, b, ALU.mult, ALU.add), cyc(width(out), 1, out, in_))}
+        step({e: calls[e] for e in on}, [in_, bias] if col else [in_], [out])
 
-    def gather_s(out, win, off):
-        run("s", lambda q: q.activation(out[0], win[0].indirect(off[0]), ACTF.Copy), [win, off], [out])
+    def gather(out, win, off, on="sv"):
+        c = width(out) * GA * CY
+        calls = {"s": (lambda q: q.activation(out[0], win[0].indirect(off[0]), ACTF.Copy), 0.03 + c),
+                 "v": (lambda q: q.tensor_copy(out[0], win[0].indirect(off[0])), c)}
+        step({e: calls[e] for e in on}, [win, off], [out])
+
+    def gather_tt(out, win, off, b, op):
+        step({"v": (lambda q: q.tensor_tensor(out[0], win[0].indirect(off[0]), b[0], op), width(out) * GA * CY)}, [win, off, b], [out])
 
     def fill(out, c):
-        run("v", lambda q: q.memset(out[0], c), [], [out])
+        step({"v": (lambda q: q.memset(out[0], c), cyc(width(out), 1, out))}, [], [out])
 
-    def iota(out, pattern, base, cm):
-        run("g", lambda q: q.iota(out[0], pattern, base, cm), [], [out])
+    def iota(out, pattern, cm, small=True):
+        kw = {"allow_small_or_imprecise_dtypes": True} if small else {}
+        step({"g": (lambda q: q.iota(out[0], pattern, 0, cm, **kw), 0.13 + 2 * width(out) * CY)}, [], [out])
 
-    arrives("zi0", 0, G, "za0")
-    arrives("li0", 0, CH, "la0")
-    arrives("li0", CH, 2 * CH, "lb0")
-    arrives("li0", 2 * CH, G, "lc0")
-    for t in range(NT):
-        for c in range(NC):
-            arrives("nm%d" % t, 16 * c, 16 * c + 16, "nm%d%d" % (t, c))
-            arrives("zi%d" % (t + 1), CH * c, CH * c + CH, "za%d%d" % (t + 1, c))
-            if t:
-                arrives("li%d" % t, CH * c, CH * c + CH, "la%d%d" % (t, c))
+    c1, c2, LC = CHS[1], CHS[2], NC - 1
+    d = dma("s", "ld_z", T.zst[:], T.z0[:], 131072, writes=[A("zst")])
+    dma("s", "ld_wt", T.wti[:, 0:1], T.wt[:], 131072, writes=[A("wti", 0, 1)], after=[d])
+    d = dma("y", "ld_mv", T.mvs[:], T.mv[:], 131072, writes=[A("mvs")])
+    d = dma("y", "ld_p", T.pt0[:], T.vp[:], 655360, writes=[A("pt0")], after=[d])
+    dma("y", "ld_r", T.rw[:, 0:4096], T.strat[:], 1703936, writes=[A("rw", 0, 4096)], after=[d])
 
-    dma("s", "ld_z", T.zst[:], T.z0[:], writes=[A("zst")])
-    dma("y", "ld_mv", T.mvs[:], T.mv[:], writes=[A("mvs")])
-    dma("y", "ld_p", T.pt[:, 0:1024], T.vp[:], writes=[A("pt", 0, 1024)])
-    dma("s", "ld_wt", T.wti[:, 0:1], T.wt[:], writes=[A("wti", 0, 1)])
-    dma("s", "ld_r", T.rw[:, 0:4096], T.strat[:], writes=[A("rw", 0, 4096)])
-    dma("y", "ld_o", T.ot[:, 0:1024], T.vo[:], writes=[A("ot", 0, 1024)])
+    def shifted(buf, src, sem, after):
+        dma("y", sem, T[buf][1:128, 0:1024], src[0:127, :], 524288, reads=[after], writes=[A(buf, 0, 1024)])
+        recs[buf].append((0, 1024, 1, dma("y", sem + "0", T[buf][0:1, 0:1024], src[0:1, :], 4096, reads=[after])))
 
     C = lambda i: A("col", i, i + 1)
-    cp, ck, cg16, cz15, c37, ck16, c8k, cj0, cj1, cnl, cshp, cthr, cw, cg, ct, cadd = [C(i) for i in range(16)]
-    cv = [C(16 + i) for i in range(NT)]
+    cp, ck, cg16, cz15, c37, ck16, c8k, cj0, cp1, cp2, m15, m14, chit, crel, ck1, ca15, cw, cq, cadd, cyp = [C(i) for i in range(20)]
 
-    def addr1(t, lo, hi):
-        mm(A("pu", 0, hi - lo), A("bw"), A("zi%d" % t, lo, hi))
+    def zi(t, *r):
+        return A("zi%d" % t, *r)
 
-    def addr2(t, lo, hi):
+    def address(t, lo, hi):
         n = hi - lo
         pu = A("pu", 0, n)
-        ts(A("qf", lo, hi), pu, 1.0 / 4096, ALU.mult, 1025 - 2047.5 / 4096, ALU.add)
-        mm(pu, A("kc"), A("one", 0, n), True, False)
-        mm(pu, A("bw"), A("zi%d" % t, lo, hi), False, False)
+        mm(pu, A("bw"), zi(t, lo, hi))
+        lin(A("qf", lo, hi), pu, 1.0 / 4096, cq if t else QO - 2047.5 / 4096)
+        mm(pu, A("kcw" if t else "kc"), A("neg", 0, n), True, False)
+        mm(pu, A("bw"), zi(t, lo, hi), False, False)
         mm(pu, A("i4"), A("qf", lo, hi), False, True)
-
-    def addr3(t, lo, hi):
-        tt(A("xi", lo, hi), A("li%d" % t, lo, hi), A("pu", 0, hi - lo), ALU.mult)
+        tt(A("xi", lo, hi), A("li%d" % t, lo, hi), pu, ALU.mult)
         ts(A("ai", lo, hi), A("xi", lo, hi), 5, ALU.arith_shift_right, 4095, ALU.bitwise_and)
 
-    def addr(t, lo, hi):
-        addr1(t, lo, hi)
-        addr2(t, lo, hi)
-        addr3(t, lo, hi)
+    def columns(t, c):
+        a, b = CHS[c], CHS[c + 1]
+        lin(A("of%d" % t, a, b), A("ai", a, b), 1.0, cadd if t else c37)
+        for i in range(a, b, PC):
+            gather(A("yy", 16 * i, 16 * (i + PC)), A("rw", 0, RW), A("of%d" % t, i, i + PC))
 
-    def afin(t, lo, hi):
-        ts(A("of%d" % t, lo, hi), A("ai", lo, hi), cadd if t else c37, ALU.add)
-
-    def gath(t, c, pieces, e="s"):
-        for s in pieces:
-            i0 = CH * c + 32 * s
-            (gather_s if e == "s" else gather_v)(A("yy", 16 * i0, 16 * i0 + 512), A("rw", 0, RW), A("of%d" % t, i0, i0 + 32))
-
-    def blk(c, q):
-        return (2048 * c + 512 * q, 2048 * c + 512 * q + 512)
-
-    def zx(t, c):
-        for e in range(4):
-            mm(A("pz", e, 512, 4), A("ib"), A("zi%d" % t, CH * c, CH * c + CH), inc=e == 3)
-
-    def cmpv(t, c, qs):
-        for q in qs:
-            tt(A("bt", *blk(c, q)), A("yy", 2048 * c + q, 2048 * c + 2048, 4), A("pz"), ALU.is_gt)
-
-    def count(t, c):
-        ks = [(q, m) for q in range(4) for m in range(4)]
-        for n, (q, m) in enumerate(ks):
-            k = 4 * m + q
-            lo, hi = blk(c, q)
-            mm(A("pc", 0, CH), A("zb_", 15 - k, 143 - k), A("bt", lo + m, hi, 4), n == 0, n == 15)
+    def beats(t, c):
+        a, b, pz = CHS[c], CHS[c + 1], "pz%d" % ((t * NC + c) % 2)
+        n = b - a
+        if t:
+            mm(A(pz, 0, 4 * n), A("ib"), A("neg", 0, 4 * n), True, False)
+        for j in range(4):
+            mm(A(pz, j, 4 * n, 4), A("ib"), zi(t, a, b), not t, not t or j == 3)
+        lo = 16 * a
+        for q, s in ((0, 4), (1, 4), (2, 4), (3, 8), (7, 16)):
+            e = 16 // s
+            tt(A("bt", lo, lo + e * n), A("yy", 16 * a + q, 16 * b, s), A(pz, 0, 4 * n, s // 4), ALU.is_gt)
+            for j in range(e):
+                k = q + s * j
+                mm(A("pc", 0, n), A("zb_", 15 - k, 143 - k), A("bt", lo + j, lo + e * n, e), k == 0, k == 7)
+            lo += e * n
 
     def scan(t, c, hi):
-        s = (2048 * c, 2048 * c + 2048)
-        o, m = (A("hi", *s), A("mhi")) if hi else (A("lo", *s), A("mlo"))
+        a, b = CHS[c], CHS[c + 1]
+        s = (16 * a, 16 * b)
+        o, m = (A("hi", *s), A("mhi", 0, 16 * (b - a))) if hi else (A("lo", *s), A("mlo", 0, 16 * (b - a)))
         o0, o1 = (ALU.min, ALU.max) if hi else (ALU.max, ALU.min)
         y = A("yy", *s)
-        run("v", lambda q: q.tensor_tensor_scan(o[0], m[0], y[0], 0.0, o0, o1), [m, y], [o])
+        step({"v": (lambda q: q.tensor_tensor_scan(o[0], m[0], y[0], 0.0, o0, o1), cyc(width(o), 1, o))}, [m, y], [o])
 
-    def hits(t, c):
-        h = A("hit", CH * c, CH * c + CH)
-        ts(h, A("pc", 0, CH), cthr, ALU.is_ge)
-        mm(A("pd0", 0, CH), A("tri"), h)
-        mm(A("pf", 0, CH), A("tri"), h)
-        act(A("pr", 0, CH), A("pd0", 0, CH), ACTF.Relu, acc=A("acc", 4 * t + c, 4 * t + c + 1), scale=4096.0)
+    def vlist(buf, t, c, second):
+        a, b = CHS[c] // 8, CHS[c + 1] // 8
+        m = (a + b) // 2
+        return A("%s%d" % (buf, t), m, b) if second else A("%s%d" % (buf, t), a, m)
 
-    def lists1(t, c):
-        o = 2 * CH * c
-        ts(A("oh", o, o + CH), A("pf", 0, CH), 0.0, ALU.max, ck, ALU.mult)
-        tt(A("oh", o + CH, o + 2 * CH), A("li%d" % t, CH * c, CH * c + CH), A("pr", 0, CH), ALU.min)
-        pl = A("pf", 256, 272)
-        mm(pl, A("ih"), A("cst"), True, False)
+    def verdict(t, c):
+        a, b = CHS[c], CHS[c + 1]
+        n, s = b - a, A("sg", a, b)
+        act(s, A("pc", 0, n), ACTF.Sign, bias=chit)
+        mm(A("pf", 0, n), A("ib"), A("k1", 0, n), True, False)
+        mm(A("pf", 0, n), A("tri"), s, False, True)
+        mm(A("pf", n, 2 * n), A("ib"), A("li%d" % t, a, b), True, False)
+        mm(A("pf", n, 2 * n), A("tri"), s, False, True)
+        act(A("oh", 2 * a, 2 * b), A("pf", 0, 2 * n), ACTF.Relu, bias=crel)
+        pl = A("pl", 0, n // 8)
+        mm(pl, A("ib"), A("cst", a // 8, b // 8), True, False)
         for k in range(16):
-            mm(pl, A("zh_", 15 - k, 143 - k), A("oh", o + k, o + 2 * CH, 16), False, k == 15)
+            mm(pl, A("zb_", 15 - k, 143 - k), A("oh", 2 * a + k, 2 * b, 16), False, k == 15)
+        lin(A("sb%d" % t, a // 8, b // 8), pl, 1.0, 0.0, "vs")
+        send("nm%d" % t, "sb%d" % t, (a + b) // 16, b // 8, "nm%d%d" % (t, c), me - 1 - t)
 
-    def lists2(t, c):
-        copy(A("sb%d" % t, 16 * c, 16 * c + 16), A("pf", 256, 272))
-        send("nm%d" % t, "sb%d" % t, 16 * c, 16 * c + 16, "nm%d%d" % (t, c), me - 1 - t)
+    def newz(t, c):
+        a, b = CHS[c], CHS[c + 1]
+        last = t + 1 == NT
+        gather(A("hp", a, b), A("hi", 16 * a, 16 * b), vlist("sb", t, c, 0))
+        gather(A("lp", a, b), A("lo", 16 * a, 16 * b), vlist("sb", t, c, 0))
+        mm(A("ph", 0, b - a), A("hib"), A("hp", a, b), True, False)
+        mm(A("ph", 0, b - a), A("hib"), A("lp", a, b), False, True)
+        lin(A("z16" if last else "zo%d" % t, a, b), A("ph", 0, b - a), 1.0, ZO - 0.25)
+        if last:
+            lin(A("zo%d" % t, a, b), A("z16", a, b), 1.0, -ZO, "vs")
+        send("zi%d" % (t + 1), "zo%d" % t, a, b, "za%d%d" % (t + 1, c), me - 1 - t if last else me + 1)
 
-    def pick1(t, c):
-        a, b = CH * c, CH * c + CH
-        gather_s(A("hp", a, b), A("hi", 16 * a, 16 * b), A("sb%d" % t, 16 * c, 16 * c + 8))
-        if c < 3:
-            gather_s(A("lp", a, b), A("lo", 16 * a, 16 * b), A("sb%d" % t, 16 * c, 16 * c + 8))
+    def window(lo):
+        return A("rw", 0, 8 * SEG) if lo < SEG else A("rw", 8 * SEG, 4096)
 
-    def send_z(t, c):
-        send("zi%d" % (t + 1), "zo%d" % t, CH * c, CH * c + CH, "za%d%d" % (t + 1, c), me + 1 if t + 1 < NT else me - 1 - t)
-
-    def half(p, a, b, lo, hi):
-        mm(p, A("kq"), A("one", lo, hi), True, False)
-        mm(p, A("hib"), A(a, lo, hi), False, False)
-        mm(p, A("hib"), A(b, lo, hi), False, True)
-
-    def whole(out, p, lo, hi):
-        act(A("big", lo, hi), p, ACTF.Copy, bias=BIG)
-        act(A(out, lo, hi), A("big", lo, hi), ACTF.Copy, bias=-BIG)
-
-    def pick3(t, c):
-        half(A("pr", CH, 2 * CH), "hp", "lp", CH * c, CH * c + CH)
-        whole("zo%d" % t, A("pr", CH, 2 * CH), CH * c, CH * c + CH)
-        send_z(t, c)
-
-    def pick2(t, c):
-        a, b = CH * c, CH * c + CH
-        off, w, h, s = A("sb%d" % t, 16 * c, 16 * c + 8), A("lo", 16 * a, 16 * b), A("hp", a, b), A("sm", a, b)
-        run("v", lambda q: q.tensor_tensor(s[0], w[0].indirect(off[0]), h[0], ALU.add), [w, off, h], [s])
-        ts(A("z16", a, b), s, 0.5, ALU.mult, 1024.75, ALU.add)
-        ts(A("zo%d" % t, a, b), A("z16", a, b), -1025.0, ALU.add)
-        send_z(t, c)
-
-    def place1(t):
+    def place(t):
         for k in range(16):
-            mm(A("pr", 256, 288), A("zw_", 15 - k, 143 - k), A("zi%d" % t, k, G, 16), k == 0, k == 15)
-
-    def place2(t):
-        copy(A("pli"), A("pr", 256, 288))
+            mm(A("pe", 0, 32), A("zw_", 15 - k, 143 - k), zi(t, k, G, 16), k == 0, k == 15)
+        copy(A("pli"), A("pe", 0, 32))
         ts(A("plm"), A("pli"), 7, ALU.bitwise_and)
         tt(A("pli"), A("plm"), A("c8"), ALU.add)
         copy(A("plu"), A("pli"))
+        for lo, hi in ((0, SEG), (SEG, G)):
+            o, w, x = A("old", lo, hi), window(lo), A("plu", lo // 16, hi // 16)
+            step({"s": (lambda q, o=o, w=w, x=x: q.activation(o[0], w[0].indirect(x[0]), ACTF.Copy, scale=2.0), 0.03 + (hi - lo) * GA * CY)}, [w, x], [o])
 
-    def olds(t):
-        gather_s(A("old"), A("rw", 0, 4096), A("plu"))
+    def update(t, lo, hi):
+        p = A("pe", 0, hi - lo)
+        mm(p, A("qib"), A("old", lo, hi), True, False)
+        mm(p, A("hib"), A("zo%d" % t, lo, hi), False, True)
+        lin(A("nw", lo, hi), p, 1.0, -ZO / 2 - 0.25)
 
-    def upd1(t, lo, hi):
-        mm(A("ps", CH, CH + hi - lo), A("hib"), A("old", lo, hi), True, False)
-        mm(A("ps", CH, CH + hi - lo), A("hib"), A("zo%d" % t, lo, hi), False, True)
+    def update_v(t, c):
+        a, b = CHS[c], CHS[c + 1]
+        gather_tt(A("sm", a, b), A("hi", 16 * a, 16 * b), vlist("sb", t, c, 0), A("old", a, b), ALU.add)
+        gather_tt(A("s2", a, b), A("lo", 16 * a, 16 * b), vlist("sb", t, c, 0), A("sm", a, b), ALU.add)
+        ts(A("nw", a, b), A("s2", a, b), 0.25, ALU.mult, -0.375, ALU.add)
 
-    def upd2(t, lo, hi):
-        ts(A("nw", lo, hi), A("ps", CH, CH + hi - lo), -0.25, ALU.add)
-
-    def upd3(t, lo, hi):
-        p = A("ps", CH, CH + hi - lo)
-        half(p, "old", "zo%d" % t, lo, hi)
-        whole("nwb", p, lo, hi)
-
-    def scat(t, lo, hi, src):
-        w, o, i = A("rw", 0, 4096), A("plu", lo // 16, hi // 16), A(src, lo, hi)
-        run("v", lambda q: q.tensor_copy(w[0].indirect(o[0]), i[0]), [o, i], [w])
+    def scatter(t, lo, hi):
+        w, o, i = window(lo), A("plu", lo // 16, hi // 16), A("nw", lo, hi)
+        step({"v": (lambda q: q.tensor_copy(w[0].indirect(o[0]), i[0]), (hi - lo) * SC * CY)}, [o, i], [w])
 
     def mirror():
-        copy(A("rw", 4096, RW), A("rw", 0, RW - 4096))
+        lin(A("rw", 4096, RW), A("rw", 0, RW - 4096), 1.0, 0.0)
 
-    def tally1(t):
-        mm(A("pr", 320, 324), A("a15"), A("acc", 4 * t, 4 * t + 4))
-
-    def tally2(t):
-        o, i = A("an", 0, 1), A("pr", 320, 324)
-        run("v", lambda q: q.tensor_reduce(o[0], i[0], AxisListType.X, ALU.add, negate=True), [i], [o])
+    def tally(t):
+        cs = sorted(range(LC), key=lambda c: CHS[c] - CHS[c + 1]) + [LC]
+        for c in cs:
+            a, b = CHS[c], CHS[c + 1]
+            mm(A("pc", 128, 128 + b - a), A("a15"), A("oh", 2 * a, a + b), c == cs[0], c == LC)
+        o, i = A("an", 0, 1), A("pc", 128, 128 + CHS[cs[0] + 1] - CHS[cs[0]])
+        step({"v": (lambda q: q.tensor_reduce(o[0], i[0], AxisListType.X, ALU.add), cyc(width(i), 1))}, [i], [o])
         copy(A("ani", 0, 1), o)
         ts(A("ani", 1, 2), A("ani", 0, 1), 255, ALU.bitwise_and)
         ts(cadd, A("ani", 1, 2), c37, ALU.add)
 
-    def shift(t, src, lo, hi, b="ps"):
-        p = A(b, 0, hi - lo)
-        mm(p, A("sh"), A(src, lo, hi), True, False)
-        mm(p, A("nn%d" % t), A("it2", lo, hi), False, True)
+    def verdicts(t):
+        for c in range(NC):
+            for i in range(CHS[c], CHS[c + 1], 32):
+                j = i // 32
+                mm(A("pc", 256, 288), A("zb_", 15 - j, 143 - j), A("oh", CHS[c] + i, CHS[c] + i + 32), j == 0, j == 15)
+        lin(A("vs%d" % t), A("pc", 256, 288), 1.0, -1.0)
+        send("vi%d" % t, "vs%d" % t, 0, 32, "va%d" % t, me - 1 - t)
+        dma("y", "o_k%d" % t, T.yk[:, t * G:t * G + G], T["vi%d" % t][:], 16384, reads=[A("vi%d" % t)])
 
-    def home1(t, c):
-        a, b = CH * c, CH * c + CH
-        gather_v(A("res", a, b), A(("ot", "pt", "ot")[t], 0, 1024 + 512 * t), A("nm%d" % t, 16 * c + 8, 16 * c + 16))
-
-    def home2(t, c):
-        a, b = CH * c, CH * c + CH
-        p = A("ps", 0, CH)
+    def home(t, c):
+        a, b = CHS[c], CHS[c + 1]
+        out = A("ls%d" % (t + 1) if t + 1 < NT else "yos", a, b)
+        gather_tt(out, A(("ots", "pts", "ots")[t], 0, 1024 + 512 * t), vlist("nm", t, c, 1), A("nr%d" % t, a, b), ALU.max)
         if t + 1 < NT:
-            copy(A("ls%d" % (t + 1), a, b), p)
             send("li%d" % (t + 1), "ls%d" % (t + 1), a, b, "la%d%d" % (t + 1, c), me + 2 + t)
-            if t == 0:
-                copy(A("ot", 1024 + a, 1024 + b), p)
+
+    def extend(t):
+        p = A("pe")
+        if t == 1:
+            mm(p, A("sh1"), A("ls1"))
+            lin(A("ots", 1024, 1536), p, 1.0, 0.0)
+        if t < 2:
+            mm(p, A("sh2"), A("ls%d" % t), True, False)
+            mm(p, A("sh1"), A("nr%d" % t), False, True)
+            lin(A("ots", 1536, 2048) if t else A("pts", 1024, 1536), p, 1.0, 0.0)
         else:
-            act(A("yos", a, b), p, ACTF.Copy)
-        copy(A("kint", 8 * c, 8 * c + 8), A("nm%d" % t, 16 * c, 16 * c + 8))
+            mm(p, A("sh1"), A("ls2"), True, False)
+            mm(p, A("ib"), A("nr1"), False, True)
+            lin(A("yps"), p, 1.0, cyp)
+            dma("y", "o_p", T.yp[:], T.yps[:], 262144, reads=[A("yps")])
 
-    def ext2(t):
-        p = A("pu", 0, G)
-        if t == 0:
-            copy(A("pt", 1024, 1536), p)
-        elif t == 1:
-            copy(A("ot", 1536, 2048), p)
-        else:
-            act(A("yps"), p, ACTF.Copy)
-            dma("y", "o_p", T.yp[:], T.yps[:], reads=[A("yps")])
-
-    def kand(t):
-        ts(A("kand"), A("kint"), 15, ALU.bitwise_and)
-        copy(A("kf"), A("kand"))
-
-    def verd1(t):
-        for k in range(16):
-            mm(A("pd1", k, 512, 16, p=8), A("ib", k, 128, 16), A("kf"), inc=k == 15)
-
-    def verd2(t):
-        act(A("yks", t * G, t * G + G, p=8), A("pd1", 0, 512, p=8), ACTF.Copy)
-        dma("y", "o_k%d" % t, T.yk[:, t * G:t * G + G], T.yks[0:8, t * G:t * G + G], reads=[A("yks", t * G, t * G + G)])
-
-    iota(A("pint", 0, 1), [[1, 1]], 0, 1)
-    iota(A("xint"), [[1, G]], 0, 0)
-    X, X144 = A("xx", 0, 128), A("xx", 0, 144)
+    iota(A("pint", 0, 1), [[1, 1]], 1, False)
+    iota(A("xb"), [[1, 144]], 0)
+    iota(A("xg"), [[16, 8], [0, 16]], 0)
+    iota(A("xx"), [[1, G]], 0)
+    X = A("xb", 0, 128)
+    fill(A("neg"), -ZO)
+    fill(A("kc"), -32.0)
+    fill(A("kc", p=1), -1.0)
+    fill(A("cst"), 0.0)
     ts(A("pint", 1, 2), A("pint", 0, 1), 15, ALU.bitwise_and)
     copy(cp, A("pint", 0, 1))
     copy(ck, A("pint", 1, 2))
-    tt(cg16, cp, ck, ALU.subtract)
-    ts(c37, ck, 37.0, ALU.mult)
-    ts(ct, cp, 0.0, ALU.is_equal, 32.0, ALU.mult)
-    ts(cg, cg16, 1.0 / 16, ALU.mult)
-    ts(cz15, cg16, 15.0, ALU.add)
-    ts(ct, ct, 32800.0, ALU.add)
-    copy(A("xx"), A("xint"))
-    send("zi0", "zst", 0, G, "za0", me + 1)
-    ts(A("xgi"), A("xint", 0, 128), 4, ALU.arith_shift_right)
-    ts(A("one"), A("xx"), 0.0, ALU.mult, 1.0, ALU.add)
-    copy(A("xg"), A("xgi"))
-    ts(A("kc"), X, 0.0, ALU.mult, ct, ALU.add)
-    ts(A("i4"), X, cp, ALU.is_equal, -4096.0, ALU.mult)
-    ts(A("ib"), X, cp, ALU.is_equal)
-    copy(A("mvu"), A("mvs"))
-    ts(A("kq"), X, 0.0, ALU.mult, -2.0 ** -9, ALU.add)
-    ts(A("zb_"), X144, cz15, ALU.is_equal)
-    ts(A("zh_"), X144, cz15, ALU.is_equal)
-    ts(A("bb"), A("xg"), cg, ALU.is_equal)
-    ts(A("tr2"), X, cp, ALU.is_gt)
-    ts(A("ih"), X, cp, ALU.is_equal)
-    tt(A("tr2"), A("tr2"), A("bb"), ALU.mult)
-    gather_v(A("ls0", 0, CH), A("pt", 0, 1024), A("mvu", 0, CH // 16))
-    send("li0", "ls0", 0, CH, "la0", me + 1)
-    gather_v(A("ls0", CH, G), A("pt", 0, 1024), A("mvu", CH // 16, 32))
-    send("li0", "ls0", CH, 2 * CH, "lb0", me + 1)
-    send("li0", "ls0", 2 * CH, G, "lc0", me + 1)
     copy(cw, A("wti", 0, 1))
-    ts(ck16, ck, 16.0, ALU.mult)
-    ts(A("bw"), A("xg"), cg, ALU.is_equal, cw, ALU.mult)
-    tt(A("tri"), A("ib"), A("tr2"), ALU.subtract)
-    ts(ct, ck, 15.0, ALU.is_equal, 1.0 / 4096, ALU.mult)
-    act(A("hib"), A("ib"), ACTF.Copy, scale=0.5)
-    act(A("zw_"), A("zb_"), ACTF.Copy, scale=cw)
-    act(A("a15"), X, ACTF.Identity, scale=0.0, bias=ct)
-    for i in range(0, 16 * CH, G):
-        act(A("mhi", i, i + G), A("xx"), ACTF.Copy, scale=0.0, bias=256.0)
-        act(A("mlo", i, i + G), A("xx"), ACTF.Copy, scale=0.0)
-    act(A("mhi", 0, 16 * CH, 16), X, ACTF.Copy, scale=0.0)
-    act(A("mlo", 0, 16 * CH, 16), X, ACTF.Copy, scale=0.0, bias=256.0)
+    tt(cg16, cp, ck, ALU.subtract)
+    for i in range(0, 2048, G):
+        lin(A("mhi", i, i + G), A("neg"), 0.0, 256.0)
+        lin(A("mlo", i, i + G), A("neg"), 0.0, 0.0)
+    lin(A("mhi", 0, 2048, 16), A("neg", 0, 128), 0.0, 0.0)
+    lin(A("mlo", 0, 2048, 16), A("neg", 0, 128), 0.0, 256.0)
+    ts(cz15, cg16, 15.0, ALU.add)
+    ts(c37, ck, 37.0, ALU.mult)
+    ts(ck1, ck, 1.0, ALU.add)
     ts(cj0, ck, 0.0, ALU.is_equal)
-    ts(cj1, ck, 1.0, ALU.is_equal)
-    ts(cnl, ck, 15.0, ALU.is_lt)
-    ts(cshp, cp, 1.0, ALU.add)
+    ts(m15, ck, 15.0, ALU.is_lt)
+    ts(m14, ck, 14.0, ALU.is_lt)
+    ts(cp1, cp, 1.0, ALU.add)
+    ts(cp2, cp, 2.0, ALU.add)
+    ts(crel, ck, 1.0, ALU.add, -2048.0, ALU.mult)
+    ts(ca15, ck, 15.0, ALU.is_equal, -1.0 / 16, ALU.mult)
+    ts(ck16, ck, 16.0, ALU.mult, -1.0, ALU.add)
     ts(c8k, ck, 8.0, ALU.mult)
-    ts(A("it2"), A("xx"), cj0, ALU.mult, cj1, ALU.add)
+    ts(chit, m15, -100.0, ALU.mult, 91.5, ALU.add)
+    ts(cyp, cj0, 512.0, ALU.mult)
+    ts(A("ib"), X, cp, ALU.is_equal)
+    for name, x in (("i4", -4096.0), ("hib", 0.5), ("qib", 0.25), ("tri", 2048.0)):
+        ts(A(name), X, cp, ALU.is_equal, x, ALU.mult)
+    ts(A("zb_"), A("xb"), cz15, ALU.is_equal)
+    ts(A("zw_"), A("xb"), cz15, ALU.is_equal, cw, ALU.mult)
+    ts(A("bw"), A("xg"), cg16, ALU.is_equal, cw, ALU.mult)
+    tt(A("kcw"), A("bw"), A("kc"), ALU.add)
+    ts(A("tr1"), X, cp, ALU.is_gt, -2048.0, ALU.mult)
+    ts(A("tr2"), X, cz15, ALU.is_gt, 2048.0, ALU.mult)
+    tt(A("tr1"), A("tr1"), A("tr2"), ALU.add)
+    tt(A("tri"), A("tri"), A("tr1"), ALU.add)
+    ts(A("sh1"), X, cp1, ALU.is_equal, m15, ALU.mult)
+    ts(A("sh2"), X, cp2, ALU.is_equal, m14, ALU.mult)
+    ts(A("a15"), X, 0.0, ALU.mult, ca15, ALU.add)
+    ts(A("k1"), X, 0.0, ALU.mult, ck1, ALU.add)
+    mm(A("ph", 0, 2), A("bw"), A("neg", 0, 2))
+    ts(cq, A("ph", 0, 1), 1.0 / 4096, ALU.mult, QO - 2047.5 / 4096, ALU.add)
+    ts(A("c8", 0, SEG // 16), A("xx", 0, SEG // 16), 128.0, ALU.mult, c8k, ALU.add)
+    ts(A("c8", SEG // 16, 32), A("xx", 0, 32 - SEG // 16), 128.0, ALU.mult, c8k, ALU.add)
+    for c in range(NC):
+        a, b = CHS[c], CHS[c + 1]
+        ts(A("cst", a // 8, (a + b) // 16), A("xx", 0, (b - a) // 16), 256.0, ALU.mult, ck16, ALU.add)
     for t in range(NT):
-        ts(cv[t], cj1, 1024.0 + 512 * t, ALU.mult)
-    ts(A("sh"), X, cshp, ALU.is_equal, cnl, ALU.mult)
-    for t in range(NT):
-        tt(cv[t], cv[t], cj0, ALU.add)
-    for t in range(NT):
-        ts(A("nn%d" % t), X, cg16, ALU.is_equal, cv[t], ALU.mult)
-    ts(A("c8"), A("xx", 0, 32), 128.0, ALU.mult, c8k, ALU.add)
-    ts(cthr, ck, 15.0, ALU.is_equal, -100.0, ALU.mult)
-    ts(A("cst", 8, 16), A("xx", 0, 8), 0.0, ALU.mult)
-    ts(cthr, cthr, 9.0, ALU.add)
-    ts(A("cst", 0, 8), A("xx", 0, 8), 256.0, ALU.mult, ck16, ALU.add)
-    addr(0, 0, CH)
-    afin(0, 0, CH)
+        ts(A("nr%d" % t), A("xx"), 1024.0 + 512 * t, ALU.add, cj0, ALU.mult)
+    send("zi0", "zst", 0, c2, "za0", me + 1)
+    send("zi0", "zst", c2, G, "zb0", me + 1)
+    copy(A("mvu"), A("mvs"))
+    gather(A("ls0", 0, c1), A("pt0"), A("mvu", 0, c1 // 16), "v")
+    gather(A("ls0", c1, G), A("pt0"), A("mvu", c1 // 16, 32), "v")
+    send("li0", "ls0", 0, c1, "la0", me + 1)
+    send("li0", "ls0", c1, c2, "lb0", me + 1)
+    send("li0", "ls0", c2, G, "lc0", me + 1)
     mirror()
-    gath(0, 0, [s for s in range(4) if s not in DG])
-    gath(0, 0, DG, "v")
-    addr(0, CH, 2 * CH)
-    afin(0, CH, 2 * CH)
-    gath(0, 1, (0, 1))
-    zx(0, 0)
+    shifted("ots", T.vo, "ld_o", A("rw", 0, 16))
 
     for t in range(NT):
         last = t + 1 == NT
-        if t:
-            afin(t, 0, CH)
-            gath(t, 0, [s for s in range(4) if s not in DG])
-            gath(t, 0, DG, "v")
-            zx(t, 0)
-            addr3(t, CH, 2 * CH)
-            afin(t, CH, 2 * CH)
-            gath(t, 1, (0, 1))
-            home1(t - 1, 2)
-            shift(t - 1, "res", 2 * CH, 3 * CH)
-            if t > 1:
-                verd1(t - 2)
-                verd2(t - 2)
         for c in range(NC):
-            n = c + 1 if c + 1 < NC else None
-            j = None
-            if t and c < 2:
-                j = (t, CH * (c + 2), CH * (c + 3))
-            elif c == 0:
-                j = (0, 2 * CH, G)
-            elif c == 3 and not last:
-                j = (t + 1, 0, CH)
-            if j and c < 3:
-                addr1(*j)
-            cmpv(t, c, (0, 1))
-            if t and c == 0:
-                home2(t - 1, 2)
-            if n and c:
-                gath(t, n, (0,))
-            if c:
-                lists2(t, c - 1)
-                pick1(t, c - 1)
-                if n:
-                    gath(t, n, (1,))
-            cmpv(t, c, (2, 3))
+            address(t, CHS[c], CHS[c + 1])
+            columns(t, c)
+        if not last:
+            place(t)
+        for c in range(NC):
+            beats(t, c)
             scan(t, c, True)
-            count(t, c)
-            if c:
-                pick3(t, c - 1)
-            if c >= 2:
-                shift(t, "res", CH * (c - 2), CH * (c - 1))
-            if j and c < 3:
-                addr2(*j)
-            if t and c == 0:
-                home1(t - 1, 3)
-                shift(t - 1, "res", 3 * CH, G)
-            hits(t, c)
-            if c == 1 and not last:
-                place1(t)
-            if c == 2:
-                shift(t, "ls%d" % t, 0, G, "pu")
-            if n:
-                gath(t, n, (2, 3))
-            if c == 2 and not last:
-                olds(t)
-            if c == 3:
-                home2(t, 1)
-            if c < 3:
-                scan(t, c, False)
-                if c == 2:
-                    home2(t, 0)
-                if j and c:
-                    addr3(*j)
-                    afin(*j)
-            elif not last:
-                addr1(*j)
-                addr2(*j)
-                upd3(t, 0, 3 * CH)
-            if t and c == 0:
-                home2(t - 1, 3)
-            if c + 1 < NC:
-                zx(t, c + 1)
-            lists1(t, c)
-            if j and c == 0:
-                addr3(*j)
-                afin(*j)
-            if c == 3:
-                scan(t, c, False)
-                if not last:
-                    addr3(*j)
-            if c == 1 and not last:
-                place2(t)
-            if c == 2:
-                ext2(t)
-            if 1 <= c < 3:
-                home1(t, c - 1)
-            if t and c == 1:
-                kand(t - 1)
-        lists2(t, 3)
-        pick1(t, 3)
+            scan(t, c, False)
+            verdict(t, c)
+            newz(t, c)
+            home(t, c)
+            if c == 1:
+                extend(t)
+            if not last and c < LC:
+                update(t, CHS[c], CHS[c + 1])
+        if t == 0:
+            shifted("pts", T.vp, "ld_q", A("sb0", 0, 2))
         if not last:
-            addr1(t + 1, CH, 2 * CH)
-            scat(t, 0, 3 * CH, "nwb")
-            tally1(t)
-            act(A("rw", 4096, RW), A("rw", 0, RW - 4096), ACTF.Copy)
-            addr2(t + 1, CH, 2 * CH)
-        pick2(t, 3)
-        if not last:
-            upd1(t, 3 * CH, G)
-            tally2(t)
-            upd2(t, 3 * CH, G)
-            scat(t, 3 * CH, G, "nw")
-    home1(2, 2)
-    shift(2, "res", 2 * CH, 3 * CH)
-    verd1(1)
-    home2(2, 2)
-    verd2(1)
-    dma("y", "o_o0", T.yo[:, 0:3 * CH], T.yos[:, 0:3 * CH], reads=[A("yos", 0, 3 * CH)])
-    dma("y", "o_z0", T.yz[:, 0:3 * CH], T.zi3[:, 0:3 * CH], reads=[A("zi3", 0, 3 * CH)])
-    home1(2, 3)
-    shift(2, "res", 3 * CH, G)
-    home2(2, 3)
-    dma("s", "o_o1", T.yo[:, 3 * CH:G], T.yos[:, 3 * CH:G], reads=[A("yos", 3 * CH, G)])
-    kand(2)
-    verd1(2)
-    verd2(2)
-    dma("y", "o_z1", T.yz[:, 3 * CH:G], T.zi3[:, 3 * CH:G], reads=[A("zi3", 3 * CH, G)])
-    for s in OUTS + ["loc", "qv", "qs", "qp", "qg"]:
-        if cnt.get(s, 0) > known["g"].get(s, 0):
-            g.wait_ge(T.sem[s], cnt[s])
+            update_v(t, LC)
+            tally(t)
+            for lo, hi in ((0, SEG), (SEG, CHS[LC - 1]), (CHS[LC - 1], CHS[LC]), (CHS[LC], G)):
+                scatter(t, lo, hi)
+            mirror()
+        verdicts(t)
+    b = CHS[LC]
+    dma("y", "o_o0", T.yo[:, 0:b], T.yos[:, 0:b], 512 * b, reads=[A("yos", 0, b)])
+    dma("y", "o_z0", T.yz[:, 0:b], T.zi3[:, 0:b], 256 * b, reads=[A("zi3", 0, b)])
+    dma("y", "o_o1", T.yo[:, b:G], T.yos[:, b:G], 512 * (G - b), reads=[A("yos", b, G)])
+    dma("s", "o_z1", T.yz[:, b:G], T.zi3[:, b:G], 256 * (G - b), reads=[A("zi3", b, G)])
+    issue()

@@ -3,14 +3,18 @@ from concourse.mybir import AluOpType as ALU, AxisListType, ActivationFunctionTy
 NT, G = 3, 512
 CHS = (0, 128, 256, 384, 448, 512)
 NC = len(CHS) - 1
-PC = 32
+UNITS = ((0, 1), (2, 3), (4,))
+PARTS = (0, 32, 64, 128, 192, 256, 320, 384, 448, 512)
 RW = 4096 + 816
 SEG = 128
 EN = 8
 ZO, QO = 1056.0, 1048.0
 CY, GA, SC = 0.83e-3, 1.5, 3.5
 LAT, HOP = 0.1, 1.6
-HOLD, SPARE = 0.1, 0.3
+FIX, CALL = 0.065, 0.45
+HOLD, SPARE = 0.05, 0.6
+SMALL = 0.25
+PASSES = 3
 
 SCRATCH = {
     "rw": ("sbuf", [128, RW], "bfloat16"), "pt0": ("sbuf", [128, 1024], "int32"),
@@ -49,11 +53,11 @@ BANKS = ("pz0", "pz1", "pu", "pc", "pf", "pl", "ph", "pe")
 for _b in BANKS:
     SCRATCH[_b] = ("psum", [128, 512], "float32")
 
-LDS = ["ld_mv", "ld_wt", "ld_z", "ld_p", "ld_r", "ld_o", "ld_o0", "ld_q", "ld_q0"]
+LDS = ["ld_mv", "ld_wt", "ld_z", "ld_p", "ld_r", "ld_o", "ld_o0", "ld_q", "ld_q0", "mir0", "mir1"]
 OUTS = ["o_p", "o_o0", "o_o1", "o_z0", "o_z1", "o_k0", "o_k1", "o_k2"]
-SEMAPHORES = ["qv", "qs", "qp", "qg", "loc", "za0", "zb0", "la0", "lb0", "lc0", "va0", "va1", "va2"] + LDS + OUTS
+SEMAPHORES = ["qv", "qs", "qp", "qg", "loc", "za0", "zb0", "zc0", "la0", "lb0", "lc0", "va0", "va1", "va2"] + LDS + OUTS
 for _t in range(NT):
-    for _c in range(NC):
+    for _c in range(len(UNITS)):
         SEMAPHORES += ["nm%d%d" % (_t, _c), "za%d%d" % (_t + 1, _c)]
         if _t:
             SEMAPHORES.append("la%d%d" % (_t, _c))
@@ -107,14 +111,14 @@ def rank_program(g, core, T, topo):
     def dma(e, sem, out, in_, size, reads=(), writes=(), after=()):
         return step({e: (lambda q: q.dma_start(out, in_), 0.05)}, reads, writes, HOP + size / 4e5, sem, 16, after=after)
 
-    def send(buf, src, lo, hi, sem, to):
+    def send(buf, src, lo, hi, sem, to, start=0.0, late=0.0):
         dst = cores[to % N]
         rid, pid, _ = topo.addr(dst)
         m = 0
         for x in topo.engines(core, dst)[:EN]:
             m |= 1 << x
         call = lambda q: q.remote_dma(T[buf][:, lo:hi], T[src][:, lo:hi], T.sem[sem], T.sem["loc"], pid, rid, m)
-        step({"g": (call, 0.3)}, [A(src, lo, hi)], [], HOP + 256 * (hi - lo) / 1e5, sem, -EN, (buf, lo, hi))
+        step({"g": (call, CALL + start)}, [A(src, lo, hi)], [], HOP + late + 256 * (hi - lo) / 1e5, sem, -EN, (buf, lo, hi))
 
     def issue():
         n = len(steps)
@@ -128,36 +132,50 @@ def rank_program(g, core, T, topo):
                 return 0.0
             return steps[j]["lat"]
 
-        first = [list(s["on"])[0] for s in steps]
+        def plan(before, behind, way, fixed):
+            left, free, eng, end = [len(x) for x in before], {e: 0.0 for e in Q}, [None] * n, [0.0] * n
+            pool, order = {e: {} for e in Q}, []
+
+            def offer(i):
+                for e in [fixed[i]] if fixed else steps[i]["on"]:
+                    pool[e][i] = max([end[j] + (gap(i, j, e, eng[j]) if fixed else gap(j, i, eng[j], e)) for j in before[i]]
+                                     + [steps[i]["lat"] if fixed else 0.0])
+
+            for i in range(n):
+                if not left[i]:
+                    offer(i)
+            while len(order) < n:
+                now, e = min((max(free[e], min(pool[e].values())), e) for e in Q if pool[e])
+                near = [i for i, r in pool[e].items() if r <= now + HOLD]
+                if e == "v" and not fixed:
+                    near = ([i for i, r in pool[e].items() if r <= now + SPARE and len(steps[i]["on"]) == 1]
+                            + [i for i in near if steps[i]["on"]["v"][1] < SMALL]) or near
+                    near = [i for i in near if pool[e][i] <= max(now, min(pool[e][j] for j in near)) + HOLD]
+                i = max(near, key=lambda i: (way[i], -i))
+                free[e] = end[i] = max(now, pool[e][i]) + steps[i]["on"][e][1]
+                eng[i] = e
+                order.append(i)
+                for x in Q:
+                    pool[x].pop(i, None)
+                for j in behind[i]:
+                    left[j] -= 1
+                    if not left[j]:
+                        offer(j)
+            return order, eng, end
+
+        pre = [list(s["pre"]) for s in steps]
+        eng = [list(s["on"])[0] for s in steps]
         way = [0.0] * n
         for i in range(n - 1, -1, -1):
-            way[i] = steps[i]["on"][first[i]][1] + max([way[j] + gap(i, j, first[i], first[j]) for j in post[i]] + [steps[i]["lat"]])
-        left, free, eng, end = [len(s["pre"]) for s in steps], {e: 0.0 for e in Q}, [None] * n, [0.0] * n
-        pool, order = {e: {} for e in Q}, []
-
-        def offer(i):
-            for e in steps[i]["on"]:
-                pool[e][i] = max([end[j] + gap(j, i, eng[j], e) for j in steps[i]["pre"]] + [0.0])
-
-        for i in range(n):
-            if not left[i]:
-                offer(i)
-        while len(order) < n:
-            now, e = min((max(free[e], min(pool[e].values())), e) for e in Q if pool[e])
-            near = [i for i, r in pool[e].items() if r <= now + HOLD]
-            if e == "v":
-                near = [i for i, r in pool[e].items() if r <= now + SPARE and len(steps[i]["on"]) == 1] or near
-                near = [i for i in near if pool[e][i] <= max(now, min(pool[e][j] for j in near)) + HOLD]
-            i = max(near, key=lambda i: (way[i], -i))
-            free[e] = end[i] = max(now, pool[e][i]) + steps[i]["on"][e][1]
-            eng[i] = e
-            order.append(i)
-            for x in steps[i]["on"]:
-                del pool[x][i]
-            for j in post[i]:
-                left[j] -= 1
-                if not left[j]:
-                    offer(j)
+            way[i] = steps[i]["on"][eng[i]][1] + max([way[j] + gap(i, j, eng[i], eng[j]) for j in post[i]] + [steps[i]["lat"]])
+        best = None
+        for _ in range(PASSES):
+            order, eng, end = plan(pre, post, way, None)
+            span = max(end[i] + steps[i]["lat"] for i in range(n))
+            if best is None or span < best[0]:
+                best = (span, order, eng)
+            way = plan(post, pre, end, eng)[2]
+        order, eng = best[1:]
         cnt, known, tok = {}, {e: {} for e in Q}, {}
         for i in order:
             s, e = steps[i], eng[i]
@@ -184,7 +202,7 @@ def rank_program(g, core, T, topo):
                 g.wait_ge(T.sem[sem], cnt[sem])
 
     def mm(out, l, r, start=True, stop=True):
-        step({"p": (lambda q: q.matmul(out[0], l[0], r[0], start, stop), max(64, width(r)) * CY / 2)}, [l, r], [out])
+        step({"p": (lambda q: q.matmul(out[0], l[0], r[0], start, stop), max(64, width(r)) * CY / 2)}, [l, r], [out], 1.5 * LAT)
 
     def copy(out, in_):
         step({"v": (lambda q: q.tensor_copy(out[0], in_[0]), cyc(width(out), 1, out, in_))}, [in_], [out])
@@ -205,23 +223,23 @@ def rank_program(g, core, T, topo):
     def act(out, in_, fn, **kw):
         rd = [in_] + [x for x in kw.values() if isinstance(x, tuple)]
         kw = {n: x[0] if isinstance(x, tuple) else x for n, x in kw.items()}
-        step({"s": (lambda q: q.activation(out[0], in_[0], fn, **kw), 0.03 + cyc(width(out), 1))}, rd, [out])
+        step({"s": (lambda q: q.activation(out[0], in_[0], fn, **kw), FIX + cyc(width(out), 1))}, rd, [out])
 
     def lin(out, in_, scale, bias, on="sv"):
         col = isinstance(bias, tuple)
         b = bias[0] if col else bias
-        calls = {"s": (lambda q: q.activation(out[0], in_[0], ACTF.Identity if col else ACTF.Copy, scale=scale, bias=b), 0.03 + cyc(width(out), 1)),
+        calls = {"s": (lambda q: q.activation(out[0], in_[0], ACTF.Identity if col else ACTF.Copy, scale=scale, bias=b), FIX + cyc(width(out), 1)),
                  "v": (lambda q: q.tensor_scalar(out[0], in_[0], scale, b, ALU.mult, ALU.add), cyc(width(out), 1, out, in_))}
         step({e: calls[e] for e in on}, [in_, bias] if col else [in_], [out])
 
     def gather(out, win, off, on="sv"):
         c = width(out) * GA * CY
-        calls = {"s": (lambda q: q.activation(out[0], win[0].indirect(off[0]), ACTF.Copy), 0.03 + c),
-                 "v": (lambda q: q.tensor_copy(out[0], win[0].indirect(off[0])), c)}
+        calls = {"s": (lambda q: q.activation(out[0], win[0].indirect(off[0]), ACTF.Copy), FIX + c),
+                 "v": (lambda q: q.tensor_copy(out[0], win[0].indirect(off[0])), 0.05 + c)}
         step({e: calls[e] for e in on}, [win, off], [out])
 
     def gather_tt(out, win, off, b, op):
-        step({"v": (lambda q: q.tensor_tensor(out[0], win[0].indirect(off[0]), b[0], op), width(out) * GA * CY)}, [win, off, b], [out])
+        step({"v": (lambda q: q.tensor_tensor(out[0], win[0].indirect(off[0]), b[0], op), 0.05 + width(out) * GA * CY)}, [win, off, b], [out])
 
     def fill(out, c):
         step({"v": (lambda q: q.memset(out[0], c), cyc(width(out), 1, out))}, [], [out])
@@ -236,6 +254,8 @@ def rank_program(g, core, T, topo):
     d = dma("y", "ld_mv", T.mvs[:], T.mv[:], 131072, writes=[A("mvs")])
     d = dma("y", "ld_p", T.pt0[:], T.vp[:], 655360, writes=[A("pt0")], after=[d])
     dma("y", "ld_r", T.rw[:, 0:4096], T.strat[:], 1703936, writes=[A("rw", 0, 4096)], after=[d])
+    lin(A("rw", 4096, 4096 + 560), A("rw", 0, 560), 1.0, 0.0, "v")
+    fill(A("rw", 4096 + 560, RW), 0.0)
 
     def shifted(buf, src, sem, after):
         dma("y", sem, T[buf][1:128, 0:1024], src[0:127, :], 524288, reads=[after], writes=[A(buf, 0, 1024)])
@@ -258,11 +278,13 @@ def rank_program(g, core, T, topo):
         tt(A("xi", lo, hi), A("li%d" % t, lo, hi), pu, ALU.mult)
         ts(A("ai", lo, hi), A("xi", lo, hi), 5, ALU.arith_shift_right, 4095, ALU.bitwise_and)
 
-    def columns(t, c):
-        a, b = CHS[c], CHS[c + 1]
+    def parts(a, b):
+        return [(x, y) for x, y in zip(PARTS, PARTS[1:]) if a <= x and y <= b]
+
+    def columns(t, a, b):
         lin(A("of%d" % t, a, b), A("ai", a, b), 1.0, cadd if t else c37)
-        for i in range(a, b, PC):
-            gather(A("yy", 16 * i, 16 * (i + PC)), A("rw", 0, RW), A("of%d" % t, i, i + PC))
+        for i, j in parts(a, b):
+            gather(A("yy", 16 * i, 16 * j), A("rw", 0, RW), A("of%d" % t, i, j))
 
     def beats(t, c):
         a, b, pz = CHS[c], CHS[c + 1], "pz%d" % ((t * NC + c) % 2)
@@ -271,17 +293,19 @@ def rank_program(g, core, T, topo):
             mm(A(pz, 0, 4 * n), A("ib"), A("neg", 0, 4 * n), True, False)
         for j in range(4):
             mm(A(pz, j, 4 * n, 4), A("ib"), zi(t, a, b), not t, not t or j == 3)
-        lo = 16 * a
-        for q, s in ((0, 4), (1, 4), (2, 4), (3, 8), (7, 16)):
-            e = 16 // s
-            tt(A("bt", lo, lo + e * n), A("yy", 16 * a + q, 16 * b, s), A(pz, 0, 4 * n, s // 4), ALU.is_gt)
-            for j in range(e):
-                k = q + s * j
-                mm(A("pc", 0, n), A("zb_", 15 - k, 143 - k), A("bt", lo + j, lo + e * n, e), k == 0, k == 7)
-            lo += e * n
+        for x, y in parts(a, b):
+            lo, m = 16 * x, y - x
+            for q, s in ((0, 4), (1, 4), (2, 4), (3, 8), (7, 16)):
+                e = 16 // s
+                tt(A("bt", lo, lo + e * m), A("yy", 16 * x + q, 16 * y, s), A(pz, 4 * (x - a), 4 * (y - a), s // 4), ALU.is_gt)
+                for j in range(e):
+                    k = q + s * j
+                    mm(A("pc", x - a, y - a), A("zb_", 15 - k, 143 - k), A("bt", lo + j, lo + e * m, e), k == 0, k == 7)
+                lo += e * m
+            scan(x, y, True)
+            scan(x, y, False)
 
-    def scan(t, c, hi):
-        a, b = CHS[c], CHS[c + 1]
+    def scan(a, b, hi):
         s = (16 * a, 16 * b)
         o, m = (A("hi", *s), A("mhi", 0, 16 * (b - a))) if hi else (A("lo", *s), A("mlo", 0, 16 * (b - a)))
         o0, o1 = (ALU.min, ALU.max) if hi else (ALU.max, ALU.min)
@@ -307,19 +331,29 @@ def rank_program(g, core, T, topo):
         for k in range(16):
             mm(pl, A("zb_", 15 - k, 143 - k), A("oh", 2 * a + k, 2 * b, 16), False, k == 15)
         lin(A("sb%d" % t, a // 8, b // 8), pl, 1.0, 0.0, "vs")
-        send("nm%d" % t, "sb%d" % t, (a + b) // 16, b // 8, "nm%d%d" % (t, c), me - 1 - t)
 
     def newz(t, c):
         a, b = CHS[c], CHS[c + 1]
-        last = t + 1 == NT
-        gather(A("hp", a, b), A("hi", 16 * a, 16 * b), vlist("sb", t, c, 0))
-        gather(A("lp", a, b), A("lo", 16 * a, 16 * b), vlist("sb", t, c, 0))
-        mm(A("ph", 0, b - a), A("hib"), A("hp", a, b), True, False)
-        mm(A("ph", 0, b - a), A("hib"), A("lp", a, b), False, True)
-        lin(A("z16" if last else "zo%d" % t, a, b), A("ph", 0, b - a), 1.0, ZO - 0.25)
+        last, v, sm = t + 1 == NT, vlist("sb", t, c, 0), A("sm", a, b)
+        z = A("z16" if last else "zo%d" % t, a, b)
+        if c < LC:
+            gather(A("hp", a, b), A("hi", 16 * a, 16 * b), v)
+            gather(A("lp", a, b), A("lo", 16 * a, 16 * b), v)
+            mm(A("ph", 0, b - a), A("hib"), A("hp", a, b), True, False)
+            mm(A("ph", 0, b - a), A("hib"), A("lp", a, b), False, True)
+            lin(z, A("ph", 0, b - a), 1.0, ZO - 0.25)
+        elif last:
+            gather(A("hp", a, b), A("hi", 16 * a, 16 * b), v)
+            gather_tt(sm, A("lo", 16 * a, 16 * b), v, A("hp", a, b), ALU.add)
+        else:
+            gather_tt(A("z16", a, b), A("hi", 16 * a, 16 * b), v, A("old", a, b), ALU.add)
+            gather_tt(A("s2", a, b), A("lo", 16 * a, 16 * b), v, A("z16", a, b), ALU.add)
+            ts(A("nw", a, b), A("s2", a, b), 0.25, ALU.mult, -0.375, ALU.add)
+            tt(sm, A("s2", a, b), A("old", a, b), ALU.subtract)
+        if c == LC:
+            lin(z, sm, 0.5, ZO - 0.25, "vs")
         if last:
             lin(A("zo%d" % t, a, b), A("z16", a, b), 1.0, -ZO, "vs")
-        send("zi%d" % (t + 1), "zo%d" % t, a, b, "za%d%d" % (t + 1, c), me - 1 - t if last else me + 1)
 
     def window(lo):
         return A("rw", 0, 8 * SEG) if lo < SEG else A("rw", 8 * SEG, 4096)
@@ -333,7 +367,7 @@ def rank_program(g, core, T, topo):
         copy(A("plu"), A("pli"))
         for lo, hi in ((0, SEG), (SEG, G)):
             o, w, x = A("old", lo, hi), window(lo), A("plu", lo // 16, hi // 16)
-            step({"s": (lambda q, o=o, w=w, x=x: q.activation(o[0], w[0].indirect(x[0]), ACTF.Copy, scale=2.0), 0.03 + (hi - lo) * GA * CY)}, [w, x], [o])
+            step({"s": (lambda q, o=o, w=w, x=x: q.activation(o[0], w[0].indirect(x[0]), ACTF.Copy, scale=2.0), FIX + (hi - lo) * GA * CY)}, [w, x], [o])
 
     def update(t, lo, hi):
         p = A("pe", 0, hi - lo)
@@ -341,18 +375,12 @@ def rank_program(g, core, T, topo):
         mm(p, A("hib"), A("zo%d" % t, lo, hi), False, True)
         lin(A("nw", lo, hi), p, 1.0, -ZO / 2 - 0.25)
 
-    def update_v(t, c):
-        a, b = CHS[c], CHS[c + 1]
-        gather_tt(A("sm", a, b), A("hi", 16 * a, 16 * b), vlist("sb", t, c, 0), A("old", a, b), ALU.add)
-        gather_tt(A("s2", a, b), A("lo", 16 * a, 16 * b), vlist("sb", t, c, 0), A("sm", a, b), ALU.add)
-        ts(A("nw", a, b), A("s2", a, b), 0.25, ALU.mult, -0.375, ALU.add)
-
     def scatter(t, lo, hi):
         w, o, i = window(lo), A("plu", lo // 16, hi // 16), A("nw", lo, hi)
-        step({"v": (lambda q: q.tensor_copy(w[0].indirect(o[0]), i[0]), (hi - lo) * SC * CY)}, [o, i], [w])
+        step({"v": (lambda q: q.tensor_copy(w[0].indirect(o[0]), i[0]), 0.05 + (hi - lo) * SC * CY)}, [o, i], [w])
 
-    def mirror():
-        lin(A("rw", 4096, RW), A("rw", 0, RW - 4096), 1.0, 0.0)
+    def mirror(t):
+        dma("y", "mir%d" % t, T.rw[:, 4096:RW], T.rw[:, 0:RW - 4096], 256 * (RW - 4096), reads=[A("rw", 0, RW - 4096)], writes=[A("rw", 4096, RW)])
 
     def tally(t):
         cs = sorted(range(LC), key=lambda c: CHS[c] - CHS[c + 1]) + [LC]
@@ -378,8 +406,6 @@ def rank_program(g, core, T, topo):
         a, b = CHS[c], CHS[c + 1]
         out = A("ls%d" % (t + 1) if t + 1 < NT else "yos", a, b)
         gather_tt(out, A(("ots", "pts", "ots")[t], 0, 1024 + 512 * t), vlist("nm", t, c, 1), A("nr%d" % t, a, b), ALU.max)
-        if t + 1 < NT:
-            send("li%d" % (t + 1), "ls%d" % (t + 1), a, b, "la%d%d" % (t + 1, c), me + 2 + t)
 
     def extend(t):
         p = A("pe")
@@ -453,43 +479,49 @@ def rank_program(g, core, T, topo):
         ts(A("cst", a // 8, (a + b) // 16), A("xx", 0, (b - a) // 16), 256.0, ALU.mult, ck16, ALU.add)
     for t in range(NT):
         ts(A("nr%d" % t), A("xx"), 1024.0 + 512 * t, ALU.add, cj0, ALU.mult)
-    send("zi0", "zst", 0, c2, "za0", me + 1)
-    send("zi0", "zst", c2, G, "zb0", me + 1)
+    send("zi0", "zst", 0, c1, "za0", me + 1, 1.8, 0.5)
+    send("zi0", "zst", c1, c2, "zb0", me + 1, 0.0, 0.5)
+    send("zi0", "zst", c2, G, "zc0", me + 1, 0.0, 0.5)
     copy(A("mvu"), A("mvs"))
     gather(A("ls0", 0, c1), A("pt0"), A("mvu", 0, c1 // 16), "v")
     gather(A("ls0", c1, G), A("pt0"), A("mvu", c1 // 16, 32), "v")
-    send("li0", "ls0", 0, c1, "la0", me + 1)
-    send("li0", "ls0", c1, c2, "lb0", me + 1)
-    send("li0", "ls0", c2, G, "lc0", me + 1)
-    mirror()
+    send("li0", "ls0", 0, c1, "la0", me + 1, 0.0, 0.5)
+    send("li0", "ls0", c1, c2, "lb0", me + 1, 0.0, 0.5)
+    send("li0", "ls0", c2, G, "lc0", me + 1, 0.0, 0.5)
     shifted("ots", T.vo, "ld_o", A("rw", 0, 16))
 
     for t in range(NT):
         last = t + 1 == NT
-        for c in range(NC):
-            address(t, CHS[c], CHS[c + 1])
-            columns(t, c)
+        for u in UNITS if t else ((0,), (1,), tuple(range(2, NC))):
+            a, b = CHS[u[0]], CHS[u[-1] + 1]
+            address(t, a, b)
+            for x, y in ((a, c1), (c1, b)) if a < c1 < b else ((a, b),):
+                columns(t, x, y)
         if not last:
             place(t)
-        for c in range(NC):
-            beats(t, c)
-            scan(t, c, True)
-            scan(t, c, False)
-            verdict(t, c)
-            newz(t, c)
-            home(t, c)
-            if c == 1:
-                extend(t)
-            if not last and c < LC:
-                update(t, CHS[c], CHS[c + 1])
+        for x, u in enumerate(UNITS):
+            a, b = CHS[u[0]], CHS[u[-1] + 1]
+            for c in u:
+                beats(t, c)
+                verdict(t, c)
+                newz(t, c)
+            send("nm%d" % t, "sb%d" % t, a // 8, b // 8, "nm%d%d" % (t, x), me - 1 - t)
+            send("zi%d" % (t + 1), "zo%d" % t, a, b, "za%d%d" % (t + 1, x), me - 1 - t if last else me + 1)
+            for c in u:
+                home(t, c)
+            if not last:
+                send("li%d" % (t + 1), "ls%d" % (t + 1), a, b, "la%d%d" % (t + 1, x), me + 2 + t)
+                if b < G:
+                    update(t, a, b)
+        extend(t)
         if t == 0:
             shifted("pts", T.vp, "ld_q", A("sb0", 0, 2))
         if not last:
-            update_v(t, LC)
             tally(t)
-            for lo, hi in ((0, SEG), (SEG, CHS[LC - 1]), (CHS[LC - 1], CHS[LC]), (CHS[LC], G)):
-                scatter(t, lo, hi)
-            mirror()
+            scatter(t, 0, SEG)
+            mirror(t)
+            for u in UNITS:
+                scatter(t, max(SEG, CHS[u[0]]), CHS[u[-1] + 1])
         verdicts(t)
     b = CHS[LC]
     dma("y", "o_o0", T.yo[:, 0:b], T.yos[:, 0:b], 512 * b, reads=[A("yos", 0, b)])

@@ -1,20 +1,31 @@
+from concourse.bass import DstId, RemoteDMATransfer
 from concourse.mybir import AluOpType as ALU, AxisListType, ActivationFunctionType as ACTF
 
 NT, G = 3, 512
-CHS = (0, 128, 256, 384, 448, 512)
+CHS = (0, 256, 448, 512)
 NC = len(CHS) - 1
-UNITS = ((0, 1), (2, 3), (4,))
+U0 = (0, 128, 256, 512)
 PARTS = (0, 32, 64, 128, 192, 256, 320, 384, 448, 512)
+ZB = (0, 128, 256, 384, 512)
+FIRST = 64
+SHARE = ((), (), (384, 448))
 RW = 4096 + 816
+RA = 3072
 SEG = 128
 EN = 8
 ZO, QO = 1056.0, 1048.0
+BIG = 12582912.0
 CY, GA, SC = 0.83e-3, 1.5, 3.5
 LAT, HOP = 0.1, 1.6
-FIX, CALL = 0.065, 0.45
-HOLD, SPARE = 0.05, 0.6
-SMALL = 0.25
-PASSES = 3
+FAR = 1.6
+LATE = (0.0, 0.0, 0.0, 0.0)
+FOLD = (0, 1, 2, 3)
+PA = ()
+FIX, CALL = 0.065, 0.55
+SPARE = 0.3
+RULES = [(w, s, h, f, x) for w in (6.0, 9.0, 13.0) for s in (0.12, 0.2) for h in (0.08, 0.12) for f in (0.0, 0.4, 0.8) for x in (0.1, 0.3)]
+CASES = ((-0.27, 0.0, 1.0, 63), (0.0, 0.0, 1.0, 65), (0.33, 0.0, 1.0, 76), (0.0, 1.2, 1.0, 72), (0.27, 0.0, 1.45, 100), (0.0, 0.6, 1.3, 83))
+PASSES = 4
 
 SCRATCH = {
     "rw": ("sbuf", [128, RW], "bfloat16"), "pt0": ("sbuf", [128, 1024], "int32"),
@@ -22,45 +33,48 @@ SCRATCH = {
     "mvs": ("sbuf", [128, 32], "int32"), "mvu": ("sbuf", [128, 32], "uint16"),
     "wti": ("sbuf", [128, 8], "int32"), "zst": ("sbuf", [128, G], "bfloat16"),
     "yy": ("sbuf", [128, 16 * G], "bfloat16"), "hi": ("sbuf", [128, 16 * G], "bfloat16"), "lo": ("sbuf", [128, 16 * G], "bfloat16"),
-    "bt": ("sbuf", [128, 16 * G], "bfloat16"), "mhi": ("sbuf", [128, 2048], "bfloat16"), "mlo": ("sbuf", [128, 2048], "bfloat16"),
+    "bt": ("sbuf", [128, 16 * G], "bfloat16"), "mhi": ("sbuf", [128, 1024], "bfloat16"), "mlo": ("sbuf", [128, 1024], "bfloat16"),
     "qf": ("sbuf", [128, G], "float16"), "xi": ("sbuf", [128, G], "int32"), "ai": ("sbuf", [128, G], "int32"),
-    "sg": ("sbuf", [128, G], "bfloat16"), "oh": ("sbuf", [128, 2 * G], "float16"), "vl": ("sbuf", [128, 64], "uint16"),
+    "sg": ("sbuf", [128, G], "bfloat16"), "oh": ("sbuf", [128, 2 * G], "float16"),
     "hp": ("sbuf", [128, G], "bfloat16"), "lp": ("sbuf", [128, G], "bfloat16"), "sm": ("sbuf", [128, G], "float16"), "s2": ("sbuf", [128, G], "float16"),
     "z16": ("sbuf", [128, G], "float16"), "old": ("sbuf", [128, G], "float16"), "nw": ("sbuf", [128, G], "int32"),
     "pli": ("sbuf", [128, 32], "int32"), "plm": ("sbuf", [128, 32], "int32"), "plu": ("sbuf", [128, 32], "uint16"),
     "yps": ("sbuf", [128, G], "float32"), "yos": ("sbuf", [128, G], "float32"),
+    "lsi": ("sbuf", [128, G], "int32"), "nri": ("sbuf", [128, 2 * G], "int32"), "nrf": ("sbuf", [128, 2 * G], "float32"),
+    "nrh": ("sbuf", [128, G], "float16"),
     "an": ("sbuf", [128, 4], "float32"), "ani": ("sbuf", [128, 8], "int32"),
     "xx": ("sbuf", [128, G], "float32"), "xb": ("sbuf", [128, 144], "bfloat16"), "xg": ("sbuf", [128, 128], "bfloat16"),
     "pint": ("sbuf", [128, 8], "int32"), "col": ("sbuf", [128, 32], "float32"),
-    "zb_": ("sbuf", [128, 144], "bfloat16"), "zw_": ("sbuf", [128, 144], "bfloat16"), "neg": ("sbuf", [128, G], "bfloat16"),
+    "zb_": ("sbuf", [128, 144], "bfloat16"), "zw_": ("sbuf", [128, 144], "bfloat16"), "hz_": ("sbuf", [128, 144], "bfloat16"),
+    "neg": ("sbuf", [128, G], "bfloat16"), "k1": ("sbuf", [128, 256], "bfloat16"),
     "nr0": ("sbuf", [128, G], "float16"), "nr1": ("sbuf", [128, G], "float16"), "nr2": ("sbuf", [128, G], "float32"),
     "cst": ("sbuf", [128, 64], "float16"), "c8": ("sbuf", [128, 32], "int32"),
 }
-for _n in ("bw", "kc", "kcw", "ib", "i4", "hib", "qib", "tri", "tr1", "tr2", "sh1", "sh2", "a15", "k1"):
+for _n in ("bw", "kc", "ib", "i4", "hib", "qib", "nib", "tri", "tr1", "tr2", "a15", "kq", "e8", "one"):
     SCRATCH[_n] = ("sbuf", [128, 128], "bfloat16")
 for _t in range(NT):
     SCRATCH["li%d" % _t] = ("sbuf", [128, G], "float16")
     SCRATCH["ls%d" % _t] = ("sbuf", [128, G], "float16")
     SCRATCH["of%d" % _t] = ("sbuf", [128, G], "uint16")
-    SCRATCH["sb%d" % _t] = ("sbuf", [128, 64], "uint16")
-    SCRATCH["nm%d" % _t] = ("sbuf", [128, 64], "uint16")
-    SCRATCH["vs%d" % _t] = ("sbuf", [128, 32], "float32")
+    SCRATCH["sb%d" % _t] = ("sbuf", [128, 96], "uint16")
+    SCRATCH["nm%d" % _t] = ("sbuf", [128, 96], "uint16")
     SCRATCH["vi%d" % _t] = ("sbuf", [128, 32], "float32")
     SCRATCH["zo%d" % _t] = ("sbuf", [128, G], "float16" if _t + 1 < NT else "bfloat16")
 for _t in range(NT + 1):
     SCRATCH["zi%d" % _t] = ("sbuf", [128, G], "float16" if 0 < _t < NT else "bfloat16")
-BANKS = ("pz0", "pz1", "pu", "pc", "pf", "pl", "ph", "pe")
+BANKS = ("pz0", "pz1", "pu", "pc", "pf", "pd", "pl", "pe")
 for _b in BANKS:
     SCRATCH[_b] = ("psum", [128, 512], "float32")
 
-LDS = ["ld_mv", "ld_wt", "ld_z", "ld_p", "ld_r", "ld_o", "ld_o0", "ld_q", "ld_q0", "mir0", "mir1"]
-OUTS = ["o_p", "o_o0", "o_o1", "o_z0", "o_z1", "o_k0", "o_k1", "o_k2"]
-SEMAPHORES = ["qv", "qs", "qp", "qg", "loc", "za0", "zb0", "zc0", "la0", "lb0", "lc0", "va0", "va1", "va2"] + LDS + OUTS
+LDS = ["ld_mv", "ld_wt", "ld_z", "ld_z2", "ld_p", "ld_r", "ld_r2", "ld_o", "ld_o0", "ld_q", "ld_q0", "mir0", "mir1"]
+OUTS = ["o_p", "o_k0", "o_k1", "o_k2"] + ["o_%s%d" % (x, c) for x in "oz" for c in range(NC)]
+SEMAPHORES = ["qv", "qs", "qp", "qg", "loc", "go", "za0", "zb0", "zc0", "la0", "lb0", "lc0", "o_p0"] + ["e%d" % _i for _i in range(12)] + LDS + OUTS
 for _t in range(NT):
-    for _c in range(len(UNITS)):
+    for _c in range(NC):
         SEMAPHORES += ["nm%d%d" % (_t, _c), "za%d%d" % (_t + 1, _c)]
         if _t:
             SEMAPHORES.append("la%d%d" % (_t, _c))
+PLAN = []
 
 
 def rank_program(g, core, T, topo):
@@ -71,10 +85,11 @@ def rank_program(g, core, T, topo):
     N = len(cores)
     Q = {"v": g.vector, "s": g.scalar, "p": g.tensor, "g": g, "y": g.sync}
 
-    steps, recs = [], {}
+    steps, recs, gate = [], {}, []
 
-    def step(on, reads, writes, lat=LAT, sem=None, n=1, lands=None, after=()):
-        i, pre = len(steps), {j: False for j in after}
+    def step(on, reads, writes, lat=LAT, sem=None, n=1, lands=None, after=(), ind=0.0):
+        after = list(after) + gate
+        i, pre = len(steps), {}
         for w, lst in ((0, reads), (1, writes)):
             for _, (b, lo, hi) in lst:
                 for r in recs.get(b, []):
@@ -91,8 +106,9 @@ def rank_program(g, core, T, topo):
                     recs[b] = [r for r in old if not (w and lo <= r[0] and r[1] <= hi)] + [(lo, hi, w, i)]
         if lands:
             recs.setdefault(lands[0], []).append((lands[1], lands[2], 1, i))
-        pre.pop(i, None)
-        steps.append({"on": on, "pre": pre, "lat": lat, "sem": sem, "n": n, "order": set(after)})
+        order = set(after) - set(pre)
+        pre.update({j: False for j in order})
+        steps.append({"on": on, "pre": pre, "lat": lat, "sem": sem, "n": n, "order": order, "ind": ind})
         return i
 
     def A(n, lo=0, hi=None, st=1, p=128):
@@ -111,14 +127,18 @@ def rank_program(g, core, T, topo):
     def dma(e, sem, out, in_, size, reads=(), writes=(), after=()):
         return step({e: (lambda q: q.dma_start(out, in_), 0.05)}, reads, writes, HOP + size / 4e5, sem, 16, after=after)
 
-    def send(buf, src, lo, hi, sem, to, start=0.0, late=0.0):
+    def send(buf, src, lo, hi, sem, to, start=0.0, late=0.0, after=(), fold=None):
         dst = cores[to % N]
         rid, pid, _ = topo.addr(dst)
         m = 0
         for x in topo.engines(core, dst)[:EN]:
             m |= 1 << x
         call = lambda q: q.remote_dma(T[buf][:, lo:hi], T[src][:, lo:hi], T.sem[sem], T.sem["loc"], pid, rid, m)
-        step({"g": (call, CALL + start)}, [A(src, lo, hi)], [], HOP + late + 256 * (hi - lo) / 1e5, sem, -EN, (buf, lo, hi))
+        if fold:
+            one = RemoteDMATransfer(dst_ids=[DstId(rid=rid, pnc=pid)], dma_engine_mask=m, remote_sem=T.sem[sem], alu_op=2,
+                                    srcs=[T[src][:, lo:hi], T[fold][:, lo:hi]], dsts=[T[buf][:, lo:hi]])
+            call = lambda q: q.remote_dma_fused([one], local_sem=T.sem["loc"])
+        return step({"g": (call, CALL + start)}, [A(x, lo, hi) for x in (src, fold) if x], [], FAR + late + (384 if fold else 256) * (hi - lo) / 1e5, sem, -EN, (buf, lo, hi), after)
 
     def issue():
         n = len(steps)
@@ -127,18 +147,18 @@ def rank_program(g, core, T, topo):
             for j in s["pre"]:
                 post[j].append(i)
 
-        def gap(j, i, ej, ei):
+        def gap(j, i, ej, ei, far=0.0):
             if j in steps[i]["order"] or (ej == ei and not steps[i]["pre"][j] and steps[j]["sem"] is None and steps[i]["sem"] is None):
                 return 0.0
-            return steps[j]["lat"]
+            return steps[j]["lat"] + (far if steps[j]["n"] < 0 else 0.0)
 
-        def plan(before, behind, way, fixed):
+        def plan(before, behind, way, fixed, wait, small, hold, far, spare):
             left, free, eng, end = [len(x) for x in before], {e: 0.0 for e in Q}, [None] * n, [0.0] * n
             pool, order = {e: {} for e in Q}, []
 
             def offer(i):
                 for e in [fixed[i]] if fixed else steps[i]["on"]:
-                    pool[e][i] = max([end[j] + (gap(i, j, e, eng[j]) if fixed else gap(j, i, eng[j], e)) for j in before[i]]
+                    pool[e][i] = max([end[j] + (gap(i, j, e, eng[j], far) if fixed else gap(j, i, eng[j], e, far)) for j in before[i]]
                                      + [steps[i]["lat"] if fixed else 0.0])
 
             for i in range(n):
@@ -146,12 +166,12 @@ def rank_program(g, core, T, topo):
                     offer(i)
             while len(order) < n:
                 now, e = min((max(free[e], min(pool[e].values())), e) for e in Q if pool[e])
-                near = [i for i, r in pool[e].items() if r <= now + HOLD]
+                near = [i for i, r in pool[e].items() if r <= now + hold]
                 if e == "v" and not fixed:
-                    near = ([i for i, r in pool[e].items() if r <= now + SPARE and len(steps[i]["on"]) == 1]
-                            + [i for i in near if steps[i]["on"]["v"][1] < SMALL]) or near
-                    near = [i for i in near if pool[e][i] <= max(now, min(pool[e][j] for j in near)) + HOLD]
-                i = max(near, key=lambda i: (way[i], -i))
+                    near = ([i for i, r in pool[e].items() if r <= now + spare and len(steps[i]["on"]) == 1]
+                            + [i for i in near if steps[i]["on"]["v"][1] < small]) or near
+                    near = [i for i in near if pool[e][i] <= max(now, min(pool[e][j] for j in near)) + hold]
+                i = max(near, key=lambda i: (way[i] - wait * max(0.0, pool[e][i] - now), -i))
                 free[e] = end[i] = max(now, pool[e][i]) + steps[i]["on"][e][1]
                 eng[i] = e
                 order.append(i)
@@ -163,19 +183,29 @@ def rank_program(g, core, T, topo):
                         offer(j)
             return order, eng, end
 
-        pre = [list(s["pre"]) for s in steps]
-        eng = [list(s["on"])[0] for s in steps]
-        way = [0.0] * n
-        for i in range(n - 1, -1, -1):
-            way[i] = steps[i]["on"][eng[i]][1] + max([way[j] + gap(i, j, eng[i], eng[j]) for j in post[i]] + [steps[i]["lat"]])
-        best = None
-        for _ in range(PASSES):
-            order, eng, end = plan(pre, post, way, None)
-            span = max(end[i] + steps[i]["lat"] for i in range(n))
-            if best is None or span < best[0]:
-                best = (span, order, eng)
-            way = plan(post, pre, end, eng)[2]
-        order, eng = best[1:]
+        def span(order, eng, more, far, slow):
+            free, end = {e: 0.0 for e in Q}, [0.0] * n
+            for i in order:
+                e, s = eng[i], steps[i]
+                free[e] = end[i] = (max([free[e]] + [end[j] + gap(j, i, eng[j], e, far) for j in s["pre"]]) + (far / 5 if s["n"] < 0 else 0.0)
+                                    + (s["on"][e][1] + more * s["ind"]) * (slow if e in "vsp" else 1.0))
+            return max(end[i] + steps[i]["lat"] for i in range(n))
+
+        pre, best = [list(s["pre"]) for s in steps], None
+        for rule in () if PLAN else RULES:
+            eng = [list(s["on"])[0] for s in steps]
+            way = [0.0] * n
+            for i in range(n - 1, -1, -1):
+                way[i] = steps[i]["on"][eng[i]][1] + max([way[j] + gap(i, j, eng[i], eng[j]) for j in post[i]] + [steps[i]["lat"]])
+            for _ in range(PASSES):
+                order, eng, end = plan(pre, post, way, None, *rule)
+                total = sum(span(order, eng, *c[:3]) / c[3] for c in CASES)
+                if best is None or total < best[0]:
+                    best = (total, order, eng)
+                way = plan(post, pre, end, eng, *rule)[2]
+        if best:
+            PLAN.extend(best[1:])
+        order, eng = PLAN
         cnt, known, tok = {}, {e: {} for e in Q}, {}
         for i in order:
             s, e = steps[i], eng[i]
@@ -191,12 +221,14 @@ def rank_program(g, core, T, topo):
             if s["n"] < 0:
                 cnt["loc"] = cnt.get("loc", 0) + EN
                 tok[i] = (s["sem"], EN, {})
-                continue
-            sem = s["sem"] or "q" + e
-            if e != "p" or any(eng[j] != "p" for j in post[i]):
-                cnt[sem] = cnt.get(sem, 0) + s["n"]
-                ins.then_inc(T.sem[sem], s["n"])
-            tok[i] = (sem, cnt.get(sem, 0), dict(k))
+            elif s["n"] == 0:
+                tok[i] = (s["sem"], 1, {})
+            else:
+                sem = s["sem"] or "q" + e
+                if e != "p" or any(eng[j] != "p" for j in post[i]):
+                    cnt[sem] = cnt.get(sem, 0) + s["n"]
+                    ins.then_inc(T.sem[sem], s["n"])
+                tok[i] = (sem, cnt.get(sem, 0), dict(k))
         for sem in OUTS + ["loc", "qv", "qs", "qp", "qg"]:
             if cnt.get(sem, 0) > known["g"].get(sem, 0):
                 g.wait_ge(T.sem[sem], cnt[sem])
@@ -232,29 +264,34 @@ def rank_program(g, core, T, topo):
                  "v": (lambda q: q.tensor_scalar(out[0], in_[0], scale, b, ALU.mult, ALU.add), cyc(width(out), 1, out, in_))}
         step({e: calls[e] for e in on}, [in_, bias] if col else [in_], [out])
 
-    def gather(out, win, off, on="sv"):
+    def gather(out, win, off, on="sv", scale=1.0):
         c = width(out) * GA * CY
-        calls = {"s": (lambda q: q.activation(out[0], win[0].indirect(off[0]), ACTF.Copy), FIX + c),
-                 "v": (lambda q: q.tensor_copy(out[0], win[0].indirect(off[0])), 0.05 + c)}
-        step({e: calls[e] for e in on}, [win, off], [out])
+        calls = {"s": (lambda q: q.activation(out[0], win[0].indirect(off[0]), ACTF.Copy, scale=scale), FIX + c),
+                 "v": (lambda q: q.tensor_scalar(out[0], win[0].indirect(off[0]), scale, None, ALU.mult), 0.05 + c)}
+        step({e: calls[e] for e in on}, [win, off], [out], ind=c)
 
     def gather_tt(out, win, off, b, op):
-        step({"v": (lambda q: q.tensor_tensor(out[0], win[0].indirect(off[0]), b[0], op), 0.05 + width(out) * GA * CY)}, [win, off, b], [out])
+        step({"v": (lambda q: q.tensor_tensor(out[0], win[0].indirect(off[0]), b[0], op), 0.05 + width(out) * GA * CY)}, [win, off, b], [out],
+             ind=width(out) * GA * CY)
 
     def fill(out, c):
         step({"v": (lambda q: q.memset(out[0], c), cyc(width(out), 1, out))}, [], [out])
 
-    def iota(out, pattern, cm, small=True):
+    def iota(out, pattern, cm, small=True, base=0, after=()):
         kw = {"allow_small_or_imprecise_dtypes": True} if small else {}
-        step({"g": (lambda q: q.iota(out[0], pattern, 0, cm, **kw), 0.13 + 2 * width(out) * CY)}, [], [out])
+        step({"g": (lambda q: q.iota(out[0], pattern, base, cm, **kw), 0.13 + 2 * width(out) * CY)}, list(after), [out])
 
-    c1, c2, LC = CHS[1], CHS[2], NC - 1
-    d = dma("s", "ld_z", T.zst[:], T.z0[:], 131072, writes=[A("zst")])
-    dma("s", "ld_wt", T.wti[:, 0:1], T.wt[:], 131072, writes=[A("wti", 0, 1)], after=[d])
-    d = dma("y", "ld_mv", T.mvs[:], T.mv[:], 131072, writes=[A("mvs")])
-    d = dma("y", "ld_p", T.pt0[:], T.vp[:], 655360, writes=[A("pt0")], after=[d])
-    dma("y", "ld_r", T.rw[:, 0:4096], T.strat[:], 1703936, writes=[A("rw", 0, 4096)], after=[d])
-    lin(A("rw", 4096, 4096 + 560), A("rw", 0, 560), 1.0, 0.0, "v")
+    def select(out, in_, pattern, op, other, cm):
+        step({"g": (lambda q: q.affine_select(out[0], in_[0], pattern, op, other, 0, cm), 0.17 + 2 * width(out) * CY)}, [in_], [out])
+
+    c1, c2, LC = U0[1], U0[2], NC - 1
+    d = dma("s", "ld_z", T.zst[:, 0:c1], T.z0[:, 0:c1], 256 * c1, writes=[A("zst", 0, c1)])
+    dma("s", "ld_wt", T.wti[:, 0:1], T.wt[:], 256 * c1, writes=[A("wti", 0, 1)], after=[d])
+    d = dma("y", "ld_mv", T.mvs[:], T.mv[:], 256 * c1, writes=[A("mvs")])
+    d = dma("y", "ld_p", T.pt0[:], T.vp[:], 580000, writes=[A("pt0")], after=[d])
+    d = dma("y", "ld_z2", T.zst[:, c1:G], T.z0[:, c1:G], 680000, writes=[A("zst", c1, G)], after=[d])
+    dma("y", "ld_r", T.rw[:, 0:RA], T.strat[:, 0:RA], 680000 + 256 * RA, writes=[A("rw", 0, RA)], after=[d])
+    lin(A("rw", 4096, 4096 + 560), A("rw", 0, 560), 1.0, 0.0, "s")
     fill(A("rw", 4096 + 560, RW), 0.0)
 
     def shifted(buf, src, sem, after):
@@ -262,7 +299,7 @@ def rank_program(g, core, T, topo):
         recs[buf].append((0, 1024, 1, dma("y", sem + "0", T[buf][0:1, 0:1024], src[0:1, :], 4096, reads=[after])))
 
     C = lambda i: A("col", i, i + 1)
-    cp, ck, cg16, cz15, c37, ck16, c8k, cj0, cp1, cp2, m15, m14, chit, crel, ck1, ca15, cw, cq, cadd, cyp = [C(i) for i in range(20)]
+    cp, ck, cg16, cz15, c37, ck16, c8k, cj0, cn0, chit, crel, ca15, cw, cq, cadd = [C(i) for i in range(15)]
 
     def zi(t, *r):
         return A("zi%d" % t, *r)
@@ -272,7 +309,9 @@ def rank_program(g, core, T, topo):
         pu = A("pu", 0, n)
         mm(pu, A("bw"), zi(t, lo, hi))
         lin(A("qf", lo, hi), pu, 1.0 / 4096, cq if t else QO - 2047.5 / 4096)
-        mm(pu, A("kcw" if t else "kc"), A("neg", 0, n), True, False)
+        mm(pu, A("kc"), A("neg", 0, n), True, False)
+        if t:
+            mm(pu, A("bw"), A("neg", 0, n), False, False)
         mm(pu, A("bw"), zi(t, lo, hi), False, False)
         mm(pu, A("i4"), A("qf", lo, hi), False, True)
         tt(A("xi", lo, hi), A("li%d" % t, lo, hi), pu, ALU.mult)
@@ -287,20 +326,32 @@ def rank_program(g, core, T, topo):
             gather(A("yy", 16 * i, 16 * j), A("rw", 0, RW), A("of%d" % t, i, j))
 
     def beats(t, c):
-        a, b, pz = CHS[c], CHS[c + 1], "pz%d" % ((t * NC + c) % 2)
-        n = b - a
-        if t:
-            mm(A(pz, 0, 4 * n), A("ib"), A("neg", 0, 4 * n), True, False)
-        for j in range(4):
-            mm(A(pz, j, 4 * n, 4), A("ib"), zi(t, a, b), not t, not t or j == 3)
+        a, b = CHS[c], CHS[c + 1]
         for x, y in parts(a, b):
-            lo, m = 16 * x, y - x
-            for q, s in ((0, 4), (1, 4), (2, 4), (3, 8), (7, 16)):
+            lo, m, pc = 16 * x, y - x, A("pc", x - a, y - a)
+            j = max(i for i in range(len(ZB) - 1) if ZB[i] <= x)
+            z0, z1, pz = ZB[j], ZB[j + 1], "pz%d" % (j % 2)
+            if x == z0:
+                if t:
+                    mm(A(pz, 0, 4 * (z1 - z0)), A("ib"), A("neg", 0, 4 * (z1 - z0)), True, False)
+                for j in range(4):
+                    mm(A(pz, j, 4 * (z1 - z0), 4), A("ib"), zi(t, z0, z1), not t, not t or j == 3)
+            odd = x in SHARE[t]
+            if odd:
+                pd = A("pd", 0, 8 * m)
+                mm(pd, A("ib"), A("yy", 16 * x + 1, 16 * y, 2), True, False)
+                for j in range(8):
+                    mm(A("pd", j, 8 * m, 8), A("nib"), zi(t, x, y), False, j == 7)
+                act(A("bt", lo + 8 * m, lo + 16 * m), pd, ACTF.Sign, bias=(ZO if t else 0.0) - 0.5)
+                mm(pc, A("e8"), A("one", 0, m), True, False)
+                for j in range(7):
+                    mm(pc, A("hz_", 14 - 2 * j, 142 - 2 * j), A("bt", lo + 8 * m + j, lo + 16 * m, 8), False, False)
+            for q, s in ((0, 4), (2, 4)) if odd else ((0, 4), (1, 4), (2, 4), (3, 8), (7, 16)):
                 e = 16 // s
-                tt(A("bt", lo, lo + e * m), A("yy", 16 * x + q, 16 * y, s), A(pz, 4 * (x - a), 4 * (y - a), s // 4), ALU.is_gt)
+                tt(A("bt", lo, lo + e * m), A("yy", 16 * x + q, 16 * y, s), A(pz, 4 * (x - z0), 4 * (y - z0), s // 4), ALU.is_gt)
                 for j in range(e):
                     k = q + s * j
-                    mm(A("pc", x - a, y - a), A("zb_", 15 - k, 143 - k), A("bt", lo + j, lo + e * m, e), k == 0, k == 7)
+                    mm(pc, A("zb_", 15 - k, 143 - k), A("bt", lo + j, lo + e * m, e), k == 0 and not odd, k == (14 if odd else 7))
                 lo += e * m
             scan(x, y, True)
             scan(x, y, False)
@@ -330,30 +381,38 @@ def rank_program(g, core, T, topo):
         mm(pl, A("ib"), A("cst", a // 8, b // 8), True, False)
         for k in range(16):
             mm(pl, A("zb_", 15 - k, 143 - k), A("oh", 2 * a + k, 2 * b, 16), False, k == 15)
-        lin(A("sb%d" % t, a // 8, b // 8), pl, 1.0, 0.0, "vs")
+        lin(A("sb%d" % t, a // 8, b // 8), pl, 1.0, -1.0, "v")
 
     def newz(t, c):
         a, b = CHS[c], CHS[c + 1]
-        last, v, sm = t + 1 == NT, vlist("sb", t, c, 0), A("sm", a, b)
-        z = A("z16" if last else "zo%d" % t, a, b)
-        if c < LC:
-            gather(A("hp", a, b), A("hi", 16 * a, 16 * b), v)
-            gather(A("lp", a, b), A("lo", 16 * a, 16 * b), v)
-            mm(A("ph", 0, b - a), A("hib"), A("hp", a, b), True, False)
-            mm(A("ph", 0, b - a), A("hib"), A("lp", a, b), False, True)
-            lin(z, A("ph", 0, b - a), 1.0, ZO - 0.25)
+        last, v, sm, z = t + 1 == NT, vlist("sb", t, c, 0), A("sm", a, b), A("zo%d" % t, a, b)
+        hi, lo = A("hi", 16 * a, 16 * b), A("lo", 16 * a, 16 * b)
+        if c in PA and not last:
+            gather(A("hp", a, b), hi, v)
+            gather_tt(sm, lo, v, A("hp", a, b), ALU.add)
+            lin(z, sm, 0.5, ZO - 0.25, "v")
+        elif c < LC:
+            ph = A("pe", 256, 256 + b - a)
+            gather(A("hp", a, b), hi, v)
+            gather(A("lp", a, b), lo, v)
+            mm(ph, A("hib"), A("hp", a, b), True, False)
+            mm(ph, A("hib"), A("lp", a, b), False, not last)
+            if last:
+                mm(ph, A("kq"), A("k1", 0, b - a), False, True)
+                ts(z, ph, BIG, ALU.add, -BIG, ALU.add)
+            else:
+                lin(z, ph, 1.0, ZO - 0.25)
         elif last:
-            gather(A("hp", a, b), A("hi", 16 * a, 16 * b), v)
-            gather_tt(sm, A("lo", 16 * a, 16 * b), v, A("hp", a, b), ALU.add)
+            gather(A("hp", a, b), hi, v, "v")
+            gather_tt(sm, lo, v, A("hp", a, b), ALU.add)
+            lin(A("z16", a, b), sm, 0.5, ZO - 0.25, "v")
+            lin(z, A("z16", a, b), 1.0, -ZO, "v")
         else:
-            gather_tt(A("z16", a, b), A("hi", 16 * a, 16 * b), v, A("old", a, b), ALU.add)
-            gather_tt(A("s2", a, b), A("lo", 16 * a, 16 * b), v, A("z16", a, b), ALU.add)
+            gather_tt(A("z16", a, b), hi, v, A("old", a, b), ALU.add)
+            gather_tt(A("s2", a, b), lo, v, A("z16", a, b), ALU.add)
             ts(A("nw", a, b), A("s2", a, b), 0.25, ALU.mult, -0.375, ALU.add)
             tt(sm, A("s2", a, b), A("old", a, b), ALU.subtract)
-        if c == LC:
-            lin(z, sm, 0.5, ZO - 0.25, "vs")
-        if last:
-            lin(A("zo%d" % t, a, b), A("z16", a, b), 1.0, -ZO, "vs")
+            lin(z, sm, 0.5, ZO - 0.25, "v")
 
     def window(lo):
         return A("rw", 0, 8 * SEG) if lo < SEG else A("rw", 8 * SEG, 4096)
@@ -361,13 +420,12 @@ def rank_program(g, core, T, topo):
     def place(t):
         for k in range(16):
             mm(A("pe", 0, 32), A("zw_", 15 - k, 143 - k), zi(t, k, G, 16), k == 0, k == 15)
-        copy(A("pli"), A("pe", 0, 32))
+        lin(A("pli"), A("pe", 0, 32), 1.0, 0.0)
         ts(A("plm"), A("pli"), 7, ALU.bitwise_and)
-        tt(A("pli"), A("plm"), A("c8"), ALU.add)
-        copy(A("plu"), A("pli"))
+        tt(A("plu"), A("plm"), A("c8"), ALU.add)
         for lo, hi in ((0, SEG), (SEG, G)):
             o, w, x = A("old", lo, hi), window(lo), A("plu", lo // 16, hi // 16)
-            step({"s": (lambda q, o=o, w=w, x=x: q.activation(o[0], w[0].indirect(x[0]), ACTF.Copy, scale=2.0), FIX + (hi - lo) * GA * CY)}, [w, x], [o])
+            gather(o, w, x, "sv", 2.0)
 
     def update(t, lo, hi):
         p = A("pe", 0, hi - lo)
@@ -377,17 +435,16 @@ def rank_program(g, core, T, topo):
 
     def scatter(t, lo, hi):
         w, o, i = window(lo), A("plu", lo // 16, hi // 16), A("nw", lo, hi)
-        step({"v": (lambda q: q.tensor_copy(w[0].indirect(o[0]), i[0]), 0.05 + (hi - lo) * SC * CY)}, [o, i], [w])
+        step({"v": (lambda q: q.tensor_copy(w[0].indirect(o[0]), i[0]), 0.05 + (hi - lo) * SC * CY)}, [o, i], [w], ind=(hi - lo) * SC * CY)
 
     def mirror(t):
         dma("y", "mir%d" % t, T.rw[:, 4096:RW], T.rw[:, 0:RW - 4096], 256 * (RW - 4096), reads=[A("rw", 0, RW - 4096)], writes=[A("rw", 4096, RW)])
 
     def tally(t):
-        cs = sorted(range(LC), key=lambda c: CHS[c] - CHS[c + 1]) + [LC]
-        for c in cs:
-            a, b = CHS[c], CHS[c + 1]
-            mm(A("pc", 128, 128 + b - a), A("a15"), A("oh", 2 * a, a + b), c == cs[0], c == LC)
-        o, i = A("an", 0, 1), A("pc", 128, 128 + CHS[cs[0] + 1] - CHS[cs[0]])
+        for c in range(NC):
+            for i in range(CHS[c], CHS[c + 1], 64):
+                mm(A("pc", 256, 320), A("a15"), A("oh", CHS[c] + i, CHS[c] + i + 64), i == 0, i == G - 64)
+        o, i = A("an", 0, 1), A("pc", 256, 320)
         step({"v": (lambda q: q.tensor_reduce(o[0], i[0], AxisListType.X, ALU.add), cyc(width(i), 1))}, [i], [o])
         copy(A("ani", 0, 1), o)
         ts(A("ani", 1, 2), A("ani", 0, 1), 255, ALU.bitwise_and)
@@ -397,135 +454,168 @@ def rank_program(g, core, T, topo):
         for c in range(NC):
             for i in range(CHS[c], CHS[c + 1], 32):
                 j = i // 32
-                mm(A("pc", 256, 288), A("zb_", 15 - j, 143 - j), A("oh", CHS[c] + i, CHS[c] + i + 32), j == 0, j == 15)
-        lin(A("vs%d" % t), A("pc", 256, 288), 1.0, -1.0)
-        send("vi%d" % t, "vs%d" % t, 0, 32, "va%d" % t, me - 1 - t)
+                mm(A("pc", 320, 352), A("zb_", 15 - j, 143 - j), A("oh", CHS[c] + i, CHS[c] + i + 32), j == 0, j == 15)
+        lin(A("sb%d" % t, 64, 96), A("pc", 320, 352), 1.0, -1.0, "v")
+
+    def verdicts_out(t):
+        lin(A("vi%d" % t), A("nm%d" % t, 64, 96), 1.0, 0.0)
         dma("y", "o_k%d" % t, T.yk[:, t * G:t * G + G], T["vi%d" % t][:], 16384, reads=[A("vi%d" % t)])
 
     def home(t, c):
         a, b = CHS[c], CHS[c + 1]
         out = A("ls%d" % (t + 1) if t + 1 < NT else "yos", a, b)
-        gather_tt(out, A(("ots", "pts", "ots")[t], 0, 1024 + 512 * t), vlist("nm", t, c, 1), A("nr%d" % t, a, b), ALU.max)
+        win = A(("ots", "pts", "ots")[t], 0, 1024 + 512 * t)
+        fold = t + 1 < NT and c in FOLD
+        if fold:
+            gather(out, win, vlist("nm", t, c, 1))
+        else:
+            gather_tt(out, win, vlist("nm", t, c, 1), A("nr%d" % t, a, b), ALU.max)
+        if t + 1 < NT:
+            send("li%d" % (t + 1), "ls%d" % (t + 1), a, b, "la%d%d" % (t + 1, c), me + 2 + t, late=LATE[c], fold="nr%d" % t if fold else None)
 
     def extend(t):
-        p = A("pe")
-        if t == 1:
-            mm(p, A("sh1"), A("ls1"))
-            lin(A("ots", 1024, 1536), p, 1.0, 0.0)
-        if t < 2:
-            mm(p, A("sh2"), A("ls%d" % t), True, False)
-            mm(p, A("sh1"), A("nr%d" % t), False, True)
-            lin(A("ots", 1536, 2048) if t else A("pts", 1024, 1536), p, 1.0, 0.0)
+        o, i, x = A("lsi" if t < 2 else "yps"), A("ls%d" % t), A("nri")
+        if t == 0:
+            gate.append(d)
+        select(o, i, [[0, G]], ALU.is_ge, 0.0, 0)
+        if t == 0:
+            iota(x, [[1, 2 * G]], 0, False, 1024)
+            iota(A("nrf"), [[1, 2 * G]], 0, True, 1536)
+            iota(A("nr2"), [[0, G]], 0)
+            select(A("nrh"), A("nrf", 0, G), [[0, G]], ALU.is_ge, 0.0, 0)
+            gate.pop()
+            dma("y", "e9", T.nr1[:], T.nr0[:], 131072, reads=[A("nr0"), o], writes=[A("nr1")])
+            dma("y", "e10", T.nr1[0:128:16, :], T.nrh[0:8, :], 8192, reads=[A("nrh")], writes=[A("nr1")])
+            dma("y", "e11", T.nr2[0:128:16, :], T.nrf[0:8, G:2 * G], 16384, reads=[A("nrf")], writes=[A("nr2")])
+            dma("y", "e6", T.pts[0:2, 1024:1536], T.pt0[0:2, 0:G], 4096, reads=[A("pt0"), o], writes=[A("pts", 1024, 1536)])
+            dma("y", "e7", T.pts[2:128, 1024:1536], T.lsi[0:126, :], 262144, reads=[o], writes=[A("pts", 1024, 1536)])
+            dma("y", "e8", T.pts[1:128:16, 1024:1536], T.nri[0:8, 0:G], 16384, reads=[x], writes=[A("pts", 1024, 1536)])
+        elif t == 1:
+            dma("y", "e0", T.ots[0:2, 1024:2048], T.pt0[0:2, :], 8192, reads=[A("pt0"), i], writes=[A("ots", 1024, 2048)])
+            dma("y", "e4", T.lsi[0:128:16, :], T.nri[0:8, 0:G], 16384, reads=[x], writes=[o])
+            dma("y", "e1", T.ots[1:128, 1024:1536], T.lsi[0:127, :], 262144, reads=[o], writes=[A("ots", 1024, 1536)])
+            dma("y", "e2", T.ots[2:128, 1536:2048], T.lsi[0:126, :], 262144, reads=[o], writes=[A("ots", 1536, 2048)])
+            dma("y", "e3", T.ots[1:128:16, 1536:2048], T.nri[0:8, G:2 * G], 16384, reads=[x], writes=[A("ots", 1536, 2048)])
         else:
-            mm(p, A("sh1"), A("ls2"), True, False)
-            mm(p, A("ib"), A("nr1"), False, True)
-            lin(A("yps"), p, 1.0, cyp)
-            dma("y", "o_p", T.yp[:], T.yps[:], 262144, reads=[A("yps")])
+            yp = (None, ("yp", 0, G))
+            dma("y", "e5", T.yps[0:128:16, :], T.nrf[0:8, 0:G], 16384, reads=[A("nrf")], writes=[o])
+            dma("y", "o_p0", T.yp[1:128, :], T.yps[0:127, :], 262144, reads=[o], writes=[yp])
+            dma("y", "o_p", T.yp[0:128:16, :], T.nr2[0:128:16, :], 16384, reads=[A("nr2")], writes=[yp])
 
     iota(A("pint", 0, 1), [[1, 1]], 1, False)
     iota(A("xb"), [[1, 144]], 0)
     iota(A("xg"), [[16, 8], [0, 16]], 0)
-    iota(A("xx"), [[1, G]], 0)
+    iota(A("xx", 0, G // 2), [[1, G // 2]], 0)
+    lin(A("xx", G // 2, G), A("xx", 0, G // 2), 1.0, G / 2, "s")
     X = A("xb", 0, 128)
     fill(A("neg"), -ZO)
     fill(A("kc"), -32.0)
     fill(A("kc", p=1), -1.0)
-    fill(A("cst"), 0.0)
     ts(A("pint", 1, 2), A("pint", 0, 1), 15, ALU.bitwise_and)
     copy(cp, A("pint", 0, 1))
     copy(ck, A("pint", 1, 2))
     copy(cw, A("wti", 0, 1))
     tt(cg16, cp, ck, ALU.subtract)
-    for i in range(0, 2048, G):
-        lin(A("mhi", i, i + G), A("neg"), 0.0, 256.0)
-        lin(A("mlo", i, i + G), A("neg"), 0.0, 0.0)
-    lin(A("mhi", 0, 2048, 16), A("neg", 0, 128), 0.0, 0.0)
-    lin(A("mlo", 0, 2048, 16), A("neg", 0, 128), 0.0, 256.0)
+    for i in range(0, 1024, G):
+        lin(A("mhi", i, i + G), A("neg"), 0.0, 256.0, "s")
+        lin(A("mlo", i, i + G), A("neg"), 0.0, 0.0, "s")
+    lin(A("mhi", 0, 1024, 16), A("neg", 0, 64), 0.0, 0.0, "s")
+    lin(A("mlo", 0, 1024, 16), A("neg", 0, 64), 0.0, 256.0, "s")
     ts(cz15, cg16, 15.0, ALU.add)
     ts(c37, ck, 37.0, ALU.mult)
-    ts(ck1, ck, 1.0, ALU.add)
     ts(cj0, ck, 0.0, ALU.is_equal)
-    ts(m15, ck, 15.0, ALU.is_lt)
-    ts(m14, ck, 14.0, ALU.is_lt)
-    ts(cp1, cp, 1.0, ALU.add)
-    ts(cp2, cp, 2.0, ALU.add)
-    ts(crel, ck, 1.0, ALU.add, -2048.0, ALU.mult)
-    ts(ca15, ck, 15.0, ALU.is_equal, -1.0 / 16, ALU.mult)
-    ts(ck16, ck, 16.0, ALU.mult, -1.0, ALU.add)
-    ts(c8k, ck, 8.0, ALU.mult)
-    ts(chit, m15, -100.0, ALU.mult, 91.5, ALU.add)
-    ts(cyp, cj0, 512.0, ALU.mult)
     ts(A("ib"), X, cp, ALU.is_equal)
-    for name, x in (("i4", -4096.0), ("hib", 0.5), ("qib", 0.25), ("tri", 2048.0)):
-        ts(A(name), X, cp, ALU.is_equal, x, ALU.mult)
+    ts(A("i4"), X, cp, ALU.is_equal, -4096.0, ALU.mult)
     ts(A("zb_"), A("xb"), cz15, ALU.is_equal)
-    ts(A("zw_"), A("xb"), cz15, ALU.is_equal, cw, ALU.mult)
     ts(A("bw"), A("xg"), cg16, ALU.is_equal, cw, ALU.mult)
-    tt(A("kcw"), A("bw"), A("kc"), ALU.add)
-    ts(A("tr1"), X, cp, ALU.is_gt, -2048.0, ALU.mult)
-    ts(A("tr2"), X, cz15, ALU.is_gt, 2048.0, ALU.mult)
-    tt(A("tr1"), A("tr1"), A("tr2"), ALU.add)
-    tt(A("tri"), A("tri"), A("tr1"), ALU.add)
-    ts(A("sh1"), X, cp1, ALU.is_equal, m15, ALU.mult)
-    ts(A("sh2"), X, cp2, ALU.is_equal, m14, ALU.mult)
-    ts(A("a15"), X, 0.0, ALU.mult, ca15, ALU.add)
-    ts(A("k1"), X, 0.0, ALU.mult, ck1, ALU.add)
-    mm(A("ph", 0, 2), A("bw"), A("neg", 0, 2))
-    ts(cq, A("ph", 0, 1), 1.0 / 4096, ALU.mult, QO - 2047.5 / 4096, ALU.add)
-    ts(A("c8", 0, SEG // 16), A("xx", 0, SEG // 16), 128.0, ALU.mult, c8k, ALU.add)
-    ts(A("c8", SEG // 16, 32), A("xx", 0, 32 - SEG // 16), 128.0, ALU.mult, c8k, ALU.add)
-    for c in range(NC):
-        a, b = CHS[c], CHS[c + 1]
-        ts(A("cst", a // 8, (a + b) // 16), A("xx", 0, (b - a) // 16), 256.0, ALU.mult, ck16, ALU.add)
-    for t in range(NT):
-        ts(A("nr%d" % t), A("xx"), 1024.0 + 512 * t, ALU.add, cj0, ALU.mult)
-    send("zi0", "zst", 0, c1, "za0", me + 1, 1.8, 0.5)
-    send("zi0", "zst", c1, c2, "zb0", me + 1, 0.0, 0.5)
-    send("zi0", "zst", c2, G, "zc0", me + 1, 0.0, 0.5)
+    ts(A("tr1"), A("xg"), cg16, ALU.is_equal, -2048.0, ALU.mult)
+
+    ts(cn0, cj0, 1024.0, ALU.mult)
+    act(A("nr0"), A("xx"), ACTF.Identity, scale=cj0, bias=cn0)
     copy(A("mvu"), A("mvs"))
     gather(A("ls0", 0, c1), A("pt0"), A("mvu", 0, c1 // 16), "v")
     gather(A("ls0", c1, G), A("pt0"), A("mvu", c1 // 16, 32), "v")
-    send("li0", "ls0", 0, c1, "la0", me + 1, 0.0, 0.5)
-    send("li0", "ls0", c1, c2, "lb0", me + 1, 0.0, 0.5)
-    send("li0", "ls0", c2, G, "lc0", me + 1, 0.0, 0.5)
-    shifted("ots", T.vo, "ld_o", A("rw", 0, 16))
+    gate.append(len(steps) - 1)
+    fill(A("cst"), 0.0)
+    ts(crel, ck, -2048.0, ALU.mult, -2047.0, ALU.add)
+    ts(ca15, ck, 15.0, ALU.is_equal, -1.0 / 16, ALU.mult)
+    ts(ck16, ck, 16.0, ALU.mult)
+    ts(c8k, ck, 8.0, ALU.mult)
+    ts(chit, ca15, -1600.0, ALU.mult, -8.5, ALU.add)
+    lin(A("hib"), A("ib"), 0.5, 0.0)
+    lin(A("qib"), A("ib"), 0.25, 0.0)
+    ts(A("zw_"), A("xb"), cz15, ALU.is_equal, cw, ALU.mult)
+    lin(A("a15"), X, 0.0, ca15)
+    lin(A("k1"), A("neg", 0, 256), 0.0, ck)
+    mm(A("pd", 0, 2), A("bw"), A("neg", 0, 2))
+    lin(cq, A("pd", 0, 1), 1.0 / 4096, QO - 2047.5 / 4096)
+    lin(A("c8", 0, SEG // 16), A("xx", 0, SEG // 16), 128.0, c8k)
+    lin(A("c8", SEG // 16, 32), A("xx", 0, 32 - SEG // 16), 128.0, c8k)
+    for c in range(NC):
+        a, b = CHS[c], CHS[c + 1]
+        lin(A("cst", a // 8, (a + b) // 16), A("xx", 0, (b - a) // 16), 256.0, ck16)
+    gate.pop()
+
+    def later():
+        gate.append(len(steps) - 1)
+        lin(A("hz_"), A("zb_"), 0.5, 0.0)
+        lin(A("nib"), A("ib"), -1.0, 0.0)
+        for name, x in (("kq", -1.0 / 3840), ("one", 1.0), ("e8", 0.0)):
+            lin(A(name), X, 0.0, x)
+        lin(A("e8", 1, 128, 2), A("xb", 0, 64), 0.0, 1.0 / 16)
+        gate.pop()
+
+    send("zi0", "zst", 0, c1, "za0", me + 1, 1.8, 0.5)
+    d = send("li0", "ls0", 0, c1, "la0", me + 1, 0.0, 0.5)
+    d = step({"g": (lambda q: q.sem_inc(T.sem["go"], 1), 0.01)}, [], [(None, ("go", 0, 1))], sem="go", n=0, after=[d])
+    dma("y", "ld_r2", T.rw[:, RA:4096], T.strat[:, RA:4096], 256 * (4096 - RA), reads=[(None, ("go", 0, 1))], writes=[A("rw", RA, 4096)])
+    for lo, hi, x in ((c1, c2, "b0"), (c2, G, "c0")):
+        d = send("zi0", "zst", lo, hi, "z" + x, me + 1, 0.0, 0.5, [d])
+        d = send("li0", "ls0", lo, hi, "l" + x, me + 1, 0.0, 0.5, [d])
+    gate.append(d)
+    select(A("tr2"), A("tr1"), [[1, 128]], ALU.is_gt, 0.0, -1)
+    select(A("tri"), A("tr2"), [[1, 128]], ALU.not_equal, 2048.0, -1)
+    gate.pop()
+    shifted("ots", T.vo, "ld_o", A("rw", 4080, 4096))
 
     for t in range(NT):
         last = t + 1 == NT
-        for u in UNITS if t else ((0,), (1,), tuple(range(2, NC))):
-            a, b = CHS[u[0]], CHS[u[-1] + 1]
+        us = CHS if t else U0
+        if t != 1:
+            extend(t)
+        for a, b in zip(us, us[1:]):
             address(t, a, b)
-            for x, y in ((a, c1), (c1, b)) if a < c1 < b else ((a, b),):
+            for x, y in ((a, FIRST), (FIRST, b)) if a < FIRST < b else ((a, b),):
                 columns(t, x, y)
         if not last:
             place(t)
-        for x, u in enumerate(UNITS):
-            a, b = CHS[u[0]], CHS[u[-1] + 1]
-            for c in u:
-                beats(t, c)
-                verdict(t, c)
-                newz(t, c)
-            send("nm%d" % t, "sb%d" % t, a // 8, b // 8, "nm%d%d" % (t, x), me - 1 - t)
-            send("zi%d" % (t + 1), "zo%d" % t, a, b, "za%d%d" % (t + 1, x), me - 1 - t if last else me + 1)
-            for c in u:
-                home(t, c)
-            if not last:
-                send("li%d" % (t + 1), "ls%d" % (t + 1), a, b, "la%d%d" % (t + 1, x), me + 2 + t)
-                if b < G:
-                    update(t, a, b)
-        extend(t)
+        for c in range(NC):
+            a, b = CHS[c], CHS[c + 1]
+            beats(t, c)
+            verdict(t, c)
+            newz(t, c)
+            if c == LC:
+                if t == 0:
+                    later()
+                if not last:
+                    tally(t)
+                verdicts(t)
+            send("nm%d" % t, "sb%d" % t, (a + b) // 16, 96 if c == LC else b // 8, "nm%d%d" % (t, c), me - 1 - t, late=LATE[c])
+            send("zi%d" % (t + 1), "zo%d" % t, a, b, "za%d%d" % (t + 1, c), me - 1 - t if last else me + 1, late=LATE[c])
+            home(t, c)
+            if last:
+                dma("y", "o_o%d" % c, T.yo[:, a:b], T.yos[:, a:b], 512 * (b - a), reads=[A("yos", a, b)])
+                dma("s" if c == LC else "y", "o_z%d" % c, T.yz[:, a:b], T.zi3[:, a:b], 256 * (b - a), reads=[A("zi3", a, b)])
+            if not last and b < G:
+                update(t, a, b)
+        if t == 1:
+            extend(t)
         if t == 0:
             shifted("pts", T.vp, "ld_q", A("sb0", 0, 2))
         if not last:
-            tally(t)
             scatter(t, 0, SEG)
             mirror(t)
-            for u in UNITS:
-                scatter(t, max(SEG, CHS[u[0]]), CHS[u[-1] + 1])
-        verdicts(t)
-    b = CHS[LC]
-    dma("y", "o_o0", T.yo[:, 0:b], T.yos[:, 0:b], 512 * b, reads=[A("yos", 0, b)])
-    dma("y", "o_z0", T.yz[:, 0:b], T.zi3[:, 0:b], 256 * b, reads=[A("zi3", 0, b)])
-    dma("y", "o_o1", T.yo[:, b:G], T.yos[:, b:G], 512 * (G - b), reads=[A("yos", b, G)])
-    dma("s", "o_z1", T.yz[:, b:G], T.zi3[:, b:G], 256 * (G - b), reads=[A("zi3", b, G)])
+            for c in range(NC):
+                scatter(t, max(SEG, CHS[c]), CHS[c + 1])
+        verdicts_out(t)
     issue()

@@ -1,3 +1,5 @@
+import math
+import numpy as np
 from concourse.bass import DstId, RemoteDMATransfer
 from concourse.mybir import AluOpType as ALU, AxisListType, ActivationFunctionType as ACTF
 
@@ -5,27 +7,40 @@ NT, G = 3, 512
 CHS = (0, 256, 448, 512)
 NC = len(CHS) - 1
 U0 = (0, 128, 256, 512)
+Z0 = (0, 128, 256, 512)
 PARTS = (0, 32, 64, 128, 192, 256, 320, 384, 448, 512)
-ZB = (0, 128, 256, 384, 512)
+CB = (0, 64, 192, 256, 384, 448, 512)
+SB = (0, 32, 64, 128, 192, 256, 320, 384, 448, 512)
+VG = ((0,), (0,), (0, 32))
+GO = 0
+ZL = 0
+WIDE = 256
+ZF = 3
+LONG = 300
+FOLD = 192
 FIRST = 64
-SHARE = ((), (), (384, 448))
+PC = ("pc", "pd")
+PV = "pz%d" % ((len(CB) - 1) % 2)
 RW = 4096 + 816
 RA = 3072
 SEG = 128
 EN = 8
+MW = 16 * max(b - a for a, b in zip(SB, SB[1:]))
 ZO, QO = 1056.0, 1048.0
 BIG = 12582912.0
-CY, GA, SC = 0.83e-3, 1.5, 3.5
-LAT, HOP = 0.1, 1.6
-FAR = 1.6
-LATE = (0.0, 0.0, 0.0, 0.0)
-FOLD = (0, 1, 2, 3)
-PA = ()
-FIX, CALL = 0.065, 0.55
-SPARE = 0.3
-RULES = [(w, s, h, f, x) for w in (6.0, 9.0, 13.0) for s in (0.12, 0.2) for h in (0.08, 0.12) for f in (0.0, 0.4, 0.8) for x in (0.1, 0.3)]
-CASES = ((-0.27, 0.0, 1.0, 63), (0.0, 0.0, 1.0, 65), (0.33, 0.0, 1.0, 76), (0.0, 1.2, 1.0, 72), (0.27, 0.0, 1.45, 100), (0.0, 0.6, 1.3, 83))
-PASSES = 4
+CY, FIX = 0.83e-3, 0.065
+CASES = ((1.45, 3.3, 1.0, 0.01, 0.6, 0.05, 0.12, 0.5, 1.0, 1.4, 0.015, 64.7),
+         (1.05, 2.0, 1.1, 0.005, 0.5, 0.04, 0.06, 0.4, 0.9, 1.2, 0.01, 58.5),
+         (1.1, 5.5, 1.25, 0.01, 0.65, 0.05, 0.12, 0.7, 1.5, 1.6, 0.02, 72.5),
+         (2.05, 5.5, 1.1, 0.01, 0.55, 0.05, 0.12, 0.6, 1.3, 1.6, 0.015, 83.5),
+         (1.3, 3.5, 1.1, 0.01, 0.6, 0.06, 0.16, 1.0, 2.0, 2.0, 0.04, 83.0),
+         (1.95, 3.0, 1.45, 0.01, 0.6, 0.06, 0.15, 0.7, 1.5, 1.7, 0.02, 102.5))
+RULES = [(9.0, s, h, f, x) for s in (0.1, 0.2) for h in (0.08, 0.12) for f in (0.0, 0.4, 0.8) for x in (0.1, 0.3)]
+PASSES = 3
+MOVES, HEAT, REACH, SEED, LOG = 75000, 0.002, 25, 12, []
+EARLY = 0.2
+POWER = 8
+SLACK = 0.0002
 
 SCRATCH = {
     "rw": ("sbuf", [128, RW], "bfloat16"), "pt0": ("sbuf", [128, 1024], "int32"),
@@ -33,7 +48,7 @@ SCRATCH = {
     "mvs": ("sbuf", [128, 32], "int32"), "mvu": ("sbuf", [128, 32], "uint16"),
     "wti": ("sbuf", [128, 8], "int32"), "zst": ("sbuf", [128, G], "bfloat16"),
     "yy": ("sbuf", [128, 16 * G], "bfloat16"), "hi": ("sbuf", [128, 16 * G], "bfloat16"), "lo": ("sbuf", [128, 16 * G], "bfloat16"),
-    "bt": ("sbuf", [128, 16 * G], "bfloat16"), "mhi": ("sbuf", [128, 1024], "bfloat16"), "mlo": ("sbuf", [128, 1024], "bfloat16"),
+    "bt": ("sbuf", [128, 16 * G], "bfloat16"), "mhi": ("sbuf", [128, MW], "bfloat16"), "mlo": ("sbuf", [128, MW], "bfloat16"),
     "qf": ("sbuf", [128, G], "float16"), "xi": ("sbuf", [128, G], "int32"), "ai": ("sbuf", [128, G], "int32"),
     "sg": ("sbuf", [128, G], "bfloat16"), "oh": ("sbuf", [128, 2 * G], "float16"),
     "hp": ("sbuf", [128, G], "bfloat16"), "lp": ("sbuf", [128, G], "bfloat16"), "sm": ("sbuf", [128, G], "float16"), "s2": ("sbuf", [128, G], "float16"),
@@ -41,16 +56,18 @@ SCRATCH = {
     "pli": ("sbuf", [128, 32], "int32"), "plm": ("sbuf", [128, 32], "int32"), "plu": ("sbuf", [128, 32], "uint16"),
     "yps": ("sbuf", [128, G], "float32"), "yos": ("sbuf", [128, G], "float32"),
     "lsi": ("sbuf", [128, G], "int32"), "nri": ("sbuf", [128, 2 * G], "int32"), "nrf": ("sbuf", [128, 2 * G], "float32"),
-    "nrh": ("sbuf", [128, G], "float16"),
+    "nrh": ("sbuf", [128, G], "float16"), "hh0": ("sbuf", [128, G], "float16"), "lh0": ("sbuf", [128, G], "float16"),
+    "hh1": ("sbuf", [128, G], "float16"), "lh1": ("sbuf", [128, G], "float16"),
     "an": ("sbuf", [128, 4], "float32"), "ani": ("sbuf", [128, 8], "int32"),
     "xx": ("sbuf", [128, G], "float32"), "xb": ("sbuf", [128, 144], "bfloat16"), "xg": ("sbuf", [128, 128], "bfloat16"),
     "pint": ("sbuf", [128, 8], "int32"), "col": ("sbuf", [128, 32], "float32"),
-    "zb_": ("sbuf", [128, 144], "bfloat16"), "zw_": ("sbuf", [128, 144], "bfloat16"), "hz_": ("sbuf", [128, 144], "bfloat16"),
-    "neg": ("sbuf", [128, G], "bfloat16"), "k1": ("sbuf", [128, 256], "bfloat16"),
+    "zb_": ("sbuf", [128, 144], "bfloat16"), "zw_": ("sbuf", [128, 144], "bfloat16"),
+    "x4": ("sbuf", [128, 144], "int32"), "bw4": ("sbuf", [128, 144], "bfloat16"),
+    "neg": ("sbuf", [128, G], "bfloat16"), "k1": ("sbuf", [128, 512], "bfloat16"),
     "nr0": ("sbuf", [128, G], "float16"), "nr1": ("sbuf", [128, G], "float16"), "nr2": ("sbuf", [128, G], "float32"),
     "cst": ("sbuf", [128, 64], "float16"), "c8": ("sbuf", [128, 32], "int32"),
 }
-for _n in ("bw", "kc", "ib", "i4", "hib", "qib", "nib", "tri", "tr1", "tr2", "a15", "kq", "e8", "one"):
+for _n in ("bw", "kc", "ib", "i4", "hib", "qib", "tri", "tr1", "tr2", "a15", "kq", "kw", "un0", "un1", "un2", "un3"):
     SCRATCH[_n] = ("sbuf", [128, 128], "bfloat16")
 for _t in range(NT):
     SCRATCH["li%d" % _t] = ("sbuf", [128, G], "float16")
@@ -75,6 +92,225 @@ for _t in range(NT):
         if _t:
             SEMAPHORES.append("la%d%d" % (_t, _c))
 PLAN = []
+QUEUES = "vspgy"
+
+
+def arrange(steps):
+    n, nk = len(steps), len(CASES)
+    above, pre = [0] * n, []
+    for i, s in enumerate(steps):
+        firm = [j for j in s["pre"] if j not in s["order"]]
+        for j in firm:
+            above[i] |= above[j] | 1 << j
+        pre.append([j for j in s["pre"] if not any(above[x] >> j & 1 for x in firm)])
+    post = [[] for _ in steps]
+    for i in range(n):
+        for j in pre[i]:
+            post[j].append(i)
+    leaves = [i for i in range(n) if not post[i]]
+
+    def cost(kind, size, c):
+        ga, sc, slow, call, pe, _, _, remote, far, hop, row, _ = c
+        if kind == "r":
+            return remote + size[2], 0.3, 128 / EN * row * size[3] + size[0] / 2e5, far - 0.3 + size[1]
+        if kind == "d":
+            return 0.05, 0.6 * hop, math.ceil(size[1] / 16) * row + size[0] / 4e5, 0.4 * hop
+        us = {"v": call + max(64, size) * CY * slow, "s": FIX + max(64, size) * CY * slow, "p": size * CY * pe * slow, "g": size * slow,
+              "gv": 0.05 + size * ga * CY * slow, "gs": FIX + size * ga * CY * slow, "x": 0.05 + size * sc * CY * slow}
+        return us[kind], None, None, None
+
+    dur = [{e: [cost(k, size, c) for c in CASES] for e, (_, k, size) in s["on"].items()} for s in steps]
+
+    def gap(j, i, ej, ei, c):
+        s = steps[j]
+        if j in steps[i]["order"] or s["sem"] is not None and s["n"] or ej == ei == "p":
+            return 0.0
+        return c[5] if ej == ei else c[6] * (1.5 if ej == "p" else 1.0)
+
+    def plan(before, behind, way, fixed, wait, small, hold, far, spare):
+        left, free, eng, end = [len(x) for x in before], {e: 0.0 for e in QUEUES}, [None] * n, [0.0] * n
+        pool, order = {e: {} for e in QUEUES}, []
+
+        def offer(i):
+            for e in [fixed[i]] if fixed else steps[i]["on"]:
+                pool[e][i] = max([end[j] + (lag(i, j, e, eng[j], far) if fixed else lag(j, i, eng[j], e, far)) for j in before[i]]
+                                 + [lag(i, i, e, "", far) if fixed else 0.0])
+
+        for i in range(n):
+            if not left[i]:
+                offer(i)
+        while len(order) < n:
+            now, e = min((max(free[e], min(pool[e].values())), e) for e in QUEUES if pool[e])
+            near = [i for i, r in pool[e].items() if r <= now + hold]
+            if e == "v" and not fixed:
+                near = ([i for i, r in pool[e].items() if r <= now + spare and len(steps[i]["on"]) == 1]
+                        + [i for i in near if dur[i]["v"][0][0] < small]) or near
+                near = [i for i in near if pool[e][i] <= max(now, min(pool[e][j] for j in near)) + hold]
+            i = max(near, key=lambda i: (way[i] - wait * max(0.0, pool[e][i] - now), -i))
+            free[e] = end[i] = max(now, pool[e][i]) + dur[i][e][0][0]
+            eng[i] = e
+            order.append(i)
+            for x in QUEUES:
+                pool[x].pop(i, None)
+            for j in behind[i]:
+                left[j] -= 1
+                if not left[j]:
+                    offer(j)
+        return order, eng, end
+
+    def lag(j, i, ej, ei, far):
+        d = dur[j][ej][0]
+        if d[1] is None or j in steps[i]["order"]:
+            return gap(j, i, ej, ei, CASES[0])
+        return d[1] + d[2] + d[3] + steps[j]["behind"] + (far if steps[j]["n"] < 0 else 0.0)
+
+    def edges(i, eng):
+        return [[(j + n if j in steps[i]["order"] else j, gap(j, i, eng[j], eng[i], c)) for j in pre[i]] for c in CASES]
+
+    def length(order, eng, ed, ends, q, r, reach, limit, moved=""):
+        last = {}
+        for i in reversed(order[:q]):
+            last.setdefault(eng[i], i)
+            if steps[i]["sem"] and steps[i]["n"]:
+                last.setdefault("d", i)
+            if len(last) == 6:
+                break
+        total, new, least = 0.0, [], r
+        touched = set(moved) | set(eng[i] for i in order[q:r]) | set("d" for i in order[q:r] if steps[i]["sem"] and steps[i]["n"])
+        while touched and least < n:
+            i = order[least]
+            touched.discard(eng[i])
+            if steps[i]["sem"] and steps[i]["n"]:
+                touched.discard("d")
+            least += 1
+        for k in range(nk):
+            old = ends[k]
+            end = list(old)
+            free = {e: end[n + last[e]] if e in last else 0.0 for e in QUEUES}
+            dma = end[2 * n + last["d"]] if "d" in last else 0.0
+            far = least
+            for p in range(q, n):
+                if p > far:
+                    break
+                i = order[p]
+                e = eng[i]
+                t = free[e]
+                for j, x in ed[i][k]:
+                    x += end[j]
+                    if x > t:
+                        t = x
+                us, a, b, c = dur[i][e][k]
+                free[e] = end[n + i] = t = t + us
+                if a is not None:
+                    t += a
+                    end[2 * n + i] = dma = (t if t > dma else dma) + b
+                    t = dma + c
+                    if reach[i] > far and abs(end[n + i] - old[n + i]) + abs(dma - old[2 * n + i]) > 1e-9:
+                        far = reach[i]
+                end[i] = t
+                if reach[i] > far and abs(t - old[i]) > 1e-9:
+                    far = reach[i]
+            x = ((max(end[i] for i in leaves) + EARLY * sum(end[:n]) / n) / (1 + EARLY / 2) / CASES[k][-1]) ** POWER / POWER
+            total += x - old[3 * n]
+            end[3 * n] = x
+            if total > limit + SLACK * (nk - 1 - k):
+                return total, None
+            new.append(end)
+        return total, new
+
+    def reaches(order, eng):
+        place, reach, last = [0] * n, [0] * n, dict.fromkeys(QUEUES + "d", 0)
+        for p in range(n - 1, -1, -1):
+            i = order[p]
+            place[i], e = p, eng[i]
+            x, last[e] = last[e], p
+            for j in post[i]:
+                if place[j] > x:
+                    x = place[j]
+            if dur[i][e][0][1] is not None:
+                x, last["d"] = max(x, last["d"]), p
+            reach[i] = x
+        return reach
+
+    def held(order, eng, ed, ends):
+        out, last, before, place = [], {}, {}, {}
+        for p, i in enumerate(order):
+            before[i], last[eng[i]], place[i] = last.get(eng[i]), i, p
+        for k in range(nk):
+            end = ends[k]
+            i = max(leaves, key=lambda x: end[x])
+            while i is not None:
+                t, b = end[n + i] - dur[i][eng[i]][k][0], before[i]
+                if b is not None and end[n + b] > t - 1e-9:
+                    out += [place[i], place[b]]
+                    i = b
+                else:
+                    i = max(ed[i][k], key=lambda x: end[x[0]] + x[1], default=(None,))[0]
+                    i = i if i is None else i % n
+        return out
+
+    def whole(order, eng):
+        ed = [edges(i, eng) for i in range(n)]
+        return (ed,) + length(order, eng, ed, [[0.0] * (3 * n + 1)] * nk, 0, n, [n] * n, 99.0)
+
+    def by_time(order, eng, end):
+        return sorted(order, key=lambda i: end[n + i] - dur[i][eng[i]][0][0])
+
+    best = None
+    for rule in RULES:
+        eng = [list(s["on"])[0] for s in steps]
+        way = [0.0] * n
+        for i in range(n - 1, -1, -1):
+            way[i] = dur[i][eng[i]][0][0] + max([way[j] + lag(i, j, eng[i], eng[j], 0.0) for j in post[i]] + [lag(i, i, eng[i], "", 0.0)])
+        for _ in range(PASSES):
+            order, eng, end = plan(pre, post, way, None, *rule)
+            total = whole(order, eng)[1]
+            if best is None or total < best[0]:
+                best = (total, order, eng)
+            way = plan(post, pre, end, eng, *rule)[2]
+    LOG.append(best[0])
+
+    rng = np.random.default_rng(SEED)
+    now, order, eng = best
+    ed, now, ends = whole(order, eng)
+    hot, reach, age = held(order, eng, ed, ends), reaches(order, eng), 0
+    for it in range(MOVES):
+        u = rng.random(6)
+        p = hot[int(u[0] * len(hot))] if u[1] < 0.7 else int(u[0] * n)
+        i, e2, o2, d2, q, r = order[p], eng, order, ed, p, p + 1
+        if len(steps[i]["on"]) > 1 and u[2] < 0.3:
+            e2, d2 = list(eng), list(ed)
+            e2[i] = [e for e in steps[i]["on"] if e != eng[i]][0]
+            for j in [i] + post[i]:
+                d2[j] = edges(j, e2)
+        if e2 is eng or u[3] < 0.5:
+            d, need = 1 + int(u[4] * 2 % 1 * REACH), {i}
+            if u[4] < 0.5:
+                q = max(0, p - d)
+                for x in reversed(order[q:p]):
+                    if any(y in need for y in post[x]):
+                        need.add(x)
+                o2 = order[:q] + [x for x in order[q:r] if x in need] + [x for x in order[q:p] if x not in need] + order[r:]
+            else:
+                r = min(n, r + d)
+                for x in order[p + 1:r]:
+                    if any(y in need for y in pre[x]):
+                        need.add(x)
+                o2 = order[:p] + [x for x in order[p:r] if x not in need] + [x for x in order[p:r] if x in need] + order[r:]
+        x, new = length(o2, e2, d2, ends, q, max(r, reach[i] + 1) if e2 is not eng else r, reach,
+                        -HEAT * (1 - it / MOVES) * math.log(1 - u[5]), "sv" if e2 is not eng else "")
+        if new:
+            now, order, eng, ed, ends, age = now + x, o2, e2, d2, new, age + 1
+            if age % 64 == 0:
+                order = by_time(order, eng, ends[0])
+                ed, now, ends = whole(order, eng)
+            if age % 8 == 0:
+                hot = held(order, eng, ed, ends)
+            reach = reaches(order, eng)
+            if now < best[0] and age % 64 == 0:
+                best = (now, order, eng, [max(end[i] for i in leaves) for end in ends])
+    LOG.extend([best[0], best[-1]])
+    return best[1:3]
 
 
 def rank_program(g, core, T, topo):
@@ -85,9 +321,10 @@ def rank_program(g, core, T, topo):
     N = len(cores)
     Q = {"v": g.vector, "s": g.scalar, "p": g.tensor, "g": g, "y": g.sync}
 
-    steps, recs, gate = [], {}, []
+    steps, recs, gate, run, turns = [], {}, [], [], []
 
-    def step(on, reads, writes, lat=LAT, sem=None, n=1, lands=None, after=(), ind=0.0):
+    def step(on, reads, writes, sem=None, n=1, lands=None, after=(), behind=0.0):
+        flush()
         after = list(after) + gate
         i, pre = len(steps), {}
         for w, lst in ((0, reads), (1, writes)):
@@ -96,7 +333,7 @@ def rank_program(g, core, T, topo):
                     if b in BANKS:
                         pre[r[3]] = pre.get(r[3], False) or ("p" not in on and bool(w or r[2]))
                     elif r[0] < hi and lo < r[1] and (w or r[2]):
-                        pre[r[3]] = pre.get(r[3], False) or bool(r[2])
+                        pre[r[3]] = True
         for w, lst in ((0, reads), (1, writes)):
             for _, (b, lo, hi) in lst:
                 old = recs.get(b, [])
@@ -108,7 +345,7 @@ def rank_program(g, core, T, topo):
             recs.setdefault(lands[0], []).append((lands[1], lands[2], 1, i))
         order = set(after) - set(pre)
         pre.update({j: False for j in order})
-        steps.append({"on": on, "pre": pre, "lat": lat, "sem": sem, "n": n, "order": order, "ind": ind})
+        steps.append({"on": on, "pre": pre, "sem": sem, "n": n, "order": order, "behind": behind})
         return i
 
     def A(n, lo=0, hi=None, st=1, p=128):
@@ -119,15 +356,14 @@ def rank_program(g, core, T, topo):
     def width(a):
         return a[0].shape[1]
 
-    def cyc(n, rate, *aps):
-        if aps and all(SCRATCH[a[1][0]][2] in ("bfloat16", "float16", "uint16") for a in aps):
-            rate /= 2
-        return max(64, n * rate) * CY
+    def cyc(*aps):
+        return width(aps[0]) * (0.5 if all(SCRATCH[a[1][0]][2] in ("bfloat16", "float16", "uint16") for a in aps) else 1.0)
 
-    def dma(e, sem, out, in_, size, reads=(), writes=(), after=()):
-        return step({e: (lambda q: q.dma_start(out, in_), 0.05)}, reads, writes, HOP + size / 4e5, sem, 16, after=after)
+    def dma(e, sem, out, in_, size, reads=(), writes=(), after=(), behind=0):
+        return step({e: (lambda q: q.dma_start(out, in_), "d", (size, max(out.shape[0], in_.shape[0])))}, reads, writes, sem, 16,
+                    after=after, behind=behind / 4e5)
 
-    def send(buf, src, lo, hi, sem, to, start=0.0, late=0.0, after=(), fold=None):
+    def send(buf, src, lo, hi, sem, to, start=0.0, late=0.0, after=(), fold=(), op=2):
         dst = cores[to % N]
         rid, pid, _ = topo.addr(dst)
         m = 0
@@ -135,82 +371,24 @@ def rank_program(g, core, T, topo):
             m |= 1 << x
         call = lambda q: q.remote_dma(T[buf][:, lo:hi], T[src][:, lo:hi], T.sem[sem], T.sem["loc"], pid, rid, m)
         if fold:
-            one = RemoteDMATransfer(dst_ids=[DstId(rid=rid, pnc=pid)], dma_engine_mask=m, remote_sem=T.sem[sem], alu_op=2,
-                                    srcs=[T[src][:, lo:hi], T[fold][:, lo:hi]], dsts=[T[buf][:, lo:hi]])
+            one = RemoteDMATransfer(dst_ids=[DstId(rid=rid, pnc=pid)], dma_engine_mask=m, remote_sem=T.sem[sem], alu_op=op,
+                                    srcs=[T[x][:, lo:hi] for x in (src,) + fold], dsts=[T[buf][:, lo:hi]])
             call = lambda q: q.remote_dma_fused([one], local_sem=T.sem["loc"])
-        return step({"g": (call, CALL + start)}, [A(x, lo, hi) for x in (src, fold) if x], [], FAR + late + (384 if fold else 256) * (hi - lo) / 1e5, sem, -EN, (buf, lo, hi), after)
+        i = step({"g": (call, "r", (256 * (1 + len(fold)) * (hi - lo), late, start, 1 + len(fold)))}, [A(x, lo, hi) for x in (src,) + fold], [],
+                 sem, -EN, (buf, lo, hi), after)
+        return i
 
     def issue():
-        n = len(steps)
-        post = [[] for _ in steps]
-        for i, s in enumerate(steps):
-            for j in s["pre"]:
-                post[j].append(i)
-
-        def gap(j, i, ej, ei, far=0.0):
-            if j in steps[i]["order"] or (ej == ei and not steps[i]["pre"][j] and steps[j]["sem"] is None and steps[i]["sem"] is None):
-                return 0.0
-            return steps[j]["lat"] + (far if steps[j]["n"] < 0 else 0.0)
-
-        def plan(before, behind, way, fixed, wait, small, hold, far, spare):
-            left, free, eng, end = [len(x) for x in before], {e: 0.0 for e in Q}, [None] * n, [0.0] * n
-            pool, order = {e: {} for e in Q}, []
-
-            def offer(i):
-                for e in [fixed[i]] if fixed else steps[i]["on"]:
-                    pool[e][i] = max([end[j] + (gap(i, j, e, eng[j], far) if fixed else gap(j, i, eng[j], e, far)) for j in before[i]]
-                                     + [steps[i]["lat"] if fixed else 0.0])
-
-            for i in range(n):
-                if not left[i]:
-                    offer(i)
-            while len(order) < n:
-                now, e = min((max(free[e], min(pool[e].values())), e) for e in Q if pool[e])
-                near = [i for i, r in pool[e].items() if r <= now + hold]
-                if e == "v" and not fixed:
-                    near = ([i for i, r in pool[e].items() if r <= now + spare and len(steps[i]["on"]) == 1]
-                            + [i for i in near if steps[i]["on"]["v"][1] < small]) or near
-                    near = [i for i in near if pool[e][i] <= max(now, min(pool[e][j] for j in near)) + hold]
-                i = max(near, key=lambda i: (way[i] - wait * max(0.0, pool[e][i] - now), -i))
-                free[e] = end[i] = max(now, pool[e][i]) + steps[i]["on"][e][1]
-                eng[i] = e
-                order.append(i)
-                for x in Q:
-                    pool[x].pop(i, None)
-                for j in behind[i]:
-                    left[j] -= 1
-                    if not left[j]:
-                        offer(j)
-            return order, eng, end
-
-        def span(order, eng, more, far, slow):
-            free, end = {e: 0.0 for e in Q}, [0.0] * n
-            for i in order:
-                e, s = eng[i], steps[i]
-                free[e] = end[i] = (max([free[e]] + [end[j] + gap(j, i, eng[j], e, far) for j in s["pre"]]) + (far / 5 if s["n"] < 0 else 0.0)
-                                    + (s["on"][e][1] + more * s["ind"]) * (slow if e in "vsp" else 1.0))
-            return max(end[i] + steps[i]["lat"] for i in range(n))
-
-        pre, best = [list(s["pre"]) for s in steps], None
-        for rule in () if PLAN else RULES:
-            eng = [list(s["on"])[0] for s in steps]
-            way = [0.0] * n
-            for i in range(n - 1, -1, -1):
-                way[i] = steps[i]["on"][eng[i]][1] + max([way[j] + gap(i, j, eng[i], eng[j]) for j in post[i]] + [steps[i]["lat"]])
-            for _ in range(PASSES):
-                order, eng, end = plan(pre, post, way, None, *rule)
-                total = sum(span(order, eng, *c[:3]) / c[3] for c in CASES)
-                if best is None or total < best[0]:
-                    best = (total, order, eng)
-                way = plan(post, pre, end, eng, *rule)[2]
-        if best:
-            PLAN.extend(best[1:])
+        if not PLAN:
+            PLAN.extend(arrange(steps))
         order, eng = PLAN
+        other = set(j for i, s in enumerate(steps) if eng[i] != "p" for j in s["pre"])
         cnt, known, tok = {}, {e: {} for e in Q}, {}
         for i in order:
             s, e = steps[i], eng[i]
             k = known[e]
-            for j in sorted((j for j in s["pre"] if gap(j, i, eng[j], e)), key=lambda j: -tok[j][1]):
+            need = [j for j, w in s["pre"].items() if j not in s["order"] and (w or eng[j] != e or steps[j]["sem"] or s["sem"])]
+            for j in sorted(need, key=lambda j: -tok[j][1]):
                 sem, val, vc = tok[j]
                 if k.get(sem, 0) < val:
                     Q[e].wait_ge(T.sem[sem], val)
@@ -225,19 +403,32 @@ def rank_program(g, core, T, topo):
                 tok[i] = (s["sem"], 1, {})
             else:
                 sem = s["sem"] or "q" + e
-                if e != "p" or any(eng[j] != "p" for j in post[i]):
+                if e != "p" or i in other:
                     cnt[sem] = cnt.get(sem, 0) + s["n"]
-                    ins.then_inc(T.sem[sem], s["n"])
+                    if isinstance(ins, list):
+                        for x in ins:
+                            x.then_inc(T.sem[sem], 1)
+                    else:
+                        ins.then_inc(T.sem[sem], s["n"])
                 tok[i] = (sem, cnt.get(sem, 0), dict(k))
         for sem in OUTS + ["loc", "qv", "qs", "qp", "qg"]:
             if cnt.get(sem, 0) > known["g"].get(sem, 0):
                 g.wait_ge(T.sem[sem], cnt[sem])
 
     def mm(out, l, r, start=True, stop=True):
-        step({"p": (lambda q: q.matmul(out[0], l[0], r[0], start, stop), max(64, width(r)) * CY / 2)}, [l, r], [out], 1.5 * LAT)
+        run.append((out, l, r, start, stop))
+        if stop:
+            flush()
+
+    def flush():
+        if run:
+            ms = list(run)
+            run.clear()
+            step({"p": (lambda q: [q.matmul(o[0], l[0], r[0], a, b) for o, l, r, a, b in ms][-1], "p", sum(max(64, width(m[2])) for m in ms))},
+                 [x for m in ms for x in m[1:3]], [m[0] for m in ms])
 
     def copy(out, in_):
-        step({"v": (lambda q: q.tensor_copy(out[0], in_[0]), cyc(width(out), 1, out, in_))}, [in_], [out])
+        step({"v": (lambda q: q.tensor_copy(out[0], in_[0]), "v", cyc(out, in_))}, [in_], [out])
 
     def ts(out, in_, s1, op0, s2=None, op1=None):
         rd = [in_] + [s for s in (s1, s2) if isinstance(s, tuple)]
@@ -247,51 +438,54 @@ def rank_program(g, core, T, topo):
             call = lambda q: q.tensor_scalar(out[0], in_[0], a1, None, op0)
         else:
             call = lambda q: q.tensor_scalar(out[0], in_[0], a1, a2, op0, op1)
-        step({"v": (call, cyc(width(out), 1, out, in_))}, rd, [out])
+        step({"v": (call, "v", cyc(out, in_))}, rd, [out])
 
     def tt(out, a, b, op):
-        step({"v": (lambda q: q.tensor_tensor(out[0], a[0], b[0], op), cyc(width(out), 1 if b[1][0] in BANKS else 2))}, [a, b], [out])
+        step({"v": (lambda q: q.tensor_tensor(out[0], a[0], b[0], op), "v", cyc(out, a) if b[1][0] in BANKS else 2 * width(out))}, [a, b], [out])
 
     def act(out, in_, fn, **kw):
         rd = [in_] + [x for x in kw.values() if isinstance(x, tuple)]
         kw = {n: x[0] if isinstance(x, tuple) else x for n, x in kw.items()}
-        step({"s": (lambda q: q.activation(out[0], in_[0], fn, **kw), FIX + cyc(width(out), 1))}, rd, [out])
+        step({"s": (lambda q: q.activation(out[0], in_[0], fn, **kw), "s", width(out))}, rd, [out])
 
     def lin(out, in_, scale, bias, on="sv"):
-        col = isinstance(bias, tuple)
-        b = bias[0] if col else bias
-        calls = {"s": (lambda q: q.activation(out[0], in_[0], ACTF.Identity if col else ACTF.Copy, scale=scale, bias=b), FIX + cyc(width(out), 1)),
-                 "v": (lambda q: q.tensor_scalar(out[0], in_[0], scale, b, ALU.mult, ALU.add), cyc(width(out), 1, out, in_))}
-        step({e: calls[e] for e in on}, [in_, bias] if col else [in_], [out])
+        col = isinstance(bias, tuple) or isinstance(scale, tuple)
+        if turns and cyc(out, in_) >= LONG:
+            on = "s"
+        a, b = [x[0] if isinstance(x, tuple) else x for x in (scale, bias)]
+        calls = {"s": (lambda q: q.activation(out[0], in_[0], ACTF.Identity if col else ACTF.Copy, scale=a, bias=b), "s", width(out)),
+                 "v": (lambda q: q.tensor_scalar(out[0], in_[0], a, b, ALU.mult, ALU.add), "v", cyc(out, in_))}
+        step({e: calls[e] for e in on}, [in_] + [x for x in (scale, bias) if isinstance(x, tuple)], [out])
 
-    def gather(out, win, off, on="sv", scale=1.0):
-        c = width(out) * GA * CY
-        calls = {"s": (lambda q: q.activation(out[0], win[0].indirect(off[0]), ACTF.Copy, scale=scale), FIX + c),
-                 "v": (lambda q: q.tensor_scalar(out[0], win[0].indirect(off[0]), scale, None, ALU.mult), 0.05 + c)}
-        step({e: calls[e] for e in on}, [win, off], [out], ind=c)
+    def gather(out, win, off, on="sv", scale=1.0, bias=0.0):
+        calls = {"s": (lambda q: q.activation(out[0], win[0].indirect(off[0]), ACTF.Copy, scale=scale, bias=bias), "gs", width(out)),
+                 "v": (lambda q: q.tensor_scalar(out[0], win[0].indirect(off[0]), scale, bias, ALU.mult, ALU.add), "gv", width(out))}
+        step({e: calls[e] for e in on}, [win, off], [out])
 
     def gather_tt(out, win, off, b, op):
-        step({"v": (lambda q: q.tensor_tensor(out[0], win[0].indirect(off[0]), b[0], op), 0.05 + width(out) * GA * CY)}, [win, off, b], [out],
-             ind=width(out) * GA * CY)
+        step({"v": (lambda q: q.tensor_tensor(out[0], win[0].indirect(off[0]), b[0], op), "gv", width(out))}, [win, off, b], [out])
 
     def fill(out, c):
-        step({"v": (lambda q: q.memset(out[0], c), cyc(width(out), 1, out))}, [], [out])
+        step({"v": (lambda q: q.memset(out[0], c), "v", cyc(out))}, [], [out])
 
-    def iota(out, pattern, cm, small=True, base=0, after=()):
+    def iota(out, pattern, cm, small=True, base=0):
         kw = {"allow_small_or_imprecise_dtypes": True} if small else {}
-        step({"g": (lambda q: q.iota(out[0], pattern, base, cm, **kw), 0.13 + 2 * width(out) * CY)}, list(after), [out])
+        step({"g": (lambda q: q.iota(out[0], pattern, base, cm, **kw), "g", 0.13 + 2 * width(out) * CY)}, [], [out])
 
     def select(out, in_, pattern, op, other, cm):
-        step({"g": (lambda q: q.affine_select(out[0], in_[0], pattern, op, other, 0, cm), 0.17 + 2 * width(out) * CY)}, [in_], [out])
+        step({"g": (lambda q: q.affine_select(out[0], in_[0], pattern, op, other, 0, cm), "g", 0.17 + 2 * width(out) * CY)}, [in_], [out])
 
-    c1, c2, LC = U0[1], U0[2], NC - 1
-    d = dma("s", "ld_z", T.zst[:, 0:c1], T.z0[:, 0:c1], 256 * c1, writes=[A("zst", 0, c1)])
-    dma("s", "ld_wt", T.wti[:, 0:1], T.wt[:], 256 * c1, writes=[A("wti", 0, 1)], after=[d])
-    d = dma("y", "ld_mv", T.mvs[:], T.mv[:], 256 * c1, writes=[A("mvs")])
-    d = dma("y", "ld_p", T.pt0[:], T.vp[:], 580000, writes=[A("pt0")], after=[d])
-    d = dma("y", "ld_z2", T.zst[:, c1:G], T.z0[:, c1:G], 680000, writes=[A("zst", c1, G)], after=[d])
-    dma("y", "ld_r", T.rw[:, 0:RA], T.strat[:, 0:RA], 680000 + 256 * RA, writes=[A("rw", 0, RA)], after=[d])
-    lin(A("rw", 4096, 4096 + 560), A("rw", 0, 560), 1.0, 0.0, "s")
+    c1, z1, LC = U0[1], Z0[1], NC - 1
+    d = dma("s", "ld_z", T.zst[:, 0:z1], T.z0[:, 0:z1], 256 * z1, writes=[A("zst", 0, z1)])
+    dma("s", "ld_wt", T.wti[:, 0:1], T.wt[:], 512, writes=[A("wti", 0, 1)], after=[d])
+    d = dma("y", "ld_mv", T.mvs[:], T.mv[:], 16384, writes=[A("mvs")])
+    d = dma("y", "ld_p", T.pt0[:], T.vp[:], 524288, writes=[A("pt0")], after=[d], behind=256 * z1)
+    if not ZL:
+        d = dma("y", "ld_z2", T.zst[:, z1:G], T.z0[:, z1:G], 256 * (G - z1), writes=[A("zst", z1, G)], after=[d], behind=600000)
+    d = dma("y", "ld_r", T.rw[:, 0:RA], T.strat[:, 0:RA], 256 * RA, writes=[A("rw", 0, RA)], after=[d], behind=680000)
+    if ZL:
+        d = dma("y", "ld_z2", T.zst[:, z1:G], T.z0[:, z1:G], 256 * (G - z1), writes=[A("zst", z1, G)], after=[d], behind=600000 + 256 * RA)
+    lin(A("rw", 4096, 4096 + 560), A("rw", 0, 560), 1.0, 0.0)
     fill(A("rw", 4096 + 560, RW), 0.0)
 
     def shifted(buf, src, sem, after):
@@ -299,69 +493,67 @@ def rank_program(g, core, T, topo):
         recs[buf].append((0, 1024, 1, dma("y", sem + "0", T[buf][0:1, 0:1024], src[0:1, :], 4096, reads=[after])))
 
     C = lambda i: A("col", i, i + 1)
-    cp, ck, cg16, cz15, c37, ck16, c8k, cj0, cn0, chit, crel, ca15, cw, cq, cadd = [C(i) for i in range(15)]
+    cp, ck, cg16, cz15, c37, ck16, c8k, cj0, cn0, chit, crel, ca15, cw, cq, cadd, c4 = [C(i) for i in range(16)]
 
     def zi(t, *r):
         return A("zi%d" % t, *r)
 
     def address(t, lo, hi):
         n = hi - lo
-        pu = A("pu", 0, n)
-        mm(pu, A("bw"), zi(t, lo, hi))
-        lin(A("qf", lo, hi), pu, 1.0 / 4096, cq if t else QO - 2047.5 / 4096)
-        mm(pu, A("kc"), A("neg", 0, n), True, False)
-        if t:
-            mm(pu, A("bw"), A("neg", 0, n), False, False)
+        pu, fold = A("pu", 0, n), 4 if n >= FOLD else 1
+        qf = A("qf", lo, lo + n // fold)
+        for s in range(fold):
+            mm(A("pu", 0, n // fold), A("bw4", 12 - 4 * s, 140 - 4 * s) if fold > 1 else A("bw"), zi(t, lo + s, hi, fold), s == 0, s == fold - 1)
+        lin(qf, A("pu", 0, n // fold), 1.0 / 4096, cq if t else QO - 2047.5 / 4096)
+        mm(pu, A("kw" if t else "kc"), A("neg", 0, n), True, False)
         mm(pu, A("bw"), zi(t, lo, hi), False, False)
-        mm(pu, A("i4"), A("qf", lo, hi), False, True)
+        for s in range(fold):
+            mm(A("pu", s, n, fold), A("un%d" % s if fold > 1 else "i4"), qf, False, s == fold - 1)
         tt(A("xi", lo, hi), A("li%d" % t, lo, hi), pu, ALU.mult)
         ts(A("ai", lo, hi), A("xi", lo, hi), 5, ALU.arith_shift_right, 4095, ALU.bitwise_and)
 
-    def parts(a, b):
-        return [(x, y) for x, y in zip(PARTS, PARTS[1:]) if a <= x and y <= b]
+    def within(bounds, a, b):
+        return [(x, y) for x, y in zip(bounds, bounds[1:]) if a <= x and y <= b]
 
     def columns(t, a, b):
         lin(A("of%d" % t, a, b), A("ai", a, b), 1.0, cadd if t else c37)
-        for i, j in parts(a, b):
-            gather(A("yy", 16 * i, 16 * j), A("rw", 0, RW), A("of%d" % t, i, j))
+        for i, j in within(PARTS, a, b):
+            gather(A("yy", 16 * i, 16 * j), A("rw", 0, RW), A("of%d" % t, i, j), "sv" if VG is None else "v" if i in VG[t] else "s")
 
     def beats(t, c):
         a, b = CHS[c], CHS[c + 1]
-        for x, y in parts(a, b):
-            lo, m, pc = 16 * x, y - x, A("pc", x - a, y - a)
-            j = max(i for i in range(len(ZB) - 1) if ZB[i] <= x)
-            z0, z1, pz = ZB[j], ZB[j + 1], "pz%d" % (j % 2)
-            if x == z0:
-                if t:
-                    mm(A(pz, 0, 4 * (z1 - z0)), A("ib"), A("neg", 0, 4 * (z1 - z0)), True, False)
-                for j in range(4):
-                    mm(A(pz, j, 4 * (z1 - z0), 4), A("ib"), zi(t, z0, z1), not t, not t or j == 3)
-            odd = x in SHARE[t]
-            if odd:
-                pd = A("pd", 0, 8 * m)
-                mm(pd, A("ib"), A("yy", 16 * x + 1, 16 * y, 2), True, False)
-                for j in range(8):
-                    mm(A("pd", j, 8 * m, 8), A("nib"), zi(t, x, y), False, j == 7)
-                act(A("bt", lo + 8 * m, lo + 16 * m), pd, ACTF.Sign, bias=(ZO if t else 0.0) - 0.5)
-                mm(pc, A("e8"), A("one", 0, m), True, False)
-                for j in range(7):
-                    mm(pc, A("hz_", 14 - 2 * j, 142 - 2 * j), A("bt", lo + 8 * m + j, lo + 16 * m, 8), False, False)
-            for q, s in ((0, 4), (2, 4)) if odd else ((0, 4), (1, 4), (2, 4), (3, 8), (7, 16)):
-                e = 16 // s
-                tt(A("bt", lo, lo + e * m), A("yy", 16 * x + q, 16 * y, s), A(pz, 4 * (x - z0), 4 * (y - z0), s // 4), ALU.is_gt)
-                for j in range(e):
-                    k = q + s * j
-                    mm(pc, A("zb_", 15 - k, 143 - k), A("bt", lo + j, lo + e * m, e), k == 0 and not odd, k == (14 if odd else 7))
-                lo += e * m
+        for x, y in within(CB, a, b):
+            m = y - x
+            e = max(1, WIDE // m)
+            s, pc, pz = 16 // e, A(PC[c % 2], x - a, y - a), "pz%d" % (CB.index(x) % 2)
+            if t:
+                mm(A(pz, 0, e * m), A("ib"), A("neg", 0, e * m), True, False)
+            for j in range(e):
+                mm(A(pz, j, e * m, e), A("ib"), zi(t, x, y), not t, not t or j == e - 1)
+            rows = [q for q in range(s) if q < 15]
+            for q0 in range(0, len(rows), max(1, s // 4)):
+                some = rows[q0:q0 + max(1, s // 4)]
+                f = {q: 2 if q == 7 and e == 2 and m >= 128 else 1 for q in some}
+                compare([A("bt", 16 * x + q * e * m, 16 * x + q * e * m + e * m // f[q]) for q in some],
+                        [A("yy", 16 * x + q, 16 * y, s * f[q]) for q in some], [A(pz, 0, e * m, f[q]) for q in some])
+                for q in some:
+                    lo = 16 * x + q * e * m
+                    for k in range(q, 15, s):
+                        mm(pc, A("zb_", 15 - k, 143 - k), A("bt", lo + k // s, lo + e * m // f[q], e // f[q]), k == 0, q == rows[-1] and k + s >= 15)
+        for x, y in within(SB, a, b):
             scan(x, y, True)
             scan(x, y, False)
+
+    def compare(outs, ys, zs):
+        step({"v": (lambda q: [q.tensor_tensor(o[0], y[0], z[0], ALU.is_gt) for o, y, z in zip(outs, ys, zs)], "v",
+                    sum(max(64, cyc(o)) + 12 for o in outs) - 12)}, ys + zs, outs, n=len(outs))
 
     def scan(a, b, hi):
         s = (16 * a, 16 * b)
         o, m = (A("hi", *s), A("mhi", 0, 16 * (b - a))) if hi else (A("lo", *s), A("mlo", 0, 16 * (b - a)))
         o0, o1 = (ALU.min, ALU.max) if hi else (ALU.max, ALU.min)
         y = A("yy", *s)
-        step({"v": (lambda q: q.tensor_tensor_scan(o[0], m[0], y[0], 0.0, o0, o1), cyc(width(o), 1, o))}, [m, y], [o])
+        step({"v": (lambda q: q.tensor_tensor_scan(o[0], m[0], y[0], 0.0, o0, o1), "v", cyc(o))}, [m, y], [o])
 
     def vlist(buf, t, c, second):
         a, b = CHS[c] // 8, CHS[c + 1] // 8
@@ -371,48 +563,50 @@ def rank_program(g, core, T, topo):
     def verdict(t, c):
         a, b = CHS[c], CHS[c + 1]
         n, s = b - a, A("sg", a, b)
-        act(s, A("pc", 0, n), ACTF.Sign, bias=chit)
-        mm(A("pf", 0, n), A("ib"), A("k1", 0, n), True, False)
-        mm(A("pf", 0, n), A("tri"), s, False, True)
-        mm(A("pf", n, 2 * n), A("ib"), A("li%d" % t, a, b), True, False)
+        mm(A("pf", 0, 2 * n), A("ib"), A("k1", 256 - n, 256 + n), True, False)
+        mm(A("pf", n, 2 * n), A("ib"), A("li%d" % t, a, b), False, False)
+        act(s, A(PC[c % 2], 0, n), ACTF.Sign, bias=chit)
+        mm(A("pf", 0, n), A("tri"), s, False, False)
         mm(A("pf", n, 2 * n), A("tri"), s, False, True)
-        act(A("oh", 2 * a, 2 * b), A("pf", 0, 2 * n), ACTF.Relu, bias=crel)
-        pl = A("pl", 0, n // 8)
+        o, i = A("oh", 2 * a, 2 * b), A("pf", 0, 2 * n)
+        calls = {"s": (lambda q: q.activation(o[0], i[0], ACTF.Relu, bias=crel[0]), "s", 2 * n),
+                 "v": (lambda q: q.tensor_scalar(o[0], i[0], crel[0], 0.0, ALU.add, ALU.max), "v", 2 * n)}
+        step({e: calls[e] for e in ("s" if 2 * n >= LONG else "sv")}, [i, crel], [o])
+        if c >= LC - 1:
+            verdicts(t, range(LC) if c < LC else [LC])
+        bank, more = (PV, 32) if c == LC else ("pl", 0)
+        pl = A(bank, 0, n // 8)
         mm(pl, A("ib"), A("cst", a // 8, b // 8), True, False)
         for k in range(16):
             mm(pl, A("zb_", 15 - k, 143 - k), A("oh", 2 * a + k, 2 * b, 16), False, k == 15)
-        lin(A("sb%d" % t, a // 8, b // 8), pl, 1.0, -1.0, "v")
+        lin(A("sb%d" % t, a // 8, b // 8 + more), A(bank, 0, n // 8 + more), 1.0, -1.0)
 
     def newz(t, c):
         a, b = CHS[c], CHS[c + 1]
         last, v, sm, z = t + 1 == NT, vlist("sb", t, c, 0), A("sm", a, b), A("zo%d" % t, a, b)
         hi, lo = A("hi", 16 * a, 16 * b), A("lo", 16 * a, 16 * b)
-        if c in PA and not last:
-            gather(A("hp", a, b), hi, v)
-            gather_tt(sm, lo, v, A("hp", a, b), ALU.add)
-            lin(z, sm, 0.5, ZO - 0.25, "v")
+        if c < ZF and not last:
+            gather(A("hh%d" % t, a, b), hi, v, "sv", 0.5, ZO - 256)
+            gather(A("lh%d" % t, a, b), lo, v, "sv", 0.5, 255.75)
         elif c < LC:
             ph = A("pe", 256, 256 + b - a)
             gather(A("hp", a, b), hi, v)
             gather(A("lp", a, b), lo, v)
             mm(ph, A("hib"), A("hp", a, b), True, False)
-            mm(ph, A("hib"), A("lp", a, b), False, not last)
-            if last:
-                mm(ph, A("kq"), A("k1", 0, b - a), False, True)
-                ts(z, ph, BIG, ALU.add, -BIG, ALU.add)
-            else:
-                lin(z, ph, 1.0, ZO - 0.25)
+            mm(ph, A("hib"), A("lp", a, b), False, True)
+            lin(A("z16", a, b), ph, 1.0, ZO - 0.25)
+            lin(z, A("z16", a, b), 1.0, -ZO)
         elif last:
-            gather(A("hp", a, b), hi, v, "v")
+            gather(A("hp", a, b), hi, v)
             gather_tt(sm, lo, v, A("hp", a, b), ALU.add)
-            lin(A("z16", a, b), sm, 0.5, ZO - 0.25, "v")
-            lin(z, A("z16", a, b), 1.0, -ZO, "v")
+            lin(A("z16", a, b), sm, 0.5, ZO - 0.25)
+            lin(z, A("z16", a, b), 1.0, -ZO)
         else:
             gather_tt(A("z16", a, b), hi, v, A("old", a, b), ALU.add)
             gather_tt(A("s2", a, b), lo, v, A("z16", a, b), ALU.add)
-            ts(A("nw", a, b), A("s2", a, b), 0.25, ALU.mult, -0.375, ALU.add)
+            lin(A("nw", a, b), A("s2", a, b), 0.25, -0.375)
             tt(sm, A("s2", a, b), A("old", a, b), ALU.subtract)
-            lin(z, sm, 0.5, ZO - 0.25, "v")
+            lin(z, sm, 0.5, ZO - 0.25)
 
     def window(lo):
         return A("rw", 0, 8 * SEG) if lo < SEG else A("rw", 8 * SEG, 4096)
@@ -430,48 +624,55 @@ def rank_program(g, core, T, topo):
     def update(t, lo, hi):
         p = A("pe", 0, hi - lo)
         mm(p, A("qib"), A("old", lo, hi), True, False)
-        mm(p, A("hib"), A("zo%d" % t, lo, hi), False, True)
+        flush()
+        mm(p, A("hib"), A("hh%d" % t, lo, hi), False, False)
+        mm(p, A("hib"), A("lh%d" % t, lo, hi), False, True)
         lin(A("nw", lo, hi), p, 1.0, -ZO / 2 - 0.25)
 
     def scatter(t, lo, hi):
         w, o, i = window(lo), A("plu", lo // 16, hi // 16), A("nw", lo, hi)
-        step({"v": (lambda q: q.tensor_copy(w[0].indirect(o[0]), i[0]), 0.05 + (hi - lo) * SC * CY)}, [o, i], [w], ind=(hi - lo) * SC * CY)
+        step({"v": (lambda q: q.tensor_copy(w[0].indirect(o[0]), i[0]), "x", hi - lo)}, [o, i], [w])
 
     def mirror(t):
         dma("y", "mir%d" % t, T.rw[:, 4096:RW], T.rw[:, 0:RW - 4096], 256 * (RW - 4096), reads=[A("rw", 0, RW - 4096)], writes=[A("rw", 4096, RW)])
 
-    def tally(t):
-        for c in range(NC):
+    def tally(t, cs):
+        pt = A(PC[(LC - 1) % 2], 0, 64)
+        for c in cs:
             for i in range(CHS[c], CHS[c + 1], 64):
-                mm(A("pc", 256, 320), A("a15"), A("oh", CHS[c] + i, CHS[c] + i + 64), i == 0, i == G - 64)
-        o, i = A("an", 0, 1), A("pc", 256, 320)
-        step({"v": (lambda q: q.tensor_reduce(o[0], i[0], AxisListType.X, ALU.add), cyc(width(i), 1))}, [i], [o])
-        copy(A("ani", 0, 1), o)
+                mm(pt, A("a15"), A("oh", CHS[c] + i, CHS[c] + i + 64), i == 0, i == G - 64)
+        flush()
+        if c < LC:
+            return
+        o, i = A("an", 0, 1), pt
+        step({"v": (lambda q: q.tensor_reduce(o[0], i[0], AxisListType.X, ALU.add), "v", width(i))}, [i], [o])
+        lin(A("ani", 0, 1), o, 1.0, 0.0)
         ts(A("ani", 1, 2), A("ani", 0, 1), 255, ALU.bitwise_and)
-        ts(cadd, A("ani", 1, 2), c37, ALU.add)
+        lin(cadd, A("ani", 1, 2), 1.0, c37)
 
-    def verdicts(t):
-        for c in range(NC):
+    def verdicts(t, cs):
+        pv = A(PV, 64 - CHS[LC] // 8, 96 - CHS[LC] // 8)
+        for c in cs:
             for i in range(CHS[c], CHS[c + 1], 32):
                 j = i // 32
-                mm(A("pc", 320, 352), A("zb_", 15 - j, 143 - j), A("oh", CHS[c] + i, CHS[c] + i + 32), j == 0, j == 15)
-        lin(A("sb%d" % t, 64, 96), A("pc", 320, 352), 1.0, -1.0, "v")
+                mm(pv, A("zb_", 15 - j, 143 - j), A("oh", CHS[c] + i, CHS[c] + i + 32), j == 0, j == 15)
+        flush()
 
     def verdicts_out(t):
-        lin(A("vi%d" % t), A("nm%d" % t, 64, 96), 1.0, 0.0)
+        if t + 1 < NT:
+            select(A("vi%d" % t), A("nm%d" % t, 64, 96), [[0, 32]], ALU.is_ge, 0.0, 0)
+        else:
+            lin(A("vi%d" % t), A("nm%d" % t, 64, 96), 1.0, 0.0)
         dma("y", "o_k%d" % t, T.yk[:, t * G:t * G + G], T["vi%d" % t][:], 16384, reads=[A("vi%d" % t)])
 
     def home(t, c):
         a, b = CHS[c], CHS[c + 1]
-        out = A("ls%d" % (t + 1) if t + 1 < NT else "yos", a, b)
         win = A(("ots", "pts", "ots")[t], 0, 1024 + 512 * t)
-        fold = t + 1 < NT and c in FOLD
-        if fold:
-            gather(out, win, vlist("nm", t, c, 1))
-        else:
-            gather_tt(out, win, vlist("nm", t, c, 1), A("nr%d" % t, a, b), ALU.max)
         if t + 1 < NT:
-            send("li%d" % (t + 1), "ls%d" % (t + 1), a, b, "la%d%d" % (t + 1, c), me + 2 + t, late=LATE[c], fold="nr%d" % t if fold else None)
+            gather(A("ls%d" % (t + 1), a, b), win, vlist("nm", t, c, 1))
+            send("li%d" % (t + 1), "ls%d" % (t + 1), a, b, "la%d%d" % (t + 1, c), me + 2 + t, fold=("nr%d" % t,))
+        else:
+            gather_tt(A("yos", a, b), win, vlist("nm", t, c, 1), A("nr%d" % t, a, b), ALU.max)
 
     def extend(t):
         o, i, x = A("lsi" if t < 2 else "yps"), A("ls%d" % t), A("nri")
@@ -503,10 +704,11 @@ def rank_program(g, core, T, topo):
             dma("y", "o_p", T.yp[0:128:16, :], T.nr2[0:128:16, :], 16384, reads=[A("nr2")], writes=[yp])
 
     iota(A("pint", 0, 1), [[1, 1]], 1, False)
-    iota(A("xb"), [[1, 144]], 0)
-    iota(A("xg"), [[16, 8], [0, 16]], 0)
-    iota(A("xx", 0, G // 2), [[1, G // 2]], 0)
-    lin(A("xx", G // 2, G), A("xx", 0, G // 2), 1.0, G / 2, "s")
+    for out, pattern in ((A("xg"), [[16, 8], [0, 16]]), (A("xb"), [[1, 144]])):
+        gate.append(len(steps) - 1)
+        iota(out, pattern, 0)
+        gate.pop()
+    first = len(steps) - 1
     X = A("xb", 0, 128)
     fill(A("neg"), -ZO)
     fill(A("kc"), -32.0)
@@ -516,11 +718,9 @@ def rank_program(g, core, T, topo):
     copy(ck, A("pint", 1, 2))
     copy(cw, A("wti", 0, 1))
     tt(cg16, cp, ck, ALU.subtract)
-    for i in range(0, 1024, G):
-        lin(A("mhi", i, i + G), A("neg"), 0.0, 256.0, "s")
-        lin(A("mlo", i, i + G), A("neg"), 0.0, 0.0, "s")
-    lin(A("mhi", 0, 1024, 16), A("neg", 0, 64), 0.0, 0.0, "s")
-    lin(A("mlo", 0, 1024, 16), A("neg", 0, 64), 0.0, 256.0, "s")
+    fill(A("mhi"), 256.0)
+    fill(A("mhi", 0, MW, 16), 0.0)
+    lin(A("mlo"), A("mhi"), -1.0, 256.0)
     ts(cz15, cg16, 15.0, ALU.add)
     ts(c37, ck, 37.0, ALU.mult)
     ts(cj0, ck, 0.0, ALU.is_equal)
@@ -529,50 +729,52 @@ def rank_program(g, core, T, topo):
     ts(A("zb_"), A("xb"), cz15, ALU.is_equal)
     ts(A("bw"), A("xg"), cg16, ALU.is_equal, cw, ALU.mult)
     ts(A("tr1"), A("xg"), cg16, ALU.is_equal, -2048.0, ALU.mult)
-
-    ts(cn0, cj0, 1024.0, ALU.mult)
-    act(A("nr0"), A("xx"), ACTF.Identity, scale=cj0, bias=cn0)
     copy(A("mvu"), A("mvs"))
     gather(A("ls0", 0, c1), A("pt0"), A("mvu", 0, c1 // 16), "v")
-    gather(A("ls0", c1, G), A("pt0"), A("mvu", c1 // 16, 32), "v")
-    gate.append(len(steps) - 1)
+    gather(A("ls0", c1, G), A("pt0"), A("mvu", c1 // 16, 32), "s")
+    gate.append(len(steps) - 2)
     fill(A("cst"), 0.0)
     ts(crel, ck, -2048.0, ALU.mult, -2047.0, ALU.add)
     ts(ca15, ck, 15.0, ALU.is_equal, -1.0 / 16, ALU.mult)
     ts(ck16, ck, 16.0, ALU.mult)
     ts(c8k, ck, 8.0, ALU.mult)
     ts(chit, ca15, -1600.0, ALU.mult, -8.5, ALU.add)
+    ts(c4, cg16, 0.25, ALU.mult, 3.0, ALU.add)
+    lin(A("x4"), A("xb"), 0.25, -0.375)
+    ts(A("bw4"), A("x4"), c4, ALU.is_equal, cw, ALU.mult)
+    ts(A("pint", 2, 3), A("pint", 0, 1), 124, ALU.bitwise_and)
+    for s in range(4):
+        lin(C(16 + s), A("pint", 2, 3), 1.0, -4.0 * s)
+        ts(A("un%d" % s), A("xg"), C(16 + s), ALU.is_equal, -1024.0, ALU.mult)
+    tt(A("kw"), A("kc"), A("bw"), ALU.add)
     lin(A("hib"), A("ib"), 0.5, 0.0)
     lin(A("qib"), A("ib"), 0.25, 0.0)
     ts(A("zw_"), A("xb"), cz15, ALU.is_equal, cw, ALU.mult)
     lin(A("a15"), X, 0.0, ca15)
-    lin(A("k1"), A("neg", 0, 256), 0.0, ck)
+    lin(A("k1", 0, 256), A("neg", 0, 256), 0.0, ck)
+    fill(A("k1", 256, 512), 0.0)
     mm(A("pd", 0, 2), A("bw"), A("neg", 0, 2))
     lin(cq, A("pd", 0, 1), 1.0 / 4096, QO - 2047.5 / 4096)
-    lin(A("c8", 0, SEG // 16), A("xx", 0, SEG // 16), 128.0, c8k)
-    lin(A("c8", SEG // 16, 32), A("xx", 0, 32 - SEG // 16), 128.0, c8k)
+    lin(A("c8", 0, SEG // 16), A("xb", 0, SEG // 16), 128.0, c8k)
+    lin(A("c8", SEG // 16, 32), A("xb", 0, 32 - SEG // 16), 128.0, c8k)
     for c in range(NC):
         a, b = CHS[c], CHS[c + 1]
-        lin(A("cst", a // 8, (a + b) // 16), A("xx", 0, (b - a) // 16), 256.0, ck16)
+        lin(A("cst", a // 8, (a + b) // 16), A("xb", 0, (b - a) // 16), 256.0, ck16)
     gate.pop()
 
-    def later():
-        gate.append(len(steps) - 1)
-        lin(A("hz_"), A("zb_"), 0.5, 0.0)
-        lin(A("nib"), A("ib"), -1.0, 0.0)
-        for name, x in (("kq", -1.0 / 3840), ("one", 1.0), ("e8", 0.0)):
-            lin(A(name), X, 0.0, x)
-        lin(A("e8", 1, 128, 2), A("xb", 0, 64), 0.0, 1.0 / 16)
-        gate.pop()
-
-    send("zi0", "zst", 0, c1, "za0", me + 1, 1.8, 0.5)
-    d = send("li0", "ls0", 0, c1, "la0", me + 1, 0.0, 0.5)
-    d = step({"g": (lambda q: q.sem_inc(T.sem["go"], 1), 0.01)}, [], [(None, ("go", 0, 1))], sem="go", n=0, after=[d])
+    d = send("zi0", "zst", 0, z1, "za0", me + 1, 1.6, 0.3, [first])
+    if not GO:
+        d = send("li0", "ls0", 0, c1, "la0", me + 1, 0.0, 0.3, [d])
+    d = step({"g": (lambda q: q.sem_inc(T.sem["go"], 1), "g", 0.01)}, [A("ls0", 0, c1)], [(None, ("go", 0, 1))], sem="go", n=0, after=[d])
+    if GO:
+        d = send("li0", "ls0", 0, c1, "la0", me + 1, 0.0, 0.3, [d])
     dma("y", "ld_r2", T.rw[:, RA:4096], T.strat[:, RA:4096], 256 * (4096 - RA), reads=[(None, ("go", 0, 1))], writes=[A("rw", RA, 4096)])
-    for lo, hi, x in ((c1, c2, "b0"), (c2, G, "c0")):
-        d = send("zi0", "zst", lo, hi, "z" + x, me + 1, 0.0, 0.5, [d])
-        d = send("li0", "ls0", lo, hi, "l" + x, me + 1, 0.0, 0.5, [d])
+    for lo, x, hi, s in sorted([(a, 0, b, "z" + s) for a, b, s in zip(Z0[1:], Z0[2:], ("b0", "c0"))]
+                               + [(a, 1, b, "l" + s) for a, b, s in zip(U0[1:], U0[2:], ("b0", "c0"))]):
+        d = send(("zi0", "li0")[x], ("zst", "ls0")[x], lo, hi, s, me + 1, 0.0, 0.3, [d])
     gate.append(d)
+    iota(A("xx"), [[1, G]], 0, True, 1024)
+    lin(A("nr0"), A("xx"), cj0, 0.0)
     select(A("tr2"), A("tr1"), [[1, 128]], ALU.is_gt, 0.0, -1)
     select(A("tri"), A("tr2"), [[1, 128]], ALU.not_equal, 2048.0, -1)
     gate.pop()
@@ -580,6 +782,7 @@ def rank_program(g, core, T, topo):
 
     for t in range(NT):
         last = t + 1 == NT
+        turns.append(t)
         us = CHS if t else U0
         if t != 1:
             extend(t)
@@ -594,19 +797,18 @@ def rank_program(g, core, T, topo):
             beats(t, c)
             verdict(t, c)
             newz(t, c)
-            if c == LC:
-                if t == 0:
-                    later()
-                if not last:
-                    tally(t)
-                verdicts(t)
-            send("nm%d" % t, "sb%d" % t, (a + b) // 16, 96 if c == LC else b // 8, "nm%d%d" % (t, c), me - 1 - t, late=LATE[c])
-            send("zi%d" % (t + 1), "zo%d" % t, a, b, "za%d%d" % (t + 1, c), me - 1 - t if last else me + 1, late=LATE[c])
+            if c >= LC - 1 and not last:
+                tally(t, range(LC) if c < LC else [LC])
+            send("nm%d" % t, "sb%d" % t, (a + b) // 16, 96 if c == LC else b // 8, "nm%d%d" % (t, c), me - 1 - t)
+            if c < ZF and not last:
+                send("zi%d" % (t + 1), "hh%d" % t, a, b, "za%d%d" % (t + 1, c), me + 1, fold=("lh%d" % t,), op=1)
+            else:
+                send("zi%d" % (t + 1), "zo%d" % t, a, b, "za%d%d" % (t + 1, c), me - 1 - t if last else me + 1)
             home(t, c)
             if last:
                 dma("y", "o_o%d" % c, T.yo[:, a:b], T.yos[:, a:b], 512 * (b - a), reads=[A("yos", a, b)])
                 dma("s" if c == LC else "y", "o_z%d" % c, T.yz[:, a:b], T.zi3[:, a:b], 256 * (b - a), reads=[A("zi3", a, b)])
-            if not last and b < G:
+            if not last and c < ZF:
                 update(t, a, b)
         if t == 1:
             extend(t)

import math
import numpy as np
from concourse.bass import DstId, RemoteDMATransfer
from concourse.mybir import AluOpType as ALU, AxisListType, ActivationFunctionType as ACTF

NT, G = 3, 512
CHS = (0, 256, 448, 512)
NC = len(CHS) - 1
U0 = (0, 128, 256, 512)
Z0 = (0, 128, 256, 512)
PARTS = (0, 32, 64, 128, 192, 256, 320, 384, 448, 512)
CB = (0, 64, 192, 256, 384, 448, 512)
SB = (0, 32, 64, 128, 192, 256, 320, 384, 448, 512)
VG = ((0,), (0,), (0, 32))
GO = 0
ZL = 0
WIDE = 256
ZF = 3
LONG = 300
FOLD = 192
FIRST = 64
PC = ("pc", "pd")
PV = "pz%d" % ((len(CB) - 1) % 2)
RW = 4096 + 816
RA = 3072
SEG = 128
EN = 8
MW = 16 * max(b - a for a, b in zip(SB, SB[1:]))
ZO, QO = 1056.0, 1048.0
BIG = 12582912.0
CY, FIX = 0.83e-3, 0.065
CASES = ((1.45, 3.3, 1.0, 0.01, 0.6, 0.05, 0.12, 0.5, 1.0, 1.4, 0.015, 64.7),
         (1.05, 2.0, 1.1, 0.005, 0.5, 0.04, 0.06, 0.4, 0.9, 1.2, 0.01, 58.5),
         (1.1, 5.5, 1.25, 0.01, 0.65, 0.05, 0.12, 0.7, 1.5, 1.6, 0.02, 72.5),
         (2.05, 5.5, 1.1, 0.01, 0.55, 0.05, 0.12, 0.6, 1.3, 1.6, 0.015, 83.5),
         (1.3, 3.5, 1.1, 0.01, 0.6, 0.06, 0.16, 1.0, 2.0, 2.0, 0.04, 83.0),
         (1.95, 3.0, 1.45, 0.01, 0.6, 0.06, 0.15, 0.7, 1.5, 1.7, 0.02, 102.5))
RULES = [(9.0, s, h, f, x) for s in (0.1, 0.2) for h in (0.08, 0.12) for f in (0.0, 0.4, 0.8) for x in (0.1, 0.3)]
PASSES = 3
MOVES, HEAT, REACH, SEED, LOG = 75000, 0.002, 25, 12, []
EARLY = 0.2
POWER = 8
SLACK = 0.0002

SCRATCH = {
    "rw": ("sbuf", [128, RW], "bfloat16"), "pt0": ("sbuf", [128, 1024], "int32"),
    "pts": ("sbuf", [128, 1536], "int32"), "ots": ("sbuf", [128, 2048], "int32"),
    "mvs": ("sbuf", [128, 32], "int32"), "mvu": ("sbuf", [128, 32], "uint16"),
    "wti": ("sbuf", [128, 8], "int32"), "zst": ("sbuf", [128, G], "bfloat16"),
    "yy": ("sbuf", [128, 16 * G], "bfloat16"), "hi": ("sbuf", [128, 16 * G], "bfloat16"), "lo": ("sbuf", [128, 16 * G], "bfloat16"),
    "bt": ("sbuf", [128, 16 * G], "bfloat16"), "mhi": ("sbuf", [128, MW], "bfloat16"), "mlo": ("sbuf", [128, MW], "bfloat16"),
    "qf": ("sbuf", [128, G], "float16"), "xi": ("sbuf", [128, G], "int32"), "ai": ("sbuf", [128, G], "int32"),
    "sg": ("sbuf", [128, G], "bfloat16"), "oh": ("sbuf", [128, 2 * G], "float16"),
    "hp": ("sbuf", [128, G], "bfloat16"), "lp": ("sbuf", [128, G], "bfloat16"), "sm": ("sbuf", [128, G], "float16"), "s2": ("sbuf", [128, G], "float16"),
    "z16": ("sbuf", [128, G], "float16"), "old": ("sbuf", [128, G], "float16"), "nw": ("sbuf", [128, G], "int32"),
    "pli": ("sbuf", [128, 32], "int32"), "plm": ("sbuf", [128, 32], "int32"), "plu": ("sbuf", [128, 32], "uint16"),
    "yps": ("sbuf", [128, G], "float32"), "yos": ("sbuf", [128, G], "float32"),
    "lsi": ("sbuf", [128, G], "int32"), "nri": ("sbuf", [128, 2 * G], "int32"), "nrf": ("sbuf", [128, 2 * G], "float32"),
    "nrh": ("sbuf", [128, G], "float16"), "hh0": ("sbuf", [128, G], "float16"), "lh0": ("sbuf", [128, G], "float16"),
    "hh1": ("sbuf", [128, G], "float16"), "lh1": ("sbuf", [128, G], "float16"),
    "an": ("sbuf", [128, 4], "float32"), "ani": ("sbuf", [128, 8], "int32"),
    "xx": ("sbuf", [128, G], "float32"), "xb": ("sbuf", [128, 144], "bfloat16"), "xg": ("sbuf", [128, 128], "bfloat16"),
    "pint": ("sbuf", [128, 8], "int32"), "col": ("sbuf", [128, 32], "float32"),
    "zb_": ("sbuf", [128, 144], "bfloat16"), "zw_": ("sbuf", [128, 144], "bfloat16"),
    "x4": ("sbuf", [128, 144], "int32"), "bw4": ("sbuf", [128, 144], "bfloat16"),
    "neg": ("sbuf", [128, G], "bfloat16"), "k1": ("sbuf", [128, 512], "bfloat16"),
    "nr0": ("sbuf", [128, G], "float16"), "nr1": ("sbuf", [128, G], "float16"), "nr2": ("sbuf", [128, G], "float32"),
    "cst": ("sbuf", [128, 64], "float16"), "c8": ("sbuf", [128, 32], "int32"),
}
for _n in ("bw", "kc", "ib", "i4", "hib", "qib", "tri", "tr1", "tr2", "a15", "kq", "kw", "un0", "un1", "un2", "un3"):
    SCRATCH[_n] = ("sbuf", [128, 128], "bfloat16")
for _t in range(NT):
    SCRATCH["li%d" % _t] = ("sbuf", [128, G], "float16")
    SCRATCH["ls%d" % _t] = ("sbuf", [128, G], "float16")
    SCRATCH["of%d" % _t] = ("sbuf", [128, G], "uint16")
    SCRATCH["sb%d" % _t] = ("sbuf", [128, 96], "uint16")
    SCRATCH["nm%d" % _t] = ("sbuf", [128, 96], "uint16")
    SCRATCH["vi%d" % _t] = ("sbuf", [128, 32], "float32")
    SCRATCH["zo%d" % _t] = ("sbuf", [128, G], "float16" if _t + 1 < NT else "bfloat16")
for _t in range(NT + 1):
    SCRATCH["zi%d" % _t] = ("sbuf", [128, G], "float16" if 0 < _t < NT else "bfloat16")
BANKS = ("pz0", "pz1", "pu", "pc", "pf", "pd", "pl", "pe")
for _b in BANKS:
    SCRATCH[_b] = ("psum", [128, 512], "float32")

LDS = ["ld_mv", "ld_wt", "ld_z", "ld_z2", "ld_p", "ld_r", "ld_r2", "ld_o", "ld_o0", "ld_q", "ld_q0", "mir0", "mir1"]
OUTS = ["o_p", "o_k0", "o_k1", "o_k2"] + ["o_%s%d" % (x, c) for x in "oz" for c in range(NC)]
SEMAPHORES = ["qv", "qs", "qp", "qg", "loc", "go", "za0", "zb0", "zc0", "la0", "lb0", "lc0", "o_p0"] + ["e%d" % _i for _i in range(12)] + LDS + OUTS
for _t in range(NT):
    for _c in range(NC):
        SEMAPHORES += ["nm%d%d" % (_t, _c), "za%d%d" % (_t + 1, _c)]
        if _t:
            SEMAPHORES.append("la%d%d" % (_t, _c))
PLAN = []
QUEUES = "vspgy"


def arrange(steps):
    n, nk = len(steps), len(CASES)
    above, pre = [0] * n, []
    for i, s in enumerate(steps):
        firm = [j for j in s["pre"] if j not in s["order"]]
        for j in firm:
            above[i] |= above[j] | 1 << j
        pre.append([j for j in s["pre"] if not any(above[x] >> j & 1 for x in firm)])
    post = [[] for _ in steps]
    for i in range(n):
        for j in pre[i]:
            post[j].append(i)
    leaves = [i for i in range(n) if not post[i]]

    def cost(kind, size, c):
        ga, sc, slow, call, pe, _, _, remote, far, hop, row, _ = c
        if kind == "r":
            return remote + size[2], 0.3, 128 / EN * row * size[3] + size[0] / 2e5, far - 0.3 + size[1]
        if kind == "d":
            return 0.05, 0.6 * hop, math.ceil(size[1] / 16) * row + size[0] / 4e5, 0.4 * hop
        us = {"v": call + max(64, size) * CY * slow, "s": FIX + max(64, size) * CY * slow, "p": size * CY * pe * slow, "g": size * slow,
              "gv": 0.05 + size * ga * CY * slow, "gs": FIX + size * ga * CY * slow, "x": 0.05 + size * sc * CY * slow}
        return us[kind], None, None, None

    dur = [{e: [cost(k, size, c) for c in CASES] for e, (_, k, size) in s["on"].items()} for s in steps]

    def gap(j, i, ej, ei, c):
        s = steps[j]
        if j in steps[i]["order"] or s["sem"] is not None and s["n"] or ej == ei == "p":
            return 0.0
        return c[5] if ej == ei else c[6] * (1.5 if ej == "p" else 1.0)

    def plan(before, behind, way, fixed, wait, small, hold, far, spare):
        left, free, eng, end = [len(x) for x in before], {e: 0.0 for e in QUEUES}, [None] * n, [0.0] * n
        pool, order = {e: {} for e in QUEUES}, []

        def offer(i):
            for e in [fixed[i]] if fixed else steps[i]["on"]:
                pool[e][i] = max([end[j] + (lag(i, j, e, eng[j], far) if fixed else lag(j, i, eng[j], e, far)) for j in before[i]]
                                 + [lag(i, i, e, "", far) if fixed else 0.0])

        for i in range(n):
            if not left[i]:
                offer(i)
        while len(order) < n:
            now, e = min((max(free[e], min(pool[e].values())), e) for e in QUEUES if pool[e])
            near = [i for i, r in pool[e].items() if r <= now + hold]
            if e == "v" and not fixed:
                near = ([i for i, r in pool[e].items() if r <= now + spare and len(steps[i]["on"]) == 1]
                        + [i for i in near if dur[i]["v"][0][0] < small]) or near
                near = [i for i in near if pool[e][i] <= max(now, min(pool[e][j] for j in near)) + hold]
            i = max(near, key=lambda i: (way[i] - wait * max(0.0, pool[e][i] - now), -i))
            free[e] = end[i] = max(now, pool[e][i]) + dur[i][e][0][0]
            eng[i] = e
            order.append(i)
            for x in QUEUES:
                pool[x].pop(i, None)
            for j in behind[i]:
                left[j] -= 1
                if not left[j]:
                    offer(j)
        return order, eng, end

    def lag(j, i, ej, ei, far):
        d = dur[j][ej][0]
        if d[1] is None or j in steps[i]["order"]:
            return gap(j, i, ej, ei, CASES[0])
        return d[1] + d[2] + d[3] + steps[j]["behind"] + (far if steps[j]["n"] < 0 else 0.0)

    def edges(i, eng):
        return [[(j + n if j in steps[i]["order"] else j, gap(j, i, eng[j], eng[i], c)) for j in pre[i]] for c in CASES]

    def length(order, eng, ed, ends, q, r, reach, limit, moved=""):
        last = {}
        for i in reversed(order[:q]):
            last.setdefault(eng[i], i)
            if steps[i]["sem"] and steps[i]["n"]:
                last.setdefault("d", i)
            if len(last) == 6:
                break
        total, new, least = 0.0, [], r
        touched = set(moved) | set(eng[i] for i in order[q:r]) | set("d" for i in order[q:r] if steps[i]["sem"] and steps[i]["n"])
        while touched and least < n:
            i = order[least]
            touched.discard(eng[i])
            if steps[i]["sem"] and steps[i]["n"]:
                touched.discard("d")
            least += 1
        for k in range(nk):
            old = ends[k]
            end = list(old)
            free = {e: end[n + last[e]] if e in last else 0.0 for e in QUEUES}
            dma = end[2 * n + last["d"]] if "d" in last else 0.0
            far = least
            for p in range(q, n):
                if p > far:
                    break
                i = order[p]
                e = eng[i]
                t = free[e]
                for j, x in ed[i][k]:
                    x += end[j]
                    if x > t:
                        t = x
                us, a, b, c = dur[i][e][k]
                free[e] = end[n + i] = t = t + us
                if a is not None:
                    t += a
                    end[2 * n + i] = dma = (t if t > dma else dma) + b
                    t = dma + c
                    if reach[i] > far and abs(end[n + i] - old[n + i]) + abs(dma - old[2 * n + i]) > 1e-9:
                        far = reach[i]
                end[i] = t
                if reach[i] > far and abs(t - old[i]) > 1e-9:
                    far = reach[i]
            x = ((max(end[i] for i in leaves) + EARLY * sum(end[:n]) / n) / (1 + EARLY / 2) / CASES[k][-1]) ** POWER / POWER
            total += x - old[3 * n]
            end[3 * n] = x
            if total > limit + SLACK * (nk - 1 - k):
                return total, None
            new.append(end)
        return total, new

    def reaches(order, eng):
        place, reach, last = [0] * n, [0] * n, dict.fromkeys(QUEUES + "d", 0)
        for p in range(n - 1, -1, -1):
            i = order[p]
            place[i], e = p, eng[i]
            x, last[e] = last[e], p
            for j in post[i]:
                if place[j] > x:
                    x = place[j]
            if dur[i][e][0][1] is not None:
                x, last["d"] = max(x, last["d"]), p
            reach[i] = x
        return reach

    def held(order, eng, ed, ends):
        out, last, before, place = [], {}, {}, {}
        for p, i in enumerate(order):
            before[i], last[eng[i]], place[i] = last.get(eng[i]), i, p
        for k in range(nk):
            end = ends[k]
            i = max(leaves, key=lambda x: end[x])
            while i is not None:
                t, b = end[n + i] - dur[i][eng[i]][k][0], before[i]
                if b is not None and end[n + b] > t - 1e-9:
                    out += [place[i], place[b]]
                    i = b
                else:
                    i = max(ed[i][k], key=lambda x: end[x[0]] + x[1], default=(None,))[0]
                    i = i if i is None else i % n
        return out

    def whole(order, eng):
        ed = [edges(i, eng) for i in range(n)]
        return (ed,) + length(order, eng, ed, [[0.0] * (3 * n + 1)] * nk, 0, n, [n] * n, 99.0)

    def by_time(order, eng, end):
        return sorted(order, key=lambda i: end[n + i] - dur[i][eng[i]][0][0])

    best = None
    for rule in RULES:
        eng = [list(s["on"])[0] for s in steps]
        way = [0.0] * n
        for i in range(n - 1, -1, -1):
            way[i] = dur[i][eng[i]][0][0] + max([way[j] + lag(i, j, eng[i], eng[j], 0.0) for j in post[i]] + [lag(i, i, eng[i], "", 0.0)])
        for _ in range(PASSES):
            order, eng, end = plan(pre, post, way, None, *rule)
            total = whole(order, eng)[1]
            if best is None or total < best[0]:
                best = (total, order, eng)
            way = plan(post, pre, end, eng, *rule)[2]
    LOG.append(best[0])

    rng = np.random.default_rng(SEED)
    now, order, eng = best
    ed, now, ends = whole(order, eng)
    hot, reach, age = held(order, eng, ed, ends), reaches(order, eng), 0
    for it in range(MOVES):
        u = rng.random(6)
        p = hot[int(u[0] * len(hot))] if u[1] < 0.7 else int(u[0] * n)
        i, e2, o2, d2, q, r = order[p], eng, order, ed, p, p + 1
        if len(steps[i]["on"]) > 1 and u[2] < 0.3:
            e2, d2 = list(eng), list(ed)
            e2[i] = [e for e in steps[i]["on"] if e != eng[i]][0]
            for j in [i] + post[i]:
                d2[j] = edges(j, e2)
        if e2 is eng or u[3] < 0.5:
            d, need = 1 + int(u[4] * 2 % 1 * REACH), {i}
            if u[4] < 0.5:
                q = max(0, p - d)
                for x in reversed(order[q:p]):
                    if any(y in need for y in post[x]):
                        need.add(x)
                o2 = order[:q] + [x for x in order[q:r] if x in need] + [x for x in order[q:p] if x not in need] + order[r:]
            else:
                r = min(n, r + d)
                for x in order[p + 1:r]:
                    if any(y in need for y in pre[x]):
                        need.add(x)
                o2 = order[:p] + [x for x in order[p:r] if x not in need] + [x for x in order[p:r] if x in need] + order[r:]
        x, new = length(o2, e2, d2, ends, q, max(r, reach[i] + 1) if e2 is not eng else r, reach,
                        -HEAT * (1 - it / MOVES) * math.log(1 - u[5]), "sv" if e2 is not eng else "")
        if new:
            now, order, eng, ed, ends, age = now + x, o2, e2, d2, new, age + 1
            if age % 64 == 0:
                order = by_time(order, eng, ends[0])
                ed, now, ends = whole(order, eng)
            if age % 8 == 0:
                hot = held(order, eng, ed, ends)
            reach = reaches(order, eng)
            if now < best[0] and age % 64 == 0:
                best = (now, order, eng, [max(end[i] for i in leaves) for end in ends])
    LOG.extend([best[0], best[-1]])
    return best[1:3]


def rank_program(g, core, T, topo):
    me = T.rank_of(core)
    if me is None:
        return
    cores = list(T.cores)
    N = len(cores)
    Q = {"v": g.vector, "s": g.scalar, "p": g.tensor, "g": g, "y": g.sync}

    steps, recs, gate, run, turns = [], {}, [], [], []

    def step(on, reads, writes, sem=None, n=1, lands=None, after=(), behind=0.0):
        flush()
        after = list(after) + gate
        i, pre = len(steps), {}
        for w, lst in ((0, reads), (1, writes)):
            for _, (b, lo, hi) in lst:
                for r in recs.get(b, []):
                    if b in BANKS:
                        pre[r[3]] = pre.get(r[3], False) or ("p" not in on and bool(w or r[2]))
                    elif r[0] < hi and lo < r[1] and (w or r[2]):
                        pre[r[3]] = True
        for w, lst in ((0, reads), (1, writes)):
            for _, (b, lo, hi) in lst:
                old = recs.get(b, [])
                if b in BANKS:
                    recs[b] = [(lo, hi, w or any(r[2] for r in old if r[3] == i), i)]
                else:
                    recs[b] = [r for r in old if not (w and lo <= r[0] and r[1] <= hi)] + [(lo, hi, w, i)]
        if lands:
            recs.setdefault(lands[0], []).append((lands[1], lands[2], 1, i))
        order = set(after) - set(pre)
        pre.update({j: False for j in order})
        steps.append({"on": on, "pre": pre, "sem": sem, "n": n, "order": order, "behind": behind})
        return i

    def A(n, lo=0, hi=None, st=1, p=128):
        t = T[n]
        hi = t.shape[1] if hi is None else hi
        return (t[0:p, lo:hi:st], (n, lo, hi)) if st > 1 else (t[0:p, lo:hi], (n, lo, hi))

    def width(a):
        return a[0].shape[1]

    def cyc(*aps):
        return width(aps[0]) * (0.5 if all(SCRATCH[a[1][0]][2] in ("bfloat16", "float16", "uint16") for a in aps) else 1.0)

    def dma(e, sem, out, in_, size, reads=(), writes=(), after=(), behind=0):
        return step({e: (lambda q: q.dma_start(out, in_), "d", (size, max(out.shape[0], in_.shape[0])))}, reads, writes, sem, 16,
                    after=after, behind=behind / 4e5)

    def send(buf, src, lo, hi, sem, to, start=0.0, late=0.0, after=(), fold=(), op=2):
        dst = cores[to % N]
        rid, pid, _ = topo.addr(dst)
        m = 0
        for x in topo.engines(core, dst)[:EN]:
            m |= 1 << x
        call = lambda q: q.remote_dma(T[buf][:, lo:hi], T[src][:, lo:hi], T.sem[sem], T.sem["loc"], pid, rid, m)
        if fold:
            one = RemoteDMATransfer(dst_ids=[DstId(rid=rid, pnc=pid)], dma_engine_mask=m, remote_sem=T.sem[sem], alu_op=op,
                                    srcs=[T[x][:, lo:hi] for x in (src,) + fold], dsts=[T[buf][:, lo:hi]])
            call = lambda q: q.remote_dma_fused([one], local_sem=T.sem["loc"])
        i = step({"g": (call, "r", (256 * (1 + len(fold)) * (hi - lo), late, start, 1 + len(fold)))}, [A(x, lo, hi) for x in (src,) + fold], [],
                 sem, -EN, (buf, lo, hi), after)
        return i

    def issue():
        if not PLAN:
            PLAN.extend(arrange(steps))
        order, eng = PLAN
        other = set(j for i, s in enumerate(steps) if eng[i] != "p" for j in s["pre"])
        cnt, known, tok = {}, {e: {} for e in Q}, {}
        for i in order:
            s, e = steps[i], eng[i]
            k = known[e]
            need = [j for j, w in s["pre"].items() if j not in s["order"] and (w or eng[j] != e or steps[j]["sem"] or s["sem"])]
            for j in sorted(need, key=lambda j: -tok[j][1]):
                sem, val, vc = tok[j]
                if k.get(sem, 0) < val:
                    Q[e].wait_ge(T.sem[sem], val)
                    k[sem] = val
                    for s2, v2 in vc.items():
                        k[s2] = max(k.get(s2, 0), v2)
            ins = s["on"][e][0](Q[e])
            if s["n"] < 0:
                cnt["loc"] = cnt.get("loc", 0) + EN
                tok[i] = (s["sem"], EN, {})
            elif s["n"] == 0:
                tok[i] = (s["sem"], 1, {})
            else:
                sem = s["sem"] or "q" + e
                if e != "p" or i in other:
                    cnt[sem] = cnt.get(sem, 0) + s["n"]
                    if isinstance(ins, list):
                        for x in ins:
                            x.then_inc(T.sem[sem], 1)
                    else:
                        ins.then_inc(T.sem[sem], s["n"])
                tok[i] = (sem, cnt.get(sem, 0), dict(k))
        for sem in OUTS + ["loc", "qv", "qs", "qp", "qg"]:
            if cnt.get(sem, 0) > known["g"].get(sem, 0):
                g.wait_ge(T.sem[sem], cnt[sem])

    def mm(out, l, r, start=True, stop=True):
        run.append((out, l, r, start, stop))
        if stop:
            flush()

    def flush():
        if run:
            ms = list(run)
            run.clear()
            step({"p": (lambda q: [q.matmul(o[0], l[0], r[0], a, b) for o, l, r, a, b in ms][-1], "p", sum(max(64, width(m[2])) for m in ms))},
                 [x for m in ms for x in m[1:3]], [m[0] for m in ms])

    def copy(out, in_):
        step({"v": (lambda q: q.tensor_copy(out[0], in_[0]), "v", cyc(out, in_))}, [in_], [out])

    def ts(out, in_, s1, op0, s2=None, op1=None):
        rd = [in_] + [s for s in (s1, s2) if isinstance(s, tuple)]
        a1 = s1[0] if isinstance(s1, tuple) else s1
        a2 = s2[0] if isinstance(s2, tuple) else s2
        if op1 is None:
            call = lambda q: q.tensor_scalar(out[0], in_[0], a1, None, op0)
        else:
            call = lambda q: q.tensor_scalar(out[0], in_[0], a1, a2, op0, op1)
        step({"v": (call, "v", cyc(out, in_))}, rd, [out])

    def tt(out, a, b, op):
        step({"v": (lambda q: q.tensor_tensor(out[0], a[0], b[0], op), "v", cyc(out, a) if b[1][0] in BANKS else 2 * width(out))}, [a, b], [out])

    def act(out, in_, fn, **kw):
        rd = [in_] + [x for x in kw.values() if isinstance(x, tuple)]
        kw = {n: x[0] if isinstance(x, tuple) else x for n, x in kw.items()}
        step({"s": (lambda q: q.activation(out[0], in_[0], fn, **kw), "s", width(out))}, rd, [out])

    def lin(out, in_, scale, bias, on="sv"):
        col = isinstance(bias, tuple) or isinstance(scale, tuple)
        if turns and cyc(out, in_) >= LONG:
            on = "s"
        a, b = [x[0] if isinstance(x, tuple) else x for x in (scale, bias)]
        calls = {"s": (lambda q: q.activation(out[0], in_[0], ACTF.Identity if col else ACTF.Copy, scale=a, bias=b), "s", width(out)),
                 "v": (lambda q: q.tensor_scalar(out[0], in_[0], a, b, ALU.mult, ALU.add), "v", cyc(out, in_))}
        step({e: calls[e] for e in on}, [in_] + [x for x in (scale, bias) if isinstance(x, tuple)], [out])

    def gather(out, win, off, on="sv", scale=1.0, bias=0.0):
        calls = {"s": (lambda q: q.activation(out[0], win[0].indirect(off[0]), ACTF.Copy, scale=scale, bias=bias), "gs", width(out)),
                 "v": (lambda q: q.tensor_scalar(out[0], win[0].indirect(off[0]), scale, bias, ALU.mult, ALU.add), "gv", width(out))}
        step({e: calls[e] for e in on}, [win, off], [out])

    def gather_tt(out, win, off, b, op):
        step({"v": (lambda q: q.tensor_tensor(out[0], win[0].indirect(off[0]), b[0], op), "gv", width(out))}, [win, off, b], [out])

    def fill(out, c):
        step({"v": (lambda q: q.memset(out[0], c), "v", cyc(out))}, [], [out])

    def iota(out, pattern, cm, small=True, base=0):
        kw = {"allow_small_or_imprecise_dtypes": True} if small else {}
        step({"g": (lambda q: q.iota(out[0], pattern, base, cm, **kw), "g", 0.13 + 2 * width(out) * CY)}, [], [out])

    def select(out, in_, pattern, op, other, cm):
        step({"g": (lambda q: q.affine_select(out[0], in_[0], pattern, op, other, 0, cm), "g", 0.17 + 2 * width(out) * CY)}, [in_], [out])

    c1, z1, LC = U0[1], Z0[1], NC - 1
    d = dma("s", "ld_z", T.zst[:, 0:z1], T.z0[:, 0:z1], 256 * z1, writes=[A("zst", 0, z1)])
    dma("s", "ld_wt", T.wti[:, 0:1], T.wt[:], 512, writes=[A("wti", 0, 1)], after=[d])
    d = dma("y", "ld_mv", T.mvs[:], T.mv[:], 16384, writes=[A("mvs")])
    d = dma("y", "ld_p", T.pt0[:], T.vp[:], 524288, writes=[A("pt0")], after=[d], behind=256 * z1)
    if not ZL:
        d = dma("y", "ld_z2", T.zst[:, z1:G], T.z0[:, z1:G], 256 * (G - z1), writes=[A("zst", z1, G)], after=[d], behind=600000)
    d = dma("y", "ld_r", T.rw[:, 0:RA], T.strat[:, 0:RA], 256 * RA, writes=[A("rw", 0, RA)], after=[d], behind=680000)
    if ZL:
        d = dma("y", "ld_z2", T.zst[:, z1:G], T.z0[:, z1:G], 256 * (G - z1), writes=[A("zst", z1, G)], after=[d], behind=600000 + 256 * RA)
    lin(A("rw", 4096, 4096 + 560), A("rw", 0, 560), 1.0, 0.0)
    fill(A("rw", 4096 + 560, RW), 0.0)

    def shifted(buf, src, sem, after):
        dma("y", sem, T[buf][1:128, 0:1024], src[0:127, :], 524288, reads=[after], writes=[A(buf, 0, 1024)])
        recs[buf].append((0, 1024, 1, dma("y", sem + "0", T[buf][0:1, 0:1024], src[0:1, :], 4096, reads=[after])))

    C = lambda i: A("col", i, i + 1)
    cp, ck, cg16, cz15, c37, ck16, c8k, cj0, cn0, chit, crel, ca15, cw, cq, cadd, c4 = [C(i) for i in range(16)]

    def zi(t, *r):
        return A("zi%d" % t, *r)

    def address(t, lo, hi):
        n = hi - lo
        pu, fold = A("pu", 0, n), 4 if n >= FOLD else 1
        qf = A("qf", lo, lo + n // fold)
        for s in range(fold):
            mm(A("pu", 0, n // fold), A("bw4", 12 - 4 * s, 140 - 4 * s) if fold > 1 else A("bw"), zi(t, lo + s, hi, fold), s == 0, s == fold - 1)
        lin(qf, A("pu", 0, n // fold), 1.0 / 4096, cq if t else QO - 2047.5 / 4096)
        mm(pu, A("kw" if t else "kc"), A("neg", 0, n), True, False)
        mm(pu, A("bw"), zi(t, lo, hi), False, False)
        for s in range(fold):
            mm(A("pu", s, n, fold), A("un%d" % s if fold > 1 else "i4"), qf, False, s == fold - 1)
        tt(A("xi", lo, hi), A("li%d" % t, lo, hi), pu, ALU.mult)
        ts(A("ai", lo, hi), A("xi", lo, hi), 5, ALU.arith_shift_right, 4095, ALU.bitwise_and)

    def within(bounds, a, b):
        return [(x, y) for x, y in zip(bounds, bounds[1:]) if a <= x and y <= b]

    def columns(t, a, b):
        lin(A("of%d" % t, a, b), A("ai", a, b), 1.0, cadd if t else c37)
        for i, j in within(PARTS, a, b):
            gather(A("yy", 16 * i, 16 * j), A("rw", 0, RW), A("of%d" % t, i, j), "sv" if VG is None else "v" if i in VG[t] else "s")

    def beats(t, c):
        a, b = CHS[c], CHS[c + 1]
        for x, y in within(CB, a, b):
            m = y - x
            e = max(1, WIDE // m)
            s, pc, pz = 16 // e, A(PC[c % 2], x - a, y - a), "pz%d" % (CB.index(x) % 2)
            if t:
                mm(A(pz, 0, e * m), A("ib"), A("neg", 0, e * m), True, False)
            for j in range(e):
                mm(A(pz, j, e * m, e), A("ib"), zi(t, x, y), not t, not t or j == e - 1)
            rows = [q for q in range(s) if q < 15]
            for q0 in range(0, len(rows), max(1, s // 4)):
                some = rows[q0:q0 + max(1, s // 4)]
                f = {q: 2 if q == 7 and e == 2 and m >= 128 else 1 for q in some}
                compare([A("bt", 16 * x + q * e * m, 16 * x + q * e * m + e * m // f[q]) for q in some],
                        [A("yy", 16 * x + q, 16 * y, s * f[q]) for q in some], [A(pz, 0, e * m, f[q]) for q in some])
                for q in some:
                    lo = 16 * x + q * e * m
                    for k in range(q, 15, s):
                        mm(pc, A("zb_", 15 - k, 143 - k), A("bt", lo + k // s, lo + e * m // f[q], e // f[q]), k == 0, q == rows[-1] and k + s >= 15)
        for x, y in within(SB, a, b):
            scan(x, y, True)
            scan(x, y, False)

    def compare(outs, ys, zs):
        step({"v": (lambda q: [q.tensor_tensor(o[0], y[0], z[0], ALU.is_gt) for o, y, z in zip(outs, ys, zs)], "v",
                    sum(max(64, cyc(o)) + 12 for o in outs) - 12)}, ys + zs, outs, n=len(outs))

    def scan(a, b, hi):
        s = (16 * a, 16 * b)
        o, m = (A("hi", *s), A("mhi", 0, 16 * (b - a))) if hi else (A("lo", *s), A("mlo", 0, 16 * (b - a)))
        o0, o1 = (ALU.min, ALU.max) if hi else (ALU.max, ALU.min)
        y = A("yy", *s)
        step({"v": (lambda q: q.tensor_tensor_scan(o[0], m[0], y[0], 0.0, o0, o1), "v", cyc(o))}, [m, y], [o])

    def vlist(buf, t, c, second):
        a, b = CHS[c] // 8, CHS[c + 1] // 8
        m = (a + b) // 2
        return A("%s%d" % (buf, t), m, b) if second else A("%s%d" % (buf, t), a, m)

    def verdict(t, c):
        a, b = CHS[c], CHS[c + 1]
        n, s = b - a, A("sg", a, b)
        mm(A("pf", 0, 2 * n), A("ib"), A("k1", 256 - n, 256 + n), True, False)
        mm(A("pf", n, 2 * n), A("ib"), A("li%d" % t, a, b), False, False)
        act(s, A(PC[c % 2], 0, n), ACTF.Sign, bias=chit)
        mm(A("pf", 0, n), A("tri"), s, False, False)
        mm(A("pf", n, 2 * n), A("tri"), s, False, True)
        o, i = A("oh", 2 * a, 2 * b), A("pf", 0, 2 * n)
        calls = {"s": (lambda q: q.activation(o[0], i[0], ACTF.Relu, bias=crel[0]), "s", 2 * n),
                 "v": (lambda q: q.tensor_scalar(o[0], i[0], crel[0], 0.0, ALU.add, ALU.max), "v", 2 * n)}
        step({e: calls[e] for e in ("s" if 2 * n >= LONG else "sv")}, [i, crel], [o])
        if c >= LC - 1:
            verdicts(t, range(LC) if c < LC else [LC])
        bank, more = (PV, 32) if c == LC else ("pl", 0)
        pl = A(bank, 0, n // 8)
        mm(pl, A("ib"), A("cst", a // 8, b // 8), True, False)
        for k in range(16):
            mm(pl, A("zb_", 15 - k, 143 - k), A("oh", 2 * a + k, 2 * b, 16), False, k == 15)
        lin(A("sb%d" % t, a // 8, b // 8 + more), A(bank, 0, n // 8 + more), 1.0, -1.0)

    def newz(t, c):
        a, b = CHS[c], CHS[c + 1]
        last, v, sm, z = t + 1 == NT, vlist("sb", t, c, 0), A("sm", a, b), A("zo%d" % t, a, b)
        hi, lo = A("hi", 16 * a, 16 * b), A("lo", 16 * a, 16 * b)
        if c < ZF and not last:
            gather(A("hh%d" % t, a, b), hi, v, "sv", 0.5, ZO - 256)
            gather(A("lh%d" % t, a, b), lo, v, "sv", 0.5, 255.75)
        elif c < LC:
            ph = A("pe", 256, 256 + b - a)
            gather(A("hp", a, b), hi, v)
            gather(A("lp", a, b), lo, v)
            mm(ph, A("hib"), A("hp", a, b), True, False)
            mm(ph, A("hib"), A("lp", a, b), False, True)
            lin(A("z16", a, b), ph, 1.0, ZO - 0.25)
            lin(z, A("z16", a, b), 1.0, -ZO)
        elif last:
            gather(A("hp", a, b), hi, v)
            gather_tt(sm, lo, v, A("hp", a, b), ALU.add)
            lin(A("z16", a, b), sm, 0.5, ZO - 0.25)
            lin(z, A("z16", a, b), 1.0, -ZO)
        else:
            gather_tt(A("z16", a, b), hi, v, A("old", a, b), ALU.add)
            gather_tt(A("s2", a, b), lo, v, A("z16", a, b), ALU.add)
            lin(A("nw", a, b), A("s2", a, b), 0.25, -0.375)
            tt(sm, A("s2", a, b), A("old", a, b), ALU.subtract)
            lin(z, sm, 0.5, ZO - 0.25)

    def window(lo):
        return A("rw", 0, 8 * SEG) if lo < SEG else A("rw", 8 * SEG, 4096)

    def place(t):
        for k in range(16):
            mm(A("pe", 0, 32), A("zw_", 15 - k, 143 - k), zi(t, k, G, 16), k == 0, k == 15)
        lin(A("pli"), A("pe", 0, 32), 1.0, 0.0)
        ts(A("plm"), A("pli"), 7, ALU.bitwise_and)
        tt(A("plu"), A("plm"), A("c8"), ALU.add)
        for lo, hi in ((0, SEG), (SEG, G)):
            o, w, x = A("old", lo, hi), window(lo), A("plu", lo // 16, hi // 16)
            gather(o, w, x, "sv", 2.0)

    def update(t, lo, hi):
        p = A("pe", 0, hi - lo)
        mm(p, A("qib"), A("old", lo, hi), True, False)
        flush()
        mm(p, A("hib"), A("hh%d" % t, lo, hi), False, False)
        mm(p, A("hib"), A("lh%d" % t, lo, hi), False, True)
        lin(A("nw", lo, hi), p, 1.0, -ZO / 2 - 0.25)

    def scatter(t, lo, hi):
        w, o, i = window(lo), A("plu", lo // 16, hi // 16), A("nw", lo, hi)
        step({"v": (lambda q: q.tensor_copy(w[0].indirect(o[0]), i[0]), "x", hi - lo)}, [o, i], [w])

    def mirror(t):
        dma("y", "mir%d" % t, T.rw[:, 4096:RW], T.rw[:, 0:RW - 4096], 256 * (RW - 4096), reads=[A("rw", 0, RW - 4096)], writes=[A("rw", 4096, RW)])

    def tally(t, cs):
        pt = A(PC[(LC - 1) % 2], 0, 64)
        for c in cs:
            for i in range(CHS[c], CHS[c + 1], 64):
                mm(pt, A("a15"), A("oh", CHS[c] + i, CHS[c] + i + 64), i == 0, i == G - 64)
        flush()
        if c < LC:
            return
        o, i = A("an", 0, 1), pt
        step({"v": (lambda q: q.tensor_reduce(o[0], i[0], AxisListType.X, ALU.add), "v", width(i))}, [i], [o])
        lin(A("ani", 0, 1), o, 1.0, 0.0)
        ts(A("ani", 1, 2), A("ani", 0, 1), 255, ALU.bitwise_and)
        lin(cadd, A("ani", 1, 2), 1.0, c37)

    def verdicts(t, cs):
        pv = A(PV, 64 - CHS[LC] // 8, 96 - CHS[LC] // 8)
        for c in cs:
            for i in range(CHS[c], CHS[c + 1], 32):
                j = i // 32
                mm(pv, A("zb_", 15 - j, 143 - j), A("oh", CHS[c] + i, CHS[c] + i + 32), j == 0, j == 15)
        flush()

    def verdicts_out(t):
        if t + 1 < NT:
            select(A("vi%d" % t), A("nm%d" % t, 64, 96), [[0, 32]], ALU.is_ge, 0.0, 0)
        else:
            lin(A("vi%d" % t), A("nm%d" % t, 64, 96), 1.0, 0.0)
        dma("y", "o_k%d" % t, T.yk[:, t * G:t * G + G], T["vi%d" % t][:], 16384, reads=[A("vi%d" % t)])

    def home(t, c):
        a, b = CHS[c], CHS[c + 1]
        win = A(("ots", "pts", "ots")[t], 0, 1024 + 512 * t)
        if t + 1 < NT:
            gather(A("ls%d" % (t + 1), a, b), win, vlist("nm", t, c, 1))
            send("li%d" % (t + 1), "ls%d" % (t + 1), a, b, "la%d%d" % (t + 1, c), me + 2 + t, fold=("nr%d" % t,))
        else:
            gather_tt(A("yos", a, b), win, vlist("nm", t, c, 1), A("nr%d" % t, a, b), ALU.max)

    def extend(t):
        o, i, x = A("lsi" if t < 2 else "yps"), A("ls%d" % t), A("nri")
        if t == 0:
            gate.append(d)
        select(o, i, [[0, G]], ALU.is_ge, 0.0, 0)
        if t == 0:
            iota(x, [[1, 2 * G]], 0, False, 1024)
            iota(A("nrf"), [[1, 2 * G]], 0, True, 1536)
            iota(A("nr2"), [[0, G]], 0)
            select(A("nrh"), A("nrf", 0, G), [[0, G]], ALU.is_ge, 0.0, 0)
            gate.pop()
            dma("y", "e9", T.nr1[:], T.nr0[:], 131072, reads=[A("nr0"), o], writes=[A("nr1")])
            dma("y", "e10", T.nr1[0:128:16, :], T.nrh[0:8, :], 8192, reads=[A("nrh")], writes=[A("nr1")])
            dma("y", "e11", T.nr2[0:128:16, :], T.nrf[0:8, G:2 * G], 16384, reads=[A("nrf")], writes=[A("nr2")])
            dma("y", "e6", T.pts[0:2, 1024:1536], T.pt0[0:2, 0:G], 4096, reads=[A("pt0"), o], writes=[A("pts", 1024, 1536)])
            dma("y", "e7", T.pts[2:128, 1024:1536], T.lsi[0:126, :], 262144, reads=[o], writes=[A("pts", 1024, 1536)])
            dma("y", "e8", T.pts[1:128:16, 1024:1536], T.nri[0:8, 0:G], 16384, reads=[x], writes=[A("pts", 1024, 1536)])
        elif t == 1:
            dma("y", "e0", T.ots[0:2, 1024:2048], T.pt0[0:2, :], 8192, reads=[A("pt0"), i], writes=[A("ots", 1024, 2048)])
            dma("y", "e4", T.lsi[0:128:16, :], T.nri[0:8, 0:G], 16384, reads=[x], writes=[o])
            dma("y", "e1", T.ots[1:128, 1024:1536], T.lsi[0:127, :], 262144, reads=[o], writes=[A("ots", 1024, 1536)])
            dma("y", "e2", T.ots[2:128, 1536:2048], T.lsi[0:126, :], 262144, reads=[o], writes=[A("ots", 1536, 2048)])
            dma("y", "e3", T.ots[1:128:16, 1536:2048], T.nri[0:8, G:2 * G], 16384, reads=[x], writes=[A("ots", 1536, 2048)])
        else:
            yp = (None, ("yp", 0, G))
            dma("y", "e5", T.yps[0:128:16, :], T.nrf[0:8, 0:G], 16384, reads=[A("nrf")], writes=[o])
            dma("y", "o_p0", T.yp[1:128, :], T.yps[0:127, :], 262144, reads=[o], writes=[yp])
            dma("y", "o_p", T.yp[0:128:16, :], T.nr2[0:128:16, :], 16384, reads=[A("nr2")], writes=[yp])

    iota(A("pint", 0, 1), [[1, 1]], 1, False)
    for out, pattern in ((A("xg"), [[16, 8], [0, 16]]), (A("xb"), [[1, 144]])):
        gate.append(len(steps) - 1)
        iota(out, pattern, 0)
        gate.pop()
    first = len(steps) - 1
    X = A("xb", 0, 128)
    fill(A("neg"), -ZO)
    fill(A("kc"), -32.0)
    fill(A("kc", p=1), -1.0)
    ts(A("pint", 1, 2), A("pint", 0, 1), 15, ALU.bitwise_and)
    copy(cp, A("pint", 0, 1))
    copy(ck, A("pint", 1, 2))
    copy(cw, A("wti", 0, 1))
    tt(cg16, cp, ck, ALU.subtract)
    fill(A("mhi"), 256.0)
    fill(A("mhi", 0, MW, 16), 0.0)
    lin(A("mlo"), A("mhi"), -1.0, 256.0)
    ts(cz15, cg16, 15.0, ALU.add)
    ts(c37, ck, 37.0, ALU.mult)
    ts(cj0, ck, 0.0, ALU.is_equal)
    ts(A("ib"), X, cp, ALU.is_equal)
    ts(A("i4"), X, cp, ALU.is_equal, -4096.0, ALU.mult)
    ts(A("zb_"), A("xb"), cz15, ALU.is_equal)
    ts(A("bw"), A("xg"), cg16, ALU.is_equal, cw, ALU.mult)
    ts(A("tr1"), A("xg"), cg16, ALU.is_equal, -2048.0, ALU.mult)
    copy(A("mvu"), A("mvs"))
    gather(A("ls0", 0, c1), A("pt0"), A("mvu", 0, c1 // 16), "v")
    gather(A("ls0", c1, G), A("pt0"), A("mvu", c1 // 16, 32), "s")
    gate.append(len(steps) - 2)
    fill(A("cst"), 0.0)
    ts(crel, ck, -2048.0, ALU.mult, -2047.0, ALU.add)
    ts(ca15, ck, 15.0, ALU.is_equal, -1.0 / 16, ALU.mult)
    ts(ck16, ck, 16.0, ALU.mult)
    ts(c8k, ck, 8.0, ALU.mult)
    ts(chit, ca15, -1600.0, ALU.mult, -8.5, ALU.add)
    ts(c4, cg16, 0.25, ALU.mult, 3.0, ALU.add)
    lin(A("x4"), A("xb"), 0.25, -0.375)
    ts(A("bw4"), A("x4"), c4, ALU.is_equal, cw, ALU.mult)
    ts(A("pint", 2, 3), A("pint", 0, 1), 124, ALU.bitwise_and)
    for s in range(4):
        lin(C(16 + s), A("pint", 2, 3), 1.0, -4.0 * s)
        ts(A("un%d" % s), A("xg"), C(16 + s), ALU.is_equal, -1024.0, ALU.mult)
    tt(A("kw"), A("kc"), A("bw"), ALU.add)
    lin(A("hib"), A("ib"), 0.5, 0.0)
    lin(A("qib"), A("ib"), 0.25, 0.0)
    ts(A("zw_"), A("xb"), cz15, ALU.is_equal, cw, ALU.mult)
    lin(A("a15"), X, 0.0, ca15)
    lin(A("k1", 0, 256), A("neg", 0, 256), 0.0, ck)
    fill(A("k1", 256, 512), 0.0)
    mm(A("pd", 0, 2), A("bw"), A("neg", 0, 2))
    lin(cq, A("pd", 0, 1), 1.0 / 4096, QO - 2047.5 / 4096)
    lin(A("c8", 0, SEG // 16), A("xb", 0, SEG // 16), 128.0, c8k)
    lin(A("c8", SEG // 16, 32), A("xb", 0, 32 - SEG // 16), 128.0, c8k)
    for c in range(NC):
        a, b = CHS[c], CHS[c + 1]
        lin(A("cst", a // 8, (a + b) // 16), A("xb", 0, (b - a) // 16), 256.0, ck16)
    gate.pop()

    d = send("zi0", "zst", 0, z1, "za0", me + 1, 1.6, 0.3, [first])
    if not GO:
        d = send("li0", "ls0", 0, c1, "la0", me + 1, 0.0, 0.3, [d])
    d = step({"g": (lambda q: q.sem_inc(T.sem["go"], 1), "g", 0.01)}, [A("ls0", 0, c1)], [(None, ("go", 0, 1))], sem="go", n=0, after=[d])
    if GO:
        d = send("li0", "ls0", 0, c1, "la0", me + 1, 0.0, 0.3, [d])
    dma("y", "ld_r2", T.rw[:, RA:4096], T.strat[:, RA:4096], 256 * (4096 - RA), reads=[(None, ("go", 0, 1))], writes=[A("rw", RA, 4096)])
    for lo, x, hi, s in sorted([(a, 0, b, "z" + s) for a, b, s in zip(Z0[1:], Z0[2:], ("b0", "c0"))]
                               + [(a, 1, b, "l" + s) for a, b, s in zip(U0[1:], U0[2:], ("b0", "c0"))]):
        d = send(("zi0", "li0")[x], ("zst", "ls0")[x], lo, hi, s, me + 1, 0.0, 0.3, [d])
    gate.append(d)
    iota(A("xx"), [[1, G]], 0, True, 1024)
    lin(A("nr0"), A("xx"), cj0, 0.0)
    select(A("tr2"), A("tr1"), [[1, 128]], ALU.is_gt, 0.0, -1)
    select(A("tri"), A("tr2"), [[1, 128]], ALU.not_equal, 2048.0, -1)
    gate.pop()
    shifted("ots", T.vo, "ld_o", A("rw", 4080, 4096))

    for t in range(NT):
        last = t + 1 == NT
        turns.append(t)
        us = CHS if t else U0
        if t != 1:
            extend(t)
        for a, b in zip(us, us[1:]):
            address(t, a, b)
            for x, y in ((a, FIRST), (FIRST, b)) if a < FIRST < b else ((a, b),):
                columns(t, x, y)
        if not last:
            place(t)
        for c in range(NC):
            a, b = CHS[c], CHS[c + 1]
            beats(t, c)
            verdict(t, c)
            newz(t, c)
            if c >= LC - 1 and not last:
                tally(t, range(LC) if c < LC else [LC])
            send("nm%d" % t, "sb%d" % t, (a + b) // 16, 96 if c == LC else b // 8, "nm%d%d" % (t, c), me - 1 - t)
            if c < ZF and not last:
                send("zi%d" % (t + 1), "hh%d" % t, a, b, "za%d%d" % (t + 1, c), me + 1, fold=("lh%d" % t,), op=1)
            else:
                send("zi%d" % (t + 1), "zo%d" % t, a, b, "za%d%d" % (t + 1, c), me - 1 - t if last else me + 1)
            home(t, c)
            if last:
                dma("y", "o_o%d" % c, T.yo[:, a:b], T.yos[:, a:b], 512 * (b - a), reads=[A("yos", a, b)])
                dma("s" if c == LC else "y", "o_z%d" % c, T.yz[:, a:b], T.zi3[:, a:b], 256 * (b - a), reads=[A("zi3", a, b)])
            if not last and c < ZF:
                update(t, a, b)
        if t == 1:
            extend(t)
        if t == 0:
            shifted("pts", T.vp, "ld_q", A("sb0", 0, 2))
        if not last:
            scatter(t, 0, SEG)
            mirror(t)
            for c in range(NC):
                scatter(t, max(SEG, CHS[c]), CHS[c + 1])
        verdicts_out(t)
    issue()
